import numpy as np, ml_dtypes
CORES = [3,7,11,15,131,135,139,143]
N = 8
import mx_ref
BF = ml_dtypes.bfloat16
def pick(q, e):
    c = np.concatenate([q[0].reshape(128, -1, 4), np.zeros((128, 1, 4), np.uint8)], axis=1); s = np.concatenate([q[1], np.ones((16, 1), np.uint8)], axis=1)
    return (np.ascontiguousarray(c[:, e].reshape(128, -1)), np.ascontiguousarray(s[:, e]))
def join(*qs):
    return (np.concatenate([q[0] for q in qs], axis=1), np.concatenate([q[1] for q in qs], axis=1))
def put(q, e, v):
    c, s = q[0].reshape(128, -1, 4).copy(), q[1].copy(); c[:, e] = v[0].reshape(128, -1, 4); s[:, e] = v[1]
    return (c.reshape(128, -1), s)
def pk(c, s):
    return (np.ascontiguousarray(c), mx_ref.live(s))
def emit(q):
    return q[0], q[1]
def decode(q):
    o = []
    for b in range(4):
        e = np.zeros((128, 128, 4), np.float32); e[np.arange(128), np.arange(128), b] = 1
        o.append(mx_ref.matmul(mx_ref.quantize(e.reshape(128, 512).astype(BF)), q))
    return np.stack(o, axis=2).reshape(128, -1)
def cut(t, i, w=512):
    return t[:, w * i:w * i + w]
def f(rng, *shape):
    return mx_ref.flush((rng.standard_normal(shape, dtype=np.float32) * np.exp2(rng.integers(-2, 3, shape[:-1] + (1,)))).astype(BF))
def wide(rng, *shape, cols=0):
    v = rng.standard_normal(shape, dtype=np.float32) * np.exp2(rng.integers(-12, 13, shape)).astype(np.float32)
    if cols: v *= np.repeat(np.exp2(rng.integers(-cols, cols + 1, shape[:-2] + (1, shape[-1] // 4))) * (rng.random(shape[:-2] + (1, shape[-1] // 4)) > 0.0625), 4, axis=-1).astype(np.float32)
    return mx_ref.flush(v.astype(BF))
P, O = 128, 3
PART = [4, 2]
def keep(v):
    v = v.astype(np.float32)
    v[np.abs(v) < np.float32(2.0 ** -16)] = 0
    return v.astype(BF)
def astile(m):
    return np.ascontiguousarray(m.reshape(128, 4, -1).transpose(0, 2, 1)).reshape(128, -1)
def setup_inputs(rng):
    return {"x": keep(f(rng, N, 128, 4 * P)), "u": f(rng, N, 128, 512), "w": f(rng, N, 128, 512 * O)}
def setup_inputs_spread(rng):
    return {**setup_inputs(rng), "x": keep(wide(rng, N, 128, 4 * P, cols=6)), "u": wide(rng, N, 128, 512)}
def setup_inputs_ties(rng):
    d, xs, bare = setup_inputs(rng), [], int(rng.integers(0, N))
    for r in range(N):
        which = rng.permutation(np.concatenate([np.zeros(7 * P // 8, int), rng.integers(1, 6, P // 8)]))
        v = np.array(f(rng, 128, 24)).reshape(128, 6, 4)
        if r == bare: v[:, 0] = 0
        xs.append(keep(v[:, which].reshape(128, -1)))
    return {**d, "x": np.stack(xs)}
def setup_inputs_near(rng):
    d, xs, us = setup_inputs(rng), [], np.array(f(rng, N, 128, 512))
    H, K = P // 2, P // 4
    rows = np.setdiff1d(np.arange(480), [0, 4, 32])
    R = len(rows)
    for r in range(N):
        at = np.concatenate([[P - 1], rng.permutation(np.arange(1, P - 1)), [0]])
        pair, rest = np.sort(at[:H].reshape(K, 2), axis=1), at[H:]
        base = np.zeros((512, K))
        base[rows] = np.stack([rng.permutation(R) % 4 + 4 for j in range(K)], axis=1) * rng.choice([-1.0, 1.0], (R, K))
        base[[0, 4, 32]] = 4
        m = np.zeros((512, P))
        m[:, pair[:, 0]] = base
        m[:, pair[:, 1]] = base
        m[480, pair[:, 0]] = 2.0 ** -5
        m[480, pair[:, 1]] = 2.0 ** -4
        m[484, pair[:, 0]] = 2.0 ** -5
        v = base[:, rng.permutation(np.repeat(np.arange(K), 2))]
        v[rows] *= np.stack([np.where(rng.permutation(R) < R // 4, -1.0, 1.0) for j in range(H)], axis=1)
        v[0, :K] = -4
        v[480] = 2.0 ** -5
        m[:, rest] = v
        xs.append(astile(m).astype(np.float32).astype(BF))
        us[r, :, :4] = 0
        us[r, 8, 0] = 2.0 ** 10
        us[r, 1, 0] = 2.0 ** -11
        us[r, 0, 0] = -2.0 ** -13
    return {**d, "x": np.stack(xs), "u": us}
def setup_inputs_far(rng):
    d, xs, us = setup_inputs(rng), [], []
    H, s = P // 2, rng.choice([-1.0, 1.0], (512, 1))
    for r in range(N):
        at, m = rng.permutation(P), np.zeros((512, P))
        m[:, at[:H]] = np.where(rng.random((512, H)) < 0.8, 1.0, 0.875)
        m[:, at[0]] = np.where(rng.random(512) < 0.9, 0.875, 0.75)
        m[:, at[H:]] = -np.where(rng.random((512, H)) < 0.5, 0.625, 0.75)
        xs.append(astile(m * s * 2.0 ** 28).astype(np.float32).astype(BF))
        us.append(astile(np.where(rng.random((512, 128)) < 0.5, 1.5, 1.75) * s * 2.0 ** 29).astype(np.float32).astype(BF))
    return {**d, "x": np.stack(xs), "u": np.stack(us)}
def setup_inputs_later(rng):
    d, xs = setup_inputs(rng), []
    H, K = P // 2, P // 4
    low = [r for r in range(N) if r < r ^ PART[0]]
    size = np.ones(N)
    for r in rng.permutation(low)[:len(low) // 2]: size[r ^ PART[0]] = 64
    for r in range(N):
        at, m = rng.permutation(P), np.zeros((512, P))
        z = rng.standard_normal((512, H))
        m[:, at[:H]] = z
        m[:, at[H:H + K]] = 0.6 * z[:, rng.integers(0, H, K)] + 0.05 * rng.standard_normal((512, K))
        m[:, at[H + K:]] = 0.45 * rng.standard_normal((512, P - H - K))
        xs.append(keep(astile(m * size[r])))
    return {**d, "x": np.stack(xs)}
def check_inputs(d):
    b = []
    for k, lo, hi in (("x", -20, 28), ("u", -30, 30), ("w", -30, 30)):
        v = np.abs(d[k].astype(np.float32))
        if not (np.isfinite(v).all() and ((v == 0) | (v >= 2.0 ** lo) & (v <= 2.0 ** hi)).all()): b.append("a value of " + k)
    return b
def gram(q):
    n = q[1].shape[1]
    g = np.zeros((n, n), np.float32)
    for i in range(0, n, 128):
        e = np.arange(i, i + 128)
        e[e >= n] = -1
        z = mx_ref.matmul(pick(q, e), pick(q, np.arange(i, n)))[:n - i]
        g[i:i + 128, i:] = z
        g[i:, i:i + 128] = z.T
    return g + np.float32(0)
def score(q, k):
    n = q[1].shape[1]
    e = np.arange(n + -n % 128)
    e[n:] = -1
    return np.concatenate([mx_ref.matmul(pick(q, e[i:i + 128]), pick(k, np.arange(4))) for i in range(0, len(e), 128)])[:n] + np.float32(0)
def high(s, k):
    return np.sort(np.argsort(-s, kind="stable")[:k])
def opened(qs):
    q, out, i = join(*qs), [], 0
    n = q[1].shape[1]
    e = np.arange(n + -n % 4)
    e[n:] = -1
    v = decode(pick(q, e)).reshape(128, -1, 4)
    for p in qs:
        k = p[1].shape[1]
        out.append(v[:, i:i + k])
        i += k
    return out
def anew(v):
    n = v.shape[1]
    v = np.concatenate([v, np.zeros((128, -n % 4, 4), np.float32)], axis=1)
    return pick(mx_ref.quantize(np.ascontiguousarray(v.reshape(128, -1).astype(BF))), np.arange(n))
def reference(x, u, w):
    y, pa = np.zeros((N, 128, O * P), np.float32), np.zeros((N, 1, P + P // 2 + P // 4), np.float32)
    oc, osc = np.zeros((N, 128, 4 * P), np.uint8), np.zeros((N, 16, P), np.uint8)
    uq = [mx_ref.quantize(np.ascontiguousarray(u[r])) for r in range(N)]
    front = [mx_ref.quantize(np.ascontiguousarray(x[r])) for r in range(N)]
    fronts, kin, ways, at = [], [], [], 0
    for l in range(3):
        n = P >> l
        who, done, kept, way = [], [], [], []
        for r in range(N):
            g = gram(front[r])
            piv = high(np.diagonal(g), n // 2)
            non = np.setdiff1d(np.arange(n), piv)
            par = piv[np.argmax(g[piv][:, non], axis=0)]
            pa[r, 0, at + piv] = piv
            pa[r, 0, at + non] = par
            have, first = np.unique(par, return_index=True)
            who.append((non, par, have, non[first]))
        v = opened([pick(front[r], np.concatenate([who[r][0], who[r][2]])) for r in range(N)])
        for r in range(N):
            non, par, have, kid = who[r]
            dn, dp = v[r][:, :n // 2], v[r][:, n // 2:]
            new = anew(dn - np.float32(0.5) * dp[:, np.searchsorted(have, par)])
            done.append(put(front[r], non, new))
            kept.append((have, kid, dp))
            if l < 2:
                go = non[high(score(new, uq[r])[:, l], n // 4)]
                way.append((np.setdiff1d(non, go), go))
        at += n
        fronts.append(done)
        kin.append(kept)
        ways.append(way)
        if l < 2: front = [join(pick(done[r], way[r][0]), pick(done[r ^ PART[l]], way[r ^ PART[l]][1])) for r in range(N)]
    below = None
    for l in (2, 1, 0):
        n = P >> l
        now = fronts[l]
        if l < 2:
            k = n // 4
            for r in range(N):
                stay, go = ways[l][r]
                now[r] = put(now[r], stay, pick(below[r], np.arange(k)))
                now[r] = put(now[r], go, pick(below[r ^ PART[l]], np.arange(k, 2 * k)))
        v = opened([pick(now[r], kin[l][r][1]) for r in range(N)])
        for r in range(N):
            have, kid, dp = kin[l][r]
            now[r] = put(now[r], have, anew((dp + v[r]) * np.float32(0.5)))
        below = now
    for r in range(N):
        for o in range(O):
            y[r, :, o * P:o * P + P] = mx_ref.matmul(mx_ref.quantize(np.ascontiguousarray(cut(w[r], o))), below[r])
        oc[r], osc[r] = emit(below[r])
    return {"y": y, "oc": oc, "osc": osc, "pa": pa}

@@ -1,0 +1,603 @@
+from concourse.mybir import dt, AluOpType, AxisListType, ActivationFunctionType
+
+OP = AluOpType
+AF = ActivationFunctionType
+MX, U8, F32, BF, U16, I32 = "float8_e4m3fn_x4", "uint8", "float32", "bfloat16", "uint16", "int32"
+
+CODES = {"qa": 130, "qn": 144, "qp": 144, "ql": 136, "qr": 128, "qf": 128, "qh": 192, "qs0": 128, "qs1": 128, "qs2": 128,
+         "qe": 512, "qw64": 128, "qwc": 128, "qk0": 128, "qk1": 128, "uq": 128, "ub": 32, "ur": 224,
+         "wq": 384, "pool0": 192, "pool1": 192, "buf0": 320, "buf1": 320, "buf2": 384, "ch0": 128,
+         "ch1": 128, "ch2": 128, "ff": 128}
+SCRATCH = {}
+for _n, _c in CODES.items():
+    SCRATCH[_n] = ("sbuf", [128, _c], MX)
+    SCRATCH[_n + "s"] = ("sbuf", [128, _c], U8)
+for _n, _c, _d in [("xt", 512, BF), ("ut", 512, BF), ("wt", 1536, BF), ("ta", 520, BF), ("ts", 512, BF), ("ts2", 512, BF),
+                   ("the", 516, BF), ("tz", 832, BF), ("te", 512, BF), ("th", 768, BF), ("tg", 512, BF),
+                   ("td", 512, BF), ("r16", 128, BF), ("ra", 128, BF),
+                   ("row", 128, F32), ("idn", 130, F32), ("am", 128, F32), ("sf", 128, F32),
+                   ("fm", 128, F32), ("kk", 390, F32), ("k64", 192, F32), ("ls", 128, F32), ("ones", 64, F32),
+                   ("mx", 160, F32), ("xs", 160, F32), ("zz", 128, F32), ("thr", 128, F32), ("bm", 128, F32),
+                   ("gs", 128, F32), ("mk", 128, F32), ("rm", 128, F32), ("jk", 264, F32), ("eq", 64, F32),
+                   ("dm", 512, F32), ("dn", 256, F32), ("d0", 64, F32), ("so", 128, F32), ("cs", 128, F32),
+                   ("st16", 64, F32), ("ab", 128, F32), ("sm", 112, F32),
+                   ("cf", 96, F32), ("ci", 16, I32), ("ysb", 384, F32),
+                   ("on", 16, U16), ("op", 16, U16), ("lst0", 4, U16), ("lst1", 4, U16), ("lin0", 4, U16),
+                   ("lin1", 4, U16), ("o2", 8, U16), ("oc0", 8, U16), ("oc1", 8, U16), ("oc2", 8, U16),
+                   ("or0", 8, U16), ("or1", 8, U16), ("or2", 8, U16), ("o0", 10, U16)]:
+    SCRATCH[_n] = ("sbuf", [128, _c], _d)
+for _k in range(8):
+    SCRATCH["ps%d" % _k] = ("psum", [128, 512], F32)
+
+NDMA = 16
+SEMAPHORES = ["sv", "sa", "sp", "sg", "sent"] + ["d%d" % k for k in range(NDMA)] + ["r%d" % k for k in range(8)]
+
+PART = [4, 2]
+BO = [64, 64, 128]
+TINY = 2.0 ** -100
+BIG = 1e29
+BELOW = 1.0 - 2.0 ** -24
+M16, M32 = 1.5 * 2.0 ** 27, 1.5 * 2.0 ** 28
+SA, SB = 2.0 ** 22, 2.0 ** 29
+TP, TN, TL, TF = 0, 32, 64, 80
+
+
+def rank_program(g, core, T, topo):
+    rank = T.rank_of(core)
+    if rank is None:
+        return
+    Q = {"v": g.vector, "a": g.scalar, "p": g.tensor, "g": g, "s": g.sync}
+    SEM = {"v": "sv", "a": "sa", "p": "sp", "g": "sg"}
+    clock = {q: {} for q in Q}
+    count = {}
+    snap = {}
+    log = {}
+    ndma = [0]
+
+    def A(name, c0=None, c1=None, step=1, p0=0, p1=128):
+        if c0 is None:
+            c0, c1 = 0, SCRATCH[name][1][1]
+        if c1 is None:
+            c1 = c0 + 1
+        t = T[name]
+        ps = slice(None) if (p0, p1) == (0, 128) else slice(p0, p1)
+        v = t[ps, c0:c1] if step == 1 else t[ps, c0:c1:step]
+        return (v, name, p0, p1, frozenset(range(c0, c1, step)))
+
+    def wait(q, tok):
+        s, n = tok
+        if clock[q].get(s, 0) >= n:
+            return
+        Q[q].wait_ge(T.sem[s], n)
+        clock[q][s] = n
+        for k, m in snap.get(tok, {}).items():
+            if clock[q].get(k, 0) < m:
+                clock[q][k] = m
+
+    def order(q, reads, writes):
+        need = {}
+        for accs, wr in ((reads, False), (writes, True)):
+            for a in accs:
+                psum = a[1].startswith("ps")
+                for (p0, p1, cols, w, oq, tok) in log.get(a[1], []):
+                    if psum:
+                        if oq == q and (q == "p" or not (w or wr)):
+                            continue
+                    elif not (w or wr) or p1 <= a[2] or a[3] <= p0 or cols.isdisjoint(a[4]):
+                        continue
+                    if need.get(tok[0], 0) < tok[1]:
+                        need[tok[0]] = tok[1]
+        for s in sorted(need, key=lambda k: k == SEM.get(q)):
+            wait(q, (s, need[s]))
+
+    def note(q, reads, writes, tok):
+        snap[tok] = dict(clock[q]) if q in clock else {}
+        for accs, wr in ((reads, False), (writes, True)):
+            for a in accs:
+                log.setdefault(a[1], []).append((a[2], a[3], a[4], wr, q, tok))
+
+    def run(q, reads, writes, fn):
+        reads = [a for a in reads if isinstance(a, tuple)]
+        order(q, reads, writes)
+        s = SEM[q]
+        count[s] = count.get(s, 0) + 1
+        fn().then_inc(T.sem[s], 1)
+        note(q, reads, writes, (s, count[s]))
+
+    def val(x):
+        return x[0] if isinstance(x, tuple) else x
+
+    def dma(q, out, in_, reads, writes):
+        order(q, reads, writes)
+        s = "d%d" % ndma[0]
+        ndma[0] += 1
+        Q[q].dma_start(out, in_).then_inc(T.sem[s], 16)
+        count[s] = 16
+        note("dma", reads, writes, (s, 16))
+        snap[(s, 16)] = dict(clock[q])
+
+    def remote(peer_rank, k, src, dst, codes):
+        peer = T.cores[peer_rank]
+        rid, pid = topo.addr(peer, core)
+        m = topo.mask(core, peer)
+        n = len(topo.engines(core, peer))
+        order("g", [src], [])
+        a, b = (src[0].bitcast(dt.uint8), dst[0].bitcast(dt.uint8)) if codes else (src[0], dst[0])
+        g.remote_dma(b, a, T.sem["r%d" % k], T.sem.sent, pid, rid, m)
+        count["sent"] = count.get("sent", 0) + n
+        back = len(topo.engines(peer, core))
+        count["r%d" % k] = back
+        note("net", [], [dst], ("r%d" % k, back))
+
+    def ts(out, in0, s1, op0, s2=None, op1=None):
+        if op1 is None:
+            run("v", [in0, s1], [out], lambda: g.vector.tensor_scalar(out[0], in0[0], val(s1), None, op0))
+        else:
+            run("v", [in0, s1, s2], [out], lambda: g.vector.tensor_scalar(out[0], in0[0], val(s1), val(s2), op0, op1))
+
+    def tt(out, a, b, op):
+        run("v", [a, b], [out], lambda: g.vector.tensor_tensor(out[0], a[0], b[0], op))
+
+    def cp(out, a):
+        run("v", [a], [out], lambda: g.vector.tensor_copy(out[0], a[0]))
+
+    def ms(out, c):
+        run("v", [], [out], lambda: g.vector.memset(out[0], c))
+
+    def red(out, a):
+        run("v", [a], [out], lambda: g.vector.tensor_reduce(out[0], a[0], AxisListType.X, OP.add))
+
+    def scan(out, a, b, init, op0, op1):
+        run("v", [a, b], [out], lambda: g.vector.tensor_tensor_scan(out[0], a[0], b[0], init, op0, op1))
+
+    def tr(out, a):
+        run("v", [a], [out], lambda: g.vector.transpose(out[0], a[0]))
+
+    def act(out, a, scale=1.0, bias=None, func=None, acc=None):
+        def go():
+            kw = {"scale": val(scale)}
+            if bias is not None:
+                kw["bias"] = val(bias)
+            if acc is not None:
+                kw["accum_out"] = acc[0]
+            fn = func if func is not None else (AF.Copy if bias is None else AF.Identity)
+            return g.scalar.activation(out[0], a[0], fn, **kw)
+        run("a", [a, scale, bias], [out] + ([acc] if acc is not None else []), go)
+
+    def iota(out, pat, base=0, cm=0, small=True):
+        if small:
+            run("g", [], [out], lambda: g.iota(out[0], pat, base, cm, allow_small_or_imprecise_dtypes=True))
+        else:
+            run("g", [], [out], lambda: g.iota(out[0], pat, base, cm))
+
+    def quant(name, c0, tile, e0, n):
+        o, s, i = A(name, c0, c0 + n), A(name + "s", c0, c0 + n), A(tile, e0, e0 + 4 * n)
+        run("v", [i], [o, s], lambda: g.vector.quantize_mx(o[0], s[0], i[0]))
+
+    def mm(bank, wn, wc, xn, xc, n=128, start=True, stop=True):
+        o = A("ps%d" % bank, 0, n)
+        w, ws, x, xs = A(wn, wc, wc + 128), A(wn + "s", wc, wc + 128), A(xn, xc, xc + n), A(xn + "s", xc, xc + n)
+        run("p", [w, ws, x, xs], [o], lambda: g.tensor.matmul_mx(o[0], w[0], ws[0], x[0], xs[0], start, stop))
+
+    def pick(dn, dc, sn, s0, s1, off):
+        n = 16 * len(off[4])
+        o, w = A(dn, dc, dc + n), A(sn, s0, s1)
+        run("v", [w, off], [o], lambda: g.vector.tensor_copy(o[0].bitcast(dt.uint32), w[0].bitcast(dt.uint32).indirect(off[0])))
+        o2, w2 = A(dn + "s", dc, dc + n), A(sn + "s", s0, s1)
+        run("a", [w2, off], [o2], lambda: g.scalar.activation(o2[0], w2[0].indirect(off[0]), AF.Copy))
+
+    def P(k, c0, c1=None, p0=0, p1=128):
+        return A("ps%d" % k, c0, c1, 1, p0, p1)
+
+    def C(k, p0=0, p1=128):
+        return A("cf", k, k + 1, 1, p0, p1)
+
+    P31, P15, PH, P3, PA32, PA48, PB32, PP, IL, P64, P128, PL1, CKS, NCK = list(range(13)) + [15]
+    NB, KO, KLO, KHI, OWN0, KB, KT1, KT2, ACC = 18, 19, 20, 21, 22, 24, 26, 27, 28
+
+    def LV(l, k):
+        return C(32 + 16 * l + k)
+    RANK, V_, H_, PM, NON, PIV, PC, PJ, UU, AA, PAO, T1, T2, T3, NH = range(15)
+    M8, M8B, NEG, MK0, MK1, MC0, MC0B, MC1, MC1B, R16X, KT, Q4, Q4S = [8 * k for k in range(13)]
+
+    def S(k, n=8):
+        return A("sm", k, k + n)
+
+    later, stores = [], []
+
+    def fill(n):
+        for _ in range(n):
+            if later:
+                later.pop(0)()
+
+    def nothing():
+        pass
+
+    def weave(a, b):
+        for k in range(max(len(a), len(b))):
+            for x in (a, b):
+                if k < len(x):
+                    x[k]()
+
+    dma("s", T.xt[:], T.x[:], [], [A("xt")])
+    dma("s", T.ut[:], T.u[:], [], [A("ut")])
+    iota(A("row"), [[1, 128]])
+    iota(C(PP), [[0, 1]], 0, 1)
+    iota(A("ci", 15), [[0, 1]], 0, 1, False)
+    ms(A("ta"), 0.0)
+    ms(A("ones"), 1.0)
+    ms(A("mx", 128, 160), 0.0)
+    ms(A("idn", 128, 130), 1.0)
+    act(A("the"), A("ta", 0, 516))
+    ts(A("idn", 0, 128), A("row"), C(PP), OP.is_equal)
+    ts(A("sf"), A("row"), C(PP), OP.is_lt, 1.0, OP.add)
+    run("g", [A("sf")], [A("am")], lambda: g.affine_select(T.am[:], T.sf[:], [[-1, 128]], OP.not_equal, 128.0, 0, 1))
+    iota(A("ra"), [[0, 8], [1, 4], [0, 4]])
+    iota(A("r16"), [[0, 8], [1, 16]])
+    iota(A("tz"), [[0, 832]])
+    pi = A("ci", 15)
+    ts(A("ci", P31), pi, 31, OP.bitwise_and)
+    ts(A("ci", P15), pi, 15, OP.bitwise_and)
+    ts(A("ci", PH), pi, 4, OP.logical_shift_right)
+    ts(A("ci", P3), pi, 3, OP.bitwise_and)
+    cp(A("cf", 0, 4), A("ci", 0, 4))
+    act(A("the", 3, 515, 4), A("idn", 0, 128), 0.5)
+    act(A("ts"), A("ta", 0, 512), 1.0, SA)
+    act(A("kk", 0, 130), A("idn"), 64.5, -1.0)
+    act(A("ts", 0, 512, 4), A("am"), SA)
+    act(A("ta", 1, 512, 4), A("idn", 0, 128), -0.5 * SB)
+    act(A("fm", 32, 128), A("row", 0, 96), 0.0, 1.0)
+    for c0, p0, p1 in ((32, 64, 128), (96, 64, 128), (64, 32, 64), (64, 96, 128)):
+        act(A("fm", c0, c0 + 32, 1, p0, p1), A("row", 0, 32, 1, p0, p1), 0.0, BELOW)
+    ts(A("fm", 0, 32), A("row", 0, 32), C(P31), OP.is_ge, BELOW, OP.max)
+    for b in range(4):
+        quant("qe", 128 * b, "the", 3 - b, 128)
+    for t in range(4):
+        ts(A("tg", t, 512, 4), A("ra"), float(t), OP.is_equal, 64.0, OP.mult)
+    act(C(IL), C(P15), 1.0 / 16)
+    act(C(CKS), C(PP), -SA * SB, 128 * SA * SB)
+    act(C(NCK), C(PP), 1.0, -128.0)
+    ms(A("o0", 4, 10), 1)
+    quant("qs0", 0, "ts", 0, 128)
+    quant("buf0", BO[0], "xt", 0, 128)
+    wait("s", ("d1", 16))
+    dma("s", T.wt[:], T.w[:], [], [A("wt")])
+
+    def k64(l):
+        act(A("k64", 64 * l, 64 * l + 64), A("row", 0, 64), SA * SB, C(CKS + l))
+
+    def rows(src, scal, n):
+        for t in range(n):
+            ts(A("tg", t, 512, 4), A(src), scal, OP.is_equal)
+
+    def send_u():
+        remote(rank ^ PART[0], 6, A("uq", 0, 2), A("ub", 0, 2), True)
+        remote(rank ^ PART[0], 7, A("uqs", 0, 2), A("ubs", 0, 2), False)
+        iota(A("te", 256, 512), [[0, 256]])
+        iota(A("th", 0, 256), [[0, 256]])
+
+    def columns1():
+        act(C(KT1), C(P31), -1.0, C(PP))
+        act(C(KT2), C(PP), 1.0, -63.5, AF.Sign)
+        act(C(KB), C(P15), 1.0, 0.5)
+        act(C(PA48), C(KT1), 0.5)
+        act(C(PA32), C(KT2), 16.0, 16.0)
+        act(C(KB + 1), C(P15), 1.0, 16.5)
+        act(C(PB32), C(PA32), -2.0, C(KT1))
+        act(C(PL1), C(P31), 1.0, C(PA32))
+        act(C(P64), C(PP), 1.0, 64.0)
+        act(C(NB), C(PL1), 1.0, C(PB32))
+        act(S(R16X, 4), A("row", 0, 4), 16.0)
+        act(C(CKS + 1), C(NB), -SA * SB, 64 * SA * SB)
+        act(C(NCK + 1), C(NB), 1.0, -64.0)
+        act(S(NEG), A("ones", 0, 8), -1.0)
+
+    def columns2():
+        act(C(NB), C(P31), 1.0, C(PA48))
+        act(C(P128), C(PP), 1.0, 128.0)
+        act(C(CKS + 2), C(NB), -SA * SB, 32 * SA * SB)
+        act(C(NCK + 2), C(NB), 1.0, -32.0)
+        k64(2)
+
+    def s_tile(l):
+        for b in range(4):
+            act(A(["", "ts", "ts2"][l], 128 * b, 128 * b + 128, 4), A("am", 32 * b, 32 * b + 32),
+                A("sm", Q4S + (4 + b % 2 if l == 1 else b)))
+
+    def masks():
+        ts(S(M8), A("row", 0, 8), C(PH), OP.is_equal)
+        ts(S(Q4, 4), A("row", 0, 4), 16.0, OP.mult, C(PA48), OP.is_equal)
+        ts(S(Q4 + 4, 2), A("row", 0, 2), 32.0, OP.mult, C(PB32), OP.is_equal)
+        act(A("sm", MK0, MK0 + 2), A("sm", M8, M8 + 2))
+        act(A("sm", MK0 + 2, MK0 + 4), A("sm", M8 + 6, M8 + 8))
+        act(S(Q4S, 6), S(Q4, 6), SA)
+        act(S(M8B), S(M8), 128.0)
+        act(A("sm", MK1, MK1 + 4, 2), A("sm", M8 + 3, M8 + 8, 4))
+        act(A("sm", MK1 + 1, MK1 + 4, 2), A("sm", M8, M8 + 5, 4))
+
+    def kin_piv(l):
+        ts(LV(l, PIV), LV(l, RANK), (64 >> l) - 0.5, OP.is_lt)
+        act(LV(l, NON), LV(l, PIV), -1.0, 1.0)
+        act(LV(l, PC), LV(l, PIV), C(P128 if l == 2 else P64))
+        act(LV(l, PJ), LV(l, PIV), C([PP, PL1, P31][l]))
+
+    def kin_pos(l):
+        ts(A("th", 0, 256, 4), A("k64", 64 * l, 64 * l + 64), LV(l, PM), OP.is_equal, 64.0, OP.mult)
+
+    RM = [(M8, M8B, 8, "qwc"), (MC0, MC0B, 4, "qk0"), (MC1, MC1B, 4, "qk1")]
+
+    def kin_a(l):
+        n, e = RM[l][2], 4 * (TL + 8)
+        return [lambda: act(LV(l, UU), LV(l, PM), 1.0 / (SA * SB), C(NCK + l)),
+                lambda: act(LV(l, AA), LV(l, UU), LV(l, NON), LV(l, PC)),
+                lambda: act(LV(l, T3), LV(l, AA), 1.0, M32),
+                lambda: act(LV(l, NH), LV(l, T3), -1.0, M32),
+                lambda: act(A("tz", e, e + 4 * n, 4), S(NEG, n), LV(l, NH)),
+                lambda: act(A("tz", e + 1, e + 4 * n, 4), S(RM[l][0], n), LV(l, AA), LV(l, NH))]
+
+    def kin_hs(l):
+        act(A("ab"), A("row"), -1.0, LV(l, V_), AF.Abs)
+        act(A("th", 256, 768, 4), A("ab"), -1.0, 1.0, AF.Relu)
+
+    def kin_h(l):
+        quant("qh", 0, "th", 0, 192)
+        mm(6, "qh", 64, "qh", 0)
+
+    def kin_first(l):
+        scan(A("so", 0, 64), P(6, 0, 64), A("ones"), -64.0, OP.max, OP.add)
+        scan(A("so", 64, 128), P(6, 0, 64), A("st16"), -64.0, OP.max, OP.add)
+
+    def kin_has(l):
+        n, e = RM[l][2], 4 * (TL + 8) + 2
+        ts(A("tz", e, e + 4 * n - 2, 4), S(RM[l][1], n), A("so", 63), OP.mult, 128.0, OP.min)
+
+    def kin_tile(l):
+        ts(A("tz", 4 * TL, 4 * TL + 32, 4), A("ones", 0, 8), A("so", 127), OP.mult)
+        ts(A("tz", 4 * TL + 1, 4 * TL + 32, 4), S(M8), A("so", 63), OP.mult, A("so", 127), OP.subtract)
+        if l < 2:
+            kin_has(l)
+        quant("ql", 0, "tz", 4 * TL, 136)
+        mm(6, "qwc", 0, "ql", 0)
+        if l < 2:
+            mm(7, RM[l][3], 0, "ql", 8)
+
+    def kin_c(l):
+        ts(A("oc%d" % l), P(6, 0, 8), -1.0, OP.mult, 64.0, OP.add)
+
+    def kin_r(l):
+        n = RM[l][2]
+        cp(A("or%d" % l, 0, n), P(7, 0, n))
+
+    def parents_out(l):
+        v = LV(l, V_)
+        if l == 1:
+            ts(LV(l, T1), v, 63.5, OP.is_ge, -32.0, OP.mult)
+            act(LV(l, T2), LV(l, T1), 1.0, v)
+            v = LV(l, T2)
+        act(LV(l, PAO), v, LV(l, NON), LV(l, PJ))
+        k = 32 + 16 * l + PAO
+        for p0, p1, at in [[(0, 128, 0)], [(0, 32, 128), (64, 96, 160)], [(0, 32, 192)]][l]:
+            src = C(k, p0, p1)
+            stores.append(lambda src=src, at=at, n=p1 - p0: dma("s", T.pa[0, at:at + n], src[0], [src], []))
+
+    def up(l):
+        n, bn, bo = 128 >> l, "buf%d" % l, BO[l]
+        mm(4, bn, bo, bn, bo)
+        for b in range(4):
+            mm(b, "qe", 128 * b, bn, bo)
+        fill(1)
+        tt(A("mx", 0, 128), P(4, 0, 128), A("idn", 0, 128), OP.mult)
+        act(A("gs"), P(4, 0, 128), 2.0 ** -18)
+        scan(A("xs"), A("mx"), A("mx"), TINY, OP.max, OP.max)
+        act(A("thr", 0, n), A("fm", 0, n), A("xs", 159))
+        tr(A("zz", 0, 32), A("xs", 128, 160))
+        if l < 2:
+            tr(A("zz", 32, 64, 1, 64, 128), A("xs", 128, 160, 1, 0, 64))
+            tr(A("zz", 32, 64, 1, 0, 64), A("xs", 128, 160, 1, 64, 128))
+        if l == 0:
+            act(A("zz", 64, 128, 1, 96, 128), A("zz", 0, 64, 1, 64, 96))
+            cp(A("zz", 64, 128, 1, 32, 64), A("zz", 0, 64, 1, 0, 32))
+            cp(A("zz", 64, 128, 1, 0, 32), A("zz", 0, 64, 1, 32, 64))
+            act(A("zz", 64, 128, 1, 64, 96), A("zz", 0, 64, 1, 96, 128))
+        for b in range(4):
+            act(A("dm", b, 512, 4), P(b, 0, 128), -1.0)
+        tt(A("bm", 0, n), A("zz", 0, n), A("thr", 0, n), OP.is_gt)
+        red(LV(l, RANK), A("bm", 0, n))
+        ts(A("ta", 0, 517, 4), A("kk", 130 * l, 130 * l + 130), LV(l, RANK), OP.is_gt, SB, OP.mult)
+        quant("qa", 0, "ta", 0, 130)
+        mm(5, "qs%d" % l, 0, "qa", 0, 130)
+        if l == 2:
+            kin_piv(l)
+        fill(1)
+        kk, pm = A("k64", 64 * l, 64 * l + 64), P(5, 128)
+        tt(A("mk"), A("gs"), P(5, 0, 128), OP.min)
+        ts(A("tz", 4 * TN, 4 * TN + 64), kk, pm, OP.is_equal, C(PH), OP.mult)
+        ts(A("tz", 4 * TN + 64, 4 * TN + 128), kk, pm, OP.is_equal, C(IL), OP.mult)
+        scan(A("rm"), A("mk"), A("mk"), -BIG, OP.max, OP.max)
+        act(A("jk", 0, 128), A("rm"), -1.0, A("rm", 127), AF.Sign, LV(l, V_))
+        act(A("jk", 128, 136), A("rm", 15, 128, 16), -1.0, A("rm", 127), AF.Sign, LV(l, H_))
+        if l < 2:
+            act(A("tz", 4 * TP, 4 * TP + 64), A("ones"), LV(l, H_))
+        quant("qn", 0, "tz", 4 * TN, 144)
+        mm(6, "qw64", 0, "qn", 0, 128, True, False)
+        mm(6, "qw64", 0, "qn", 16, 128, False, True)
+        ts(A("eq"), kk, pm, OP.is_equal, 1.0 / 16, OP.mult)
+        cp(LV(l, PM), pm)
+        if l == 2:
+            kin_hs(l)
+            kin_pos(l)
+            ts(A("tz", 4 * TP, 4 * TP + 64), A("ones"), LV(l, H_), OP.mult)
+        ts(A("tz", 4 * TP + 64, 4 * TP + 128), A("eq"), LV(l, V_), OP.mult, LV(l, H_), OP.subtract)
+        ts(A("on"), P(6, 0, 16), C(P3), OP.add)
+        run("a", [A("dm"), A("on")], [A("dn")],
+            lambda: g.scalar.activation(T.dn[:], T.dm[:].indirect(T.on[:]), AF.Copy, scale=-2.0))
+        quant("qp", 0, "tz", 4 * TP, 144)
+        mm(7, "qw64", 0, "qp", 0, 128, True, False)
+        mm(7, "qw64", 0, "qp", 16, 128, False, True)
+        if l == 2:
+            kin_h(l)
+            for b in range(4):
+                mm(b, "qe", 128 * b, bn, bo, 128, True, False)
+        else:
+            fill(1)
+        ts(A("op"), P(7, 0, 16), C(P3), OP.add)
+        if l == 2:
+            kin_first(l)
+            kin_tile(l)
+            weave(kin_a(l), [])
+        run("v", [A("dm"), A("op"), A("dn")], [A("te", 0, 256)],
+            lambda: g.vector.tensor_tensor(T.te[:, 0:256], T.dm[:].indirect(T["op"][:]), T.dn[:], OP.add))
+        if l == 2:
+            kin_c(l)
+        quant("buf2" if l == 2 else "pool%d" % l, 0, "te", 0, 128)
+
+    def exchange(l):
+        pool, peer = "pool%d" % l, rank ^ PART[l]
+        remote(peer, 3 * l, A(pool, 0, 64), A(pool, 128, 192), True)
+        remote(peer, 3 * l + 1, A(pool + "s", 0, 64), A(pool + "s", 128, 192), False)
+        mm(4, "ur", 96 * l, pool, 0)
+        mm(5, pool, 0, "ur", 96 * l)
+        fill(1)
+        if l == 0:
+            ts(A("mk", 0, 64, 1, 0, 64), P(4, 0, 64, 0, 64), P(5, 0, 1, 0, 64), OP.subtract)
+        else:
+            ts(A("mk", 0, 64, 1, 0, 32), P(4, 0, 64, 0, 32), P(5, 0, 1, 0, 32), OP.subtract)
+            ts(A("mk", 0, 64, 1, 32, 64), P(4, 0, 64, 32, 64), P(5, 32, 33, 32, 64), OP.subtract)
+        tt(A("tz", 4 * TF + 1, 4 * TF + 256, 4, 0, 64), A("mk", 0, 64, 1, 0, 64), A("ls", 64 * l, 64 * l + 64, 1, 0, 64), OP.is_lt)
+        quant("qf", 0, "tz", 4 * TF, 128)
+        mm(6, "qs0", 0, "qf", 0)
+        fill(1)
+        ts(A("d0"), P(6, 0, 64), ((32 >> l) - 0.5) * SA, OP.is_lt, -1.0, OP.mult)
+        scan(A("cs", 0, 64), A("d0"), A("ones"), 0.0, OP.add, OP.add)
+        scan(A("cs", 64, 128), A("d0"), A("ones"), 0.0, OP.add, OP.min)
+        for go, c in ((0, 0), (0, 1), (1, 0), (1, 1)):
+            at = 2 * go + c if l == 0 else 2 * c + 1 - go
+            act(A("jk", 64 * at, 64 * at + 64), A("cs", 64 * go, 64 * go + 64), 2.0 * go - 1.0, C(KB + c), AF.Sign, C(ACC + at))
+        fill(1)
+        acc = A("cf", ACC, ACC + 4)
+        ts(A("lst%d" % l), acc, 0.5, OP.mult, 32.0, OP.add)
+        remote(peer, 3 * l + 2, A("lst%d" % l), A("lin%d" % l), False)
+        nb, bo = "buf%d" % (l + 1), BO[l + 1]
+        if l == 0:
+            pick(nb, bo, pool, 0, 64, A("lst0", 0, 2))
+            pick(nb, bo + 96, pool, 0, 64, A("lst0", 2, 4))
+        else:
+            ts(A("o2", 0, 8, 2), acc, 0.5, OP.mult, 32.0, OP.add)
+        tt(S(KT, 4), acc, S([MK0, MK1][l], 4), OP.mult)
+        if l == 1:
+            for c, at in ((1, 0), (0, 48), (3, 64), (2, 112)):
+                pick(nb, bo + at, pool, 0, 64, A("o2", 2 * c))
+        red(C(KO), S(KT, 4))
+
+    def origin_a(l):
+        return [lambda: act(C(KT1), C(KO), 0.5, 24.5),
+                lambda: act(C(KT2), C(KT1), 1.0, M16),
+                lambda: act(C(KHI), C(KT2), 1.0, -M16),
+                lambda: act(C(KT1), C(KHI), -1.0, 32.0),
+                lambda: act(C(KLO), C(KO), 0.5, C(KT1))]
+
+    def origin_v(l):
+        mc, mcb = [(MC0, MC0B), (MC1, MC1B)][l]
+        ts(S(mc, 4), S(R16X, 4), C(KHI), OP.is_equal, C(OWN0 + l), OP.mult)
+        act(S(mcb, 4), S(mc, 4), 128.0)
+        rows("r16", C(KLO), 3)
+
+    def kin_all(l):
+        kin_pos(l)
+        kin_h(l)
+        weave(kin_a(l), origin_a(l))
+        parents_out(l)
+        kin_first(l)
+        kin_tile(l)
+        fill(1)
+        kin_c(l)
+        kin_r(l)
+
+    def arrive(l):
+        nb, bo, pool = "buf%d" % (l + 1), BO[l + 1], "pool%d" % l
+        if l == 0:
+            pick(nb, bo + 32, pool, 128, 192, A("lin0"))
+        else:
+            pick(nb, bo + 16, pool, 128, 192, A("lin1", 0, 2))
+            pick(nb, bo + 80, pool, 128, 192, A("lin1", 2, 4))
+
+    def down(l):
+        bn, bo, ch = "buf%d" % l, BO[l], "ch%d" % l
+        pick(ch, 0, bn, 0, bo + (0 if l == 2 else 128), A("oc%d" % l))
+        for b in range(4):
+            mm(b, "qe", 128 * b, ch, 0, 128, False, True)
+        if l == 2:
+            kin_has(l)
+            quant("qr", 0, "tz", 4 * (TL + 8), 128)
+            mm(7, RM[l][3], 0, "qr", 0)
+        else:
+            fill(1)
+        for b in range(4):
+            if b % 2:
+                cp(A("td", b, 512, 4), P(b, 0, 128))
+            else:
+                act(A("td", b, 512, 4), P(b, 0, 128))
+        if l == 2:
+            kin_r(l)
+        quant(bn, bo + 128, "td", 0, 128)
+        if l:
+            for b in range(4):
+                mm(b, "qe", 128 * b, "buf%d" % (l - 1), BO[l - 1], 128, True, False)
+            pick("buf%d" % (l - 1), 0, bn, 0, bo + 256, A("or%d" % l, 0, 4))
+        else:
+            pick("ff", 0, bn, 0, bo + 256, A("or0"))
+
+    k64(0)
+    later += [lambda: (quant("uq", 0, "ut", 0, 128), send_u()),
+              lambda: (quant("qw64", 0, "tg", 0, 128), ms(A("o0", 0, 4), 0), columns1()),
+              lambda: (pick("ur", 0, "uq", 0, 32, A("o0", 0, 8)),
+                       act(A("ls", 0, 64), A("am", 0, 64), -TINY, 2 * TINY, AF.Relu),
+                       act(A("th", 256, 768), A("ts"), 0.0, 1.0), k64(1))]
+    up(0)
+    later += [masks,
+              lambda: (ts(A("st16"), A("r16", 0, 64), 15.0, OP.is_equal, 16.0, OP.mult), ms(A("th", 1, 256, 4, 0, 1), -64.0)),
+              lambda: (rows("r16", C(P15), 3), kin_piv(0))]
+    exchange(0)
+    kin_hs(0)
+    s_tile(1)
+    quant("qwc", 0, "tg", 0, 128)
+    later += [lambda: quant("qs1", 0, "ts", 0, 128)]
+    kin_all(0)
+    act(A("kk", 130, 260), A("idn"), 32.5, -1.0)
+    arrive(0)
+    later += [nothing,
+              lambda: (pick("ur", 128, "ub", 0, 32, A("o0", 4, 10)), act(A("jk", 256, 260), S(MK0, 4), acc=C(OWN0)),
+                       act(A("ls", 64, 128), A("ls", 0, 64)), act(A("jk", 260, 264), S(MK1, 4), acc=C(OWN0 + 1)),
+                       act(A("ls", 96, 128, 1, 0, 32), A("ones", 0, 32, 1, 0, 32), -BIG),
+                       act(A("ls", 64, 96, 1, 32, 64), A("ones", 0, 32, 1, 32, 64), -BIG), columns2()),
+              lambda: (origin_v(0), act(A("ts2"), A("ts"), 0.0, SA), s_tile(2))]
+    up(1)
+    later += [lambda: quant("qk0", 0, "tg", 0, 128),
+              lambda: (kin_piv(1), act(A("kk", 260, 390), A("idn"), 16.5, -1.0)),
+              lambda: quant("wq", 0, "wt", 0, 128)]
+    exchange(1)
+    kin_hs(1)
+    quant("qs2", 0, "ts2", 0, 128)
+    later += [lambda: origin_v(1)]
+    kin_all(1)
+    quant("qk1", 0, "tg", 0, 128)
+    arrive(1)
+    up(2)
+    later += [lambda: quant("wq", 128, "wt", 512, 128), lambda: quant("wq", 256, "wt", 1024, 128)]
+    down(2)
+    parents_out(2)
+    for f in stores:
+        f()
+    down(1)
+    down(0)
+    for o in range(3):
+        mm(4 + o, "wq", 128 * o, "ff", 0)
+    dma("s", T.oc[:], T.ff[:].bitcast(dt.uint8), [A("ff")], [])
+    for k in range(4):
+        dma("s", T.osc[4 * k:4 * k + 4, :], T.ffs[32 * k:32 * k + 4, :], [A("ffs")], [])
+    cp(A("ysb", 0, 128), P(4, 0, 128))
+    act(A("ysb", 128, 256), P(5, 0, 128))
+    cp(A("ysb", 256, 384), P(6, 0, 128))
+    dma("a", T.y[:], T.ysb[:], [A("ysb")], [])
+    for s, n in count.items():
+        wait("g", (s, n))

@@ -20,7 +20,7 @@ for _n, _c, _d in [("xt", 512, BF), ("ut", 512, BF), ("wt", 1536, BF), ("ta", 52
                    ("mx", 160, F32), ("xs", 160, F32), ("zz", 128, F32), ("thr", 128, F32), ("bm", 128, F32),
                    ("gs", 128, F32), ("mk", 128, F32), ("rm", 128, F32), ("jk", 264, F32), ("eq", 64, F32),
                    ("dm", 512, F32), ("dn", 256, F32), ("d0", 64, F32), ("so", 128, F32), ("cs", 128, F32),
-                   ("st16", 64, F32), ("ab", 128, F32), ("sm", 112, F32),
+                   ("st16", 64, F32), ("sm", 112, F32),
                    ("cf", 96, F32), ("ci", 16, I32), ("ysb", 384, F32),
                    ("on", 16, U16), ("op", 16, U16), ("lst0", 4, U16), ("lst1", 4, U16), ("lin0", 4, U16),
                    ("lin1", 4, U16), ("o2", 8, U16), ("oc0", 8, U16), ("oc1", 8, U16), ("oc2", 8, U16),
@@ -192,13 +192,14 @@ def rank_program(g, core, T, topo):
     def C(k, p0=0, p1=128):
         return A("cf", k, k + 1, 1, p0, p1)
 
-    P31, P15, PH, P3, PA32, PA48, PB32, PP, IL, P64, P128, PL1, CKS, NCK = list(range(13)) + [15]
-    NB, KO, KLO, KHI, OWN0, KB, KT1, KT2, ACC = 18, 19, 20, 21, 22, 24, 26, 27, 28
+    P31, P15, PH, P3, PA32, PA48, PB32, IL, PL1 = range(9)
+    PP, P64, P128, NK = 82, 83, 84, [80, 16, 17]
+    KO, KLO, KHI, OWN0, KB, KT1, ACC = 19, 20, 21, 22, 24, 26, 28
 
     def LV(l, k):
         return C(32 + 16 * l + k)
-    RANK, V_, H_, PM, NON, PIV, PC, PJ, UU, AA, PAO, T1, T2, T3, NH = range(15)
-    M8, M8B, NEG, MK0, MK1, MC0, MC0B, MC1, MC1B, R16X, KT, Q4, Q4S = [8 * k for k in range(13)]
+    RANK, V_, H_, PM, NON, PC, PJ, UU, AA, PAO, T1, T2, HA = range(13)
+    M8, M8B, MK0, MC0, MC0B, MC1, MC1B, R16X, KT, Q4S = [8 * k for k in range(10)]
 
     def S(k, n=8):
         return A("sm", k, k + n)
@@ -210,9 +211,6 @@ def rank_program(g, core, T, topo):
             if later:
                 later.pop(0)()
 
-    def nothing():
-        pass
-
     def weave(a, b):
         for k in range(max(len(a), len(b))):
             for x in (a, b):
@@ -222,7 +220,7 @@ def rank_program(g, core, T, topo):
     dma("s", T.xt[:], T.x[:], [], [A("xt")])
     dma("s", T.ut[:], T.u[:], [], [A("ut")])
     iota(A("row"), [[1, 128]])
-    iota(C(PP), [[0, 1]], 0, 1)
+    iota(A("cf", 80, 85), [[64, 5]], -128, 1)
     iota(A("ci", 15), [[0, 1]], 0, 1, False)
     ms(A("ta"), 0.0)
     ms(A("ones"), 1.0)
@@ -234,6 +232,9 @@ def rank_program(g, core, T, topo):
     run("g", [A("sf")], [A("am")], lambda: g.affine_select(T.am[:], T.sf[:], [[-1, 128]], OP.not_equal, 128.0, 0, 1))
     iota(A("ra"), [[0, 8], [1, 4], [0, 4]])
     iota(A("r16"), [[0, 8], [1, 16]])
+    iota(S(R16X, 4), [[16, 4]])
+    iota(S(KT, 4), [[6, 2], [1, 2]])
+    iota(S(KT + 4, 4), [[4, 2], [-3, 2]], 3)
     iota(A("tz"), [[0, 832]])
     pi = A("ci", 15)
     ts(A("ci", P31), pi, 31, OP.bitwise_and)
@@ -246,17 +247,15 @@ def rank_program(g, core, T, topo):
     act(A("kk", 0, 130), A("idn"), 64.5, -1.0)
     act(A("ts", 0, 512, 4), A("am"), SA)
     act(A("ta", 1, 512, 4), A("idn", 0, 128), -0.5 * SB)
-    act(A("fm", 32, 128), A("row", 0, 96), 0.0, 1.0)
+    ms(A("fm", 32, 128), 1.0)
     for c0, p0, p1 in ((32, 64, 128), (96, 64, 128), (64, 32, 64), (64, 96, 128)):
-        act(A("fm", c0, c0 + 32, 1, p0, p1), A("row", 0, 32, 1, p0, p1), 0.0, BELOW)
+        ms(A("fm", c0, c0 + 32, 1, p0, p1), BELOW)
     ts(A("fm", 0, 32), A("row", 0, 32), C(P31), OP.is_ge, BELOW, OP.max)
-    for b in range(4):
+    for b in range(2):
         quant("qe", 128 * b, "the", 3 - b, 128)
     for t in range(4):
         ts(A("tg", t, 512, 4), A("ra"), float(t), OP.is_equal, 64.0, OP.mult)
     act(C(IL), C(P15), 1.0 / 16)
-    act(C(CKS), C(PP), -SA * SB, 128 * SA * SB)
-    act(C(NCK), C(PP), 1.0, -128.0)
     ms(A("o0", 4, 10), 1)
     quant("qs0", 0, "ts", 0, 128)
     quant("buf0", BO[0], "xt", 0, 128)
@@ -264,7 +263,7 @@ def rank_program(g, core, T, topo):
     dma("s", T.wt[:], T.w[:], [], [A("wt")])
 
     def k64(l):
-        act(A("k64", 64 * l, 64 * l + 64), A("row", 0, 64), SA * SB, C(CKS + l))
+        ts(A("k64", 64 * l, 64 * l + 64), A("row", 0, 64), C(NK[l]), OP.subtract, SA * SB, OP.mult)
 
     def rows(src, scal, n):
         for t in range(n):
@@ -277,27 +276,9 @@ def rank_program(g, core, T, topo):
         iota(A("th", 0, 256), [[0, 256]])
 
     def columns1():
-        act(C(KT1), C(P31), -1.0, C(PP))
-        act(C(KT2), C(PP), 1.0, -63.5, AF.Sign)
-        act(C(KB), C(P15), 1.0, 0.5)
-        act(C(PA48), C(KT1), 0.5)
-        act(C(PA32), C(KT2), 16.0, 16.0)
-        act(C(KB + 1), C(P15), 1.0, 16.5)
-        act(C(PB32), C(PA32), -2.0, C(KT1))
-        act(C(PL1), C(P31), 1.0, C(PA32))
-        act(C(P64), C(PP), 1.0, 64.0)
-        act(C(NB), C(PL1), 1.0, C(PB32))
-        act(S(R16X, 4), A("row", 0, 4), 16.0)
-        act(C(CKS + 1), C(NB), -SA * SB, 64 * SA * SB)
-        act(C(NCK + 1), C(NB), 1.0, -64.0)
-        act(S(NEG), A("ones", 0, 8), -1.0)
-
-    def columns2():
-        act(C(NB), C(P31), 1.0, C(PA48))
-        act(C(P128), C(PP), 1.0, 128.0)
-        act(C(CKS + 2), C(NB), -SA * SB, 32 * SA * SB)
-        act(C(NCK + 2), C(NB), 1.0, -32.0)
-        k64(2)
+        ts(A("ci", PA32), pi, 1, OP.logical_shift_right, 32, OP.bitwise_and)
+        ts(A("ci", PA48), pi, 1, OP.logical_shift_right, 48, OP.bitwise_and)
+        ts(A("ci", PB32), pi, 32, OP.bitwise_and)
 
     def s_tile(l):
         for b in range(4):
@@ -306,46 +287,39 @@ def rank_program(g, core, T, topo):
 
     def masks():
         ts(S(M8), A("row", 0, 8), C(PH), OP.is_equal)
-        ts(S(Q4, 4), A("row", 0, 4), 16.0, OP.mult, C(PA48), OP.is_equal)
-        ts(S(Q4 + 4, 2), A("row", 0, 2), 32.0, OP.mult, C(PB32), OP.is_equal)
-        act(A("sm", MK0, MK0 + 2), A("sm", M8, M8 + 2))
-        act(A("sm", MK0 + 2, MK0 + 4), A("sm", M8 + 6, M8 + 8))
-        act(S(Q4S, 6), S(Q4, 6), SA)
-        act(S(M8B), S(M8), 128.0)
-        act(A("sm", MK1, MK1 + 4, 2), A("sm", M8 + 3, M8 + 8, 4))
-        act(A("sm", MK1 + 1, MK1 + 4, 2), A("sm", M8, M8 + 5, 4))
+        ts(S(M8B), A("row", 0, 8), C(PH), OP.is_equal, 128.0, OP.mult)
+        ts(S(MK0), S(KT), C(PH), OP.is_equal)
 
     def kin_piv(l):
-        ts(LV(l, PIV), LV(l, RANK), (64 >> l) - 0.5, OP.is_lt)
-        act(LV(l, NON), LV(l, PIV), -1.0, 1.0)
-        act(LV(l, PC), LV(l, PIV), C(P128 if l == 2 else P64))
-        act(LV(l, PJ), LV(l, PIV), C([PP, PL1, P31][l]))
+        th = (64 >> l) - 0.5
+        ts(LV(l, NON), LV(l, RANK), th, OP.is_ge)
+        ts(LV(l, PC), LV(l, RANK), th, OP.is_lt, C(P128 if l == 2 else P64), OP.mult)
+        ts(LV(l, PJ), LV(l, RANK), th, OP.is_lt, C([PP, PL1, P31][l]), OP.mult)
 
     def kin_pos(l):
         ts(A("th", 0, 256, 4), A("k64", 64 * l, 64 * l + 64), LV(l, PM), OP.is_equal, 64.0, OP.mult)
 
+    def kin_par(l):
+        ts(A("th", 256, 768, 4), A("row"), LV(l, V_), OP.is_equal)
+
     RM = [(M8, M8B, 8, "qwc"), (MC0, MC0B, 4, "qk0"), (MC1, MC1B, 4, "qk1")]
+    HB = [7, 7, 6]
 
     def kin_a(l):
         n, e = RM[l][2], 4 * (TL + 8)
-        return [lambda: act(LV(l, UU), LV(l, PM), 1.0 / (SA * SB), C(NCK + l)),
-                lambda: act(LV(l, AA), LV(l, UU), LV(l, NON), LV(l, PC)),
-                lambda: act(LV(l, T3), LV(l, AA), 1.0, M32),
-                lambda: act(LV(l, NH), LV(l, T3), -1.0, M32),
-                lambda: act(A("tz", e, e + 4 * n, 4), S(NEG, n), LV(l, NH)),
-                lambda: act(A("tz", e + 1, e + 4 * n, 4), S(RM[l][0], n), LV(l, AA), LV(l, NH))]
-
-    def kin_hs(l):
-        act(A("ab"), A("row"), -1.0, LV(l, V_), AF.Abs)
-        act(A("th", 256, 768, 4), A("ab"), -1.0, 1.0, AF.Relu)
+        return [lambda: ts(LV(l, UU), LV(l, PM), 1.0 / (SA * SB), OP.mult, C(NK[l]), OP.add),
+                lambda: ts(LV(l, AA), LV(l, UU), LV(l, NON), OP.mult, LV(l, PC), OP.add),
+                lambda: ts(LV(l, HA), LV(l, AA), M32, OP.add, M32, OP.subtract),
+                lambda: (ts(A("tz", e, e + 4 * n, 4), A("ones", 0, n), LV(l, HA), OP.mult),
+                         ts(A("tz", e + 1, e + 4 * n, 4), S(RM[l][0], n), LV(l, AA), OP.mult, LV(l, HA), OP.subtract))]
 
     def kin_h(l):
         quant("qh", 0, "th", 0, 192)
-        mm(6, "qh", 64, "qh", 0)
+        mm(HB[l], "qh", 64, "qh", 0)
 
     def kin_first(l):
-        scan(A("so", 0, 64), P(6, 0, 64), A("ones"), -64.0, OP.max, OP.add)
-        scan(A("so", 64, 128), P(6, 0, 64), A("st16"), -64.0, OP.max, OP.add)
+        scan(A("so", 0, 64), P(HB[l], 0, 64), A("ones"), -64.0, OP.max, OP.add)
+        scan(A("so", 64, 128), P(HB[l], 0, 64), A("st16"), -64.0, OP.max, OP.add)
 
     def kin_has(l):
         n, e = RM[l][2], 4 * (TL + 8) + 2
@@ -356,6 +330,8 @@ def rank_program(g, core, T, topo):
         ts(A("tz", 4 * TL + 1, 4 * TL + 32, 4), S(M8), A("so", 63), OP.mult, A("so", 127), OP.subtract)
         if l < 2:
             kin_has(l)
+
+    def kin_list(l):
         quant("ql", 0, "tz", 4 * TL, 136)
         mm(6, "qwc", 0, "ql", 0)
         if l < 2:
@@ -383,12 +359,16 @@ def rank_program(g, core, T, topo):
     def up(l):
         n, bn, bo = 128 >> l, "buf%d" % l, BO[l]
         mm(4, bn, bo, bn, bo)
-        for b in range(4):
-            mm(b, "qe", 128 * b, bn, bo)
         fill(1)
         tt(A("mx", 0, 128), P(4, 0, 128), A("idn", 0, 128), OP.mult)
+        if l == 0:
+            quant("qe", 256, "the", 1, 128)
         act(A("gs"), P(4, 0, 128), 2.0 ** -18)
         scan(A("xs"), A("mx"), A("mx"), TINY, OP.max, OP.max)
+        if l == 0:
+            quant("qe", 384, "the", 0, 128)
+        for b in range(4):
+            mm(b, "qe", 128 * b, bn, bo)
         act(A("thr", 0, n), A("fm", 0, n), A("xs", 159))
         tr(A("zz", 0, 32), A("xs", 128, 160))
         if l < 2:
@@ -402,7 +382,11 @@ def rank_program(g, core, T, topo):
         for b in range(4):
             act(A("dm", b, 512, 4), P(b, 0, 128), -1.0)
         tt(A("bm", 0, n), A("zz", 0, n), A("thr", 0, n), OP.is_gt)
+        if l < 2:
+            fill(1)
         red(LV(l, RANK), A("bm", 0, n))
+        if l < 2:
+            fill(1)
         ts(A("ta", 0, 517, 4), A("kk", 130 * l, 130 * l + 130), LV(l, RANK), OP.is_gt, SB, OP.mult)
         quant("qa", 0, "ta", 0, 130)
         mm(5, "qs%d" % l, 0, "qa", 0, 130)
@@ -416,39 +400,43 @@ def rank_program(g, core, T, topo):
         scan(A("rm"), A("mk"), A("mk"), -BIG, OP.max, OP.max)
         act(A("jk", 0, 128), A("rm"), -1.0, A("rm", 127), AF.Sign, LV(l, V_))
         act(A("jk", 128, 136), A("rm", 15, 128, 16), -1.0, A("rm", 127), AF.Sign, LV(l, H_))
-        if l < 2:
-            act(A("tz", 4 * TP, 4 * TP + 64), A("ones"), LV(l, H_))
+        act(A("tz", 4 * TP, 4 * TP + 64), A("ones"), LV(l, H_))
         quant("qn", 0, "tz", 4 * TN, 144)
         mm(6, "qw64", 0, "qn", 0, 128, True, False)
         mm(6, "qw64", 0, "qn", 16, 128, False, True)
         ts(A("eq"), kk, pm, OP.is_equal, 1.0 / 16, OP.mult)
         cp(LV(l, PM), pm)
         if l == 2:
-            kin_hs(l)
             kin_pos(l)
-            ts(A("tz", 4 * TP, 4 * TP + 64), A("ones"), LV(l, H_), OP.mult)
+            kin_a(l)[0]()
+            kin_par(l)
         ts(A("tz", 4 * TP + 64, 4 * TP + 128), A("eq"), LV(l, V_), OP.mult, LV(l, H_), OP.subtract)
         ts(A("on"), P(6, 0, 16), C(P3), OP.add)
         run("a", [A("dm"), A("on")], [A("dn")],
             lambda: g.scalar.activation(T.dn[:], T.dm[:].indirect(T.on[:]), AF.Copy, scale=-2.0))
+        if l == 2:
+            kin_h(l)
         quant("qp", 0, "tz", 4 * TP, 144)
         mm(7, "qw64", 0, "qp", 0, 128, True, False)
         mm(7, "qw64", 0, "qp", 16, 128, False, True)
         if l == 2:
-            kin_h(l)
+            kin_a(l)[1]()
+            kin_first(l)
+            kin_a(l)[2]()
             for b in range(4):
                 mm(b, "qe", 128 * b, bn, bo, 128, True, False)
+            kin_tile(l)
         else:
             fill(1)
         ts(A("op"), P(7, 0, 16), C(P3), OP.add)
         if l == 2:
-            kin_first(l)
-            kin_tile(l)
-            weave(kin_a(l), [])
+            kin_list(l)
         run("v", [A("dm"), A("op"), A("dn")], [A("te", 0, 256)],
             lambda: g.vector.tensor_tensor(T.te[:, 0:256], T.dm[:].indirect(T["op"][:]), T.dn[:], OP.add))
         if l == 2:
             kin_c(l)
+        if l == 0:
+            fill(1)
         quant("buf2" if l == 2 else "pool%d" % l, 0, "te", 0, 128)
 
     def exchange(l):
@@ -457,61 +445,58 @@ def rank_program(g, core, T, topo):
         remote(peer, 3 * l + 1, A(pool + "s", 0, 64), A(pool + "s", 128, 192), False)
         mm(4, "ur", 96 * l, pool, 0)
         mm(5, pool, 0, "ur", 96 * l)
-        fill(1)
+        kin_pos(l)
+        kin_par(l)
         if l == 0:
             ts(A("mk", 0, 64, 1, 0, 64), P(4, 0, 64, 0, 64), P(5, 0, 1, 0, 64), OP.subtract)
         else:
             ts(A("mk", 0, 64, 1, 0, 32), P(4, 0, 64, 0, 32), P(5, 0, 1, 0, 32), OP.subtract)
             ts(A("mk", 0, 64, 1, 32, 64), P(4, 0, 64, 32, 64), P(5, 32, 33, 32, 64), OP.subtract)
+        kin_h(l)
         tt(A("tz", 4 * TF + 1, 4 * TF + 256, 4, 0, 64), A("mk", 0, 64, 1, 0, 64), A("ls", 64 * l, 64 * l + 64, 1, 0, 64), OP.is_lt)
+        fill(1)
         quant("qf", 0, "tz", 4 * TF, 128)
         mm(6, "qs0", 0, "qf", 0)
+        kin_first(l)
         fill(1)
         ts(A("d0"), P(6, 0, 64), ((32 >> l) - 0.5) * SA, OP.is_lt, -1.0, OP.mult)
+        kin_tile(l)
         scan(A("cs", 0, 64), A("d0"), A("ones"), 0.0, OP.add, OP.add)
         scan(A("cs", 64, 128), A("d0"), A("ones"), 0.0, OP.add, OP.min)
         for go, c in ((0, 0), (0, 1), (1, 0), (1, 1)):
             at = 2 * go + c if l == 0 else 2 * c + 1 - go
             act(A("jk", 64 * at, 64 * at + 64), A("cs", 64 * go, 64 * go + 64), 2.0 * go - 1.0, C(KB + c), AF.Sign, C(ACC + at))
+        ka = kin_a(l)
+        ka[0]()
         fill(1)
+        ka[1]()
         acc = A("cf", ACC, ACC + 4)
         ts(A("lst%d" % l), acc, 0.5, OP.mult, 32.0, OP.add)
         remote(peer, 3 * l + 2, A("lst%d" % l), A("lin%d" % l), False)
         nb, bo = "buf%d" % (l + 1), BO[l + 1]
+        if l == 1:
+            ts(A("o2", 0, 8, 2), acc, 0.5, OP.mult, 32.0, OP.add)
+        tt(S(KT, 4), acc, S(MK0 + 4 * l, 4), OP.mult)
+        ka[2]()
         if l == 0:
             pick(nb, bo, pool, 0, 64, A("lst0", 0, 2))
             pick(nb, bo + 96, pool, 0, 64, A("lst0", 2, 4))
         else:
-            ts(A("o2", 0, 8, 2), acc, 0.5, OP.mult, 32.0, OP.add)
-        tt(S(KT, 4), acc, S([MK0, MK1][l], 4), OP.mult)
-        if l == 1:
             for c, at in ((1, 0), (0, 48), (3, 64), (2, 112)):
                 pick(nb, bo + at, pool, 0, 64, A("o2", 2 * c))
         red(C(KO), S(KT, 4))
+        ka[3]()
 
     def origin_a(l):
-        return [lambda: act(C(KT1), C(KO), 0.5, 24.5),
-                lambda: act(C(KT2), C(KT1), 1.0, M16),
-                lambda: act(C(KHI), C(KT2), 1.0, -M16),
-                lambda: act(C(KT1), C(KHI), -1.0, 32.0),
-                lambda: act(C(KLO), C(KO), 0.5, C(KT1))]
+        return [lambda: ts(C(KT1), C(KO), 0.5, OP.mult, 24.5, OP.add),
+                lambda: ts(C(KHI), C(KT1), M16, OP.add, M16, OP.subtract),
+                lambda: ts(C(KLO), C(KT1), 7.5, OP.add, C(KHI), OP.subtract)]
 
     def origin_v(l):
         mc, mcb = [(MC0, MC0B), (MC1, MC1B)][l]
         ts(S(mc, 4), S(R16X, 4), C(KHI), OP.is_equal, C(OWN0 + l), OP.mult)
         act(S(mcb, 4), S(mc, 4), 128.0)
         rows("r16", C(KLO), 3)
-
-    def kin_all(l):
-        kin_pos(l)
-        kin_h(l)
-        weave(kin_a(l), origin_a(l))
-        parents_out(l)
-        kin_first(l)
-        kin_tile(l)
-        fill(1)
-        kin_c(l)
-        kin_r(l)
 
     def arrive(l):
         nb, bo, pool = "buf%d" % (l + 1), BO[l + 1], "pool%d" % l
@@ -527,6 +512,7 @@ def rank_program(g, core, T, topo):
         for b in range(4):
             mm(b, "qe", 128 * b, ch, 0, 128, False, True)
         if l == 2:
+            kin_a(l)[3]()
             kin_has(l)
             quant("qr", 0, "tz", 4 * (TL + 8), 128)
             mm(7, RM[l][3], 0, "qr", 0)
@@ -547,41 +533,49 @@ def rank_program(g, core, T, topo):
         else:
             pick("ff", 0, bn, 0, bo + 256, A("or0"))
 
-    k64(0)
     later += [lambda: (quant("uq", 0, "ut", 0, 128), send_u()),
-              lambda: (quant("qw64", 0, "tg", 0, 128), ms(A("o0", 0, 4), 0), columns1()),
+              lambda: (columns1(), act(A("th", 256, 768), A("ts"), 0.0, 1.0)),
+              lambda: (k64(0), ts(A("cf", KB, KB + 2), S(R16X, 2), C(P15), OP.add, 0.5, OP.add),
+                       cp(A("cf", PA32, PA32 + 3), A("ci", PA32, PA32 + 3))),
+              lambda: (quant("qw64", 0, "tg", 0, 128), ms(A("o0", 0, 4), 0),
+                       ts(A("st16"), A("r16", 0, 64), 15.0, OP.is_equal, 16.0, OP.mult)),
               lambda: (pick("ur", 0, "uq", 0, 32, A("o0", 0, 8)),
-                       act(A("ls", 0, 64), A("am", 0, 64), -TINY, 2 * TINY, AF.Relu),
-                       act(A("th", 256, 768), A("ts"), 0.0, 1.0), k64(1))]
+                       act(A("ls", 0, 64), A("am", 0, 64), -TINY, 2 * TINY, AF.Relu)),
+              lambda: (ms(A("th", 1, 256, 4, 0, 1), -64.0), ts(C(PL1), C(P31), C(PA32), OP.add),
+                       ts(S(Q4S + 4, 2), A("sm", R16X, R16X + 4, 2), C(PB32), OP.is_equal, SA, OP.mult))]
     up(0)
-    later += [masks,
-              lambda: (ts(A("st16"), A("r16", 0, 64), 15.0, OP.is_equal, 16.0, OP.mult), ms(A("th", 1, 256, 4, 0, 1), -64.0)),
-              lambda: (rows("r16", C(P15), 3), kin_piv(0))]
+    later += [lambda: (masks(), s_tile(1)),
+              lambda: kin_piv(0),
+              lambda: rows("r16", C(P15), 3)]
     exchange(0)
-    kin_hs(0)
-    s_tile(1)
-    quant("qwc", 0, "tg", 0, 128)
-    later += [lambda: quant("qs1", 0, "ts", 0, 128)]
-    kin_all(0)
+    weave(origin_a(0), [lambda: quant("qwc", 0, "tg", 0, 128),
+                        lambda: (ts(C(NK[1]), C(PL1), C(PB32), OP.add, -64.0, OP.add), quant("qs1", 0, "ts", 0, 128))])
+    kin_list(0)
+    k64(1)
     act(A("kk", 130, 260), A("idn"), 32.5, -1.0)
+    parents_out(0)
+    red(C(OWN0), S(MK0, 4))
+    red(C(OWN0 + 1), S(MK0 + 4, 4))
+    cp(A("ls", 64, 128), A("ls", 0, 64))
     arrive(0)
-    later += [nothing,
-              lambda: (pick("ur", 128, "ub", 0, 32, A("o0", 4, 10)), act(A("jk", 256, 260), S(MK0, 4), acc=C(OWN0)),
-                       act(A("ls", 64, 128), A("ls", 0, 64)), act(A("jk", 260, 264), S(MK1, 4), acc=C(OWN0 + 1)),
-                       act(A("ls", 96, 128, 1, 0, 32), A("ones", 0, 32, 1, 0, 32), -BIG),
-                       act(A("ls", 64, 96, 1, 32, 64), A("ones", 0, 32, 1, 32, 64), -BIG), columns2()),
+    later += [lambda: (kin_c(0), kin_r(0)),
+              lambda: (ms(A("ls", 96, 128, 1, 0, 32), -BIG), ms(A("ls", 64, 96, 1, 32, 64), -BIG)),
+              lambda: ts(S(Q4S, 4), S(R16X, 4), C(PA48), OP.is_equal, SA, OP.mult),
+              lambda: pick("ur", 128, "ub", 0, 32, A("o0", 4, 10)),
               lambda: (origin_v(0), act(A("ts2"), A("ts"), 0.0, SA), s_tile(2))]
     up(1)
     later += [lambda: quant("qk0", 0, "tg", 0, 128),
-              lambda: (kin_piv(1), act(A("kk", 260, 390), A("idn"), 16.5, -1.0)),
+              lambda: kin_piv(1),
               lambda: quant("wq", 0, "wt", 0, 128)]
     exchange(1)
-    kin_hs(1)
-    quant("qs2", 0, "ts2", 0, 128)
-    later += [lambda: origin_v(1)]
-    kin_all(1)
-    quant("qk1", 0, "tg", 0, 128)
+    act(A("kk", 260, 390), A("idn"), 16.5, -1.0)
+    weave(origin_a(1), [lambda: quant("qs2", 0, "ts2", 0, 128),
+                        lambda: (ts(C(NK[2]), C(P31), C(PA48), OP.add, -32.0, OP.add), kin_list(1))])
+    k64(2)
+    parents_out(1)
+    origin_v(1)
     arrive(1)
+    later += [lambda: (kin_c(1), kin_r(1)), lambda: quant("qk1", 0, "tg", 0, 128)]
     up(2)
     later += [lambda: quant("wq", 128, "wt", 512, 128), lambda: quant("wq", 256, "wt", 1024, 128)]
     down(2)

@@ -1,43 +1,42 @@
+from concourse.bass import DstId, RemoteDMATransfer
 from concourse.mybir import dt, AluOpType, AxisListType, ActivationFunctionType
 
 OP = AluOpType
 AF = ActivationFunctionType
 MX, U8, F32, BF, U16, I32 = "float8_e4m3fn_x4", "uint8", "float32", "bfloat16", "uint16", "int32"
 
-CODES = {"qa": 130, "qn": 144, "qp": 144, "ql": 136, "qr": 128, "qf": 128, "qh": 192, "qs0": 128, "qs1": 128, "qs2": 128,
-         "qe": 512, "qw64": 128, "qwc": 128, "qk0": 128, "qk1": 128, "uq": 128, "ub": 32, "ur": 224,
-         "wq": 384, "pool0": 192, "pool1": 192, "buf0": 320, "buf1": 320, "buf2": 384, "ch0": 128,
-         "ch1": 128, "ch2": 128, "ff": 128}
+CODES = {"qa": 130, "qn": 144, "qp": 144, "ql": 128, "qr": 128, "qb": 128, "qh": 320, "qs0": 128, "qs1": 128, "qs2": 128,
+         "qe": 512, "qw64": 128, "qwc": 128, "qo": 128, "uq": 160, "ur": 512, "wq": 384,
+         "buf0": 320, "buf1": 320, "buf2": 384, "ch0": 128, "ch1": 128, "ch2": 128, "ff": 128}
 SCRATCH = {}
 for _n, _c in CODES.items():
     SCRATCH[_n] = ("sbuf", [128, _c], MX)
     SCRATCH[_n + "s"] = ("sbuf", [128, _c], U8)
-for _n, _c, _d in [("xt", 512, BF), ("ut", 512, BF), ("wt", 1536, BF), ("ta", 520, BF), ("ts", 512, BF), ("ts2", 512, BF),
-                   ("the", 516, BF), ("tz", 832, BF), ("te", 512, BF), ("th", 768, BF), ("tg", 512, BF),
+for _n, _c, _d in [("xt", 512, BF), ("ut", 512, BF), ("wt", 1536, BF), ("ta", 520, BF), ("ts", 512, BF),
+                   ("the", 516, BF), ("tz", 840, BF), ("te", 512, BF), ("th", 1280, BF), ("tg", 512, BF),
                    ("td", 512, BF), ("r16", 128, BF), ("ra", 128, BF),
-                   ("row", 128, F32), ("idn", 130, F32), ("am", 128, F32), ("sf", 128, F32),
-                   ("fm", 128, F32), ("kk", 390, F32), ("k64", 192, F32), ("ls", 128, F32), ("ones", 64, F32),
-                   ("mx", 160, F32), ("xs", 160, F32), ("zz", 128, F32), ("thr", 128, F32), ("bm", 128, F32),
-                   ("gs", 128, F32), ("mk", 128, F32), ("rm", 128, F32), ("jk", 264, F32), ("eq", 64, F32),
-                   ("dm", 512, F32), ("dn", 256, F32), ("d0", 64, F32), ("so", 128, F32), ("cs", 128, F32),
-                   ("st16", 64, F32), ("sm", 112, F32),
-                   ("cf", 96, F32), ("ci", 16, I32), ("ysb", 384, F32),
-                   ("on", 16, U16), ("op", 16, U16), ("lst0", 4, U16), ("lst1", 4, U16), ("lin0", 4, U16),
-                   ("lin1", 4, U16), ("o2", 8, U16), ("oc0", 8, U16), ("oc1", 8, U16), ("oc2", 8, U16),
-                   ("or0", 8, U16), ("or1", 8, U16), ("or2", 8, U16), ("o0", 10, U16)]:
+                   ("row", 128, F32), ("idn", 128, F32), ("am", 128, F32), ("sf", 128, F32), ("kk", 128, F32),
+                   ("psi", 128, F32), ("k64", 192, F32), ("ls", 128, F32), ("ones", 64, F32), ("pc", 64, F32),
+                   ("mx", 136, F32), ("xs", 128, F32), ("zz", 128, F32), ("bm", 136, F32), ("same", 128, F32),
+                   ("gs", 128, F32), ("gt", 128, F32), ("mk", 128, F32), ("rm", 128, F32), ("jk", 272, F32),
+                   ("eq", 64, F32), ("dm", 512, F32), ("dn", 256, F32), ("so", 128, F32), ("plr", 256, F32),
+                   ("st16", 64, F32), ("sm", 16, F32), ("cf", 128, F32), ("ci", 16, I32), ("ysb", 384, F32),
+                   ("on", 16, U16), ("op", 16, U16), ("oc0", 8, U16), ("oc1", 8, U16), ("oc2", 8, U16),
+                   ("or0", 8, U16), ("or1", 8, U16), ("or2", 8, U16), ("ou", 32, U16)]:
     SCRATCH[_n] = ("sbuf", [128, _c], _d)
 for _k in range(8):
     SCRATCH["ps%d" % _k] = ("psum", [128, 512], F32)
 
 NDMA = 16
-SEMAPHORES = ["sv", "sa", "sp", "sg", "sent"] + ["d%d" % k for k in range(NDMA)] + ["r%d" % k for k in range(8)]
+SEMAPHORES = ["sv", "sa", "sp", "sg", "sent", "ru"] + ["d%d" % k for k in range(NDMA)] + ["r%d" % k for k in range(4)]
 
 PART = [4, 2]
-BO = [64, 64, 128]
+BASE = [0, 0, 64]
+USLOT = {4: 128, 2: 132, 6: 136}
 TINY = 2.0 ** -100
 BIG = 1e29
 BELOW = 1.0 - 2.0 ** -24
-M16, M32 = 1.5 * 2.0 ** 27, 1.5 * 2.0 ** 28
+M32 = 1.5 * 2.0 ** 28
 SA, SB = 2.0 ** 22, 2.0 ** 29
 TP, TN, TL, TF = 0, 32, 64, 80
 
@@ -78,7 +77,7 @@ def rank_program(g, core, T, topo):
         need = {}
         for accs, wr in ((reads, False), (writes, True)):
             for a in accs:
-                psum = a[1].startswith("ps")
+                psum = SCRATCH[a[1]][0] == "psum"
                 for (p0, p1, cols, w, oq, tok) in log.get(a[1], []):
                     if psum:
                         if oq == q and (q == "p" or not (w or wr)):
@@ -129,6 +128,25 @@ def rank_program(g, core, T, topo):
         count["r%d" % k] = back
         note("net", [], [dst], ("r%d" % k, back))
 
+    def send_u():
+        peers = [T.cores[rank ^ k] for k in USLOT]
+        m = topo.mask(core, peers[0])
+        for c in peers:
+            m &= topo.mask(core, c) & topo.mask(c, core)
+        n = bin(m).count("1")
+        ids = [DstId(rid=topo.addr(c, core)[0], pnc=topo.addr(c, core)[1]) for c in peers]
+        for name in ("uq", "uqs"):
+            src, dsts = A(name, 0, 4), [A(name, USLOT[k], USLOT[k] + 4) for k in USLOT]
+            order("g", [src], [])
+            a, bs = src[0], [d[0] for d in dsts]
+            if name == "uq":
+                a, bs = a.bitcast(dt.uint8), [b.bitcast(dt.uint8) for b in bs]
+            g.remote_dma_fused([RemoteDMATransfer(dst_ids=ids, dma_engine_mask=m, remote_sem=T.sem.ru, srcs=[a], dsts=bs)],
+                               local_sem=T.sem.sent)
+            count["sent"] = count.get("sent", 0) + n
+        count["ru"] = 2 * len(peers) * n
+        note("net", [], [A("uq", 128, 140), A("uqs", 128, 140)], ("ru", count["ru"]))
+
     def ts(out, in0, s1, op0, s2=None, op1=None):
         if op1 is None:
             run("v", [in0, s1], [out], lambda: g.vector.tensor_scalar(out[0], in0[0], val(s1), None, op0))
@@ -144,8 +162,8 @@ def rank_program(g, core, T, topo):
     def ms(out, c):
         run("v", [], [out], lambda: g.vector.memset(out[0], c))
 
-    def red(out, a):
-        run("v", [a], [out], lambda: g.vector.tensor_reduce(out[0], a[0], AxisListType.X, OP.add))
+    def red(out, a, op=OP.add):
+        run("v", [a], [out], lambda: g.vector.tensor_reduce(out[0], a[0], AxisListType.X, op))
 
     def scan(out, a, b, init, op0, op1):
         run("v", [a, b], [out], lambda: g.vector.tensor_tensor_scan(out[0], a[0], b[0], init, op0, op1))
@@ -192,138 +210,141 @@ def rank_program(g, core, T, topo):
     def C(k, p0=0, p1=128):
         return A("cf", k, k + 1, 1, p0, p1)
 
-    P31, P15, PH, P3, PA32, PA48, PB32, IL, PL1 = range(9)
-    PP, P64, P128, NK = 82, 83, 84, [80, 16, 17]
-    KO, KLO, KHI, OWN0, KB, KT1, ACC = 19, 20, 21, 22, 24, 26, 28
+    P31, P15, PH, P3, PQ, IL, HB, HS, NA, NB = range(10)
+    PP, P64 = 122, 123
 
-    def LV(l, k):
-        return C(32 + 16 * l + k)
-    RANK, V_, H_, PM, NON, PC, PJ, UU, AA, PAO, T1, T2, HA = range(13)
-    M8, M8B, MK0, MC0, MC0B, MC1, MC1B, R16X, KT, Q4S = [8 * k for k in range(10)]
+    def LV(l, k, p0=0, p1=128):
+        return C(16 + 28 * l + k, p0, p1)
+    (RANK, V_, H_, PM, PLR, NON, PC, PJ, UU, AA, VP, HA, D_, SG, R_, SH, T1, T2, KAP, PHI, TAU, NK, NR, NK2, PLV,
+     PAO) = range(26)
+    M8, M8B = 0, 8
 
     def S(k, n=8):
         return A("sm", k, k + n)
 
-    later, stores = [], []
-
-    def fill(n):
-        for _ in range(n):
-            if later:
-                later.pop(0)()
-
-    def weave(a, b):
-        for k in range(max(len(a), len(b))):
-            for x in (a, b):
-                if k < len(x):
-                    x[k]()
+    stores = []
 
     dma("s", T.xt[:], T.x[:], [], [A("xt")])
     dma("s", T.ut[:], T.u[:], [], [A("ut")])
     iota(A("row"), [[1, 128]])
-    iota(A("cf", 80, 85), [[64, 5]], -128, 1)
+    iota(A("cf", 120, 125), [[64, 5]], -128, 1)
     iota(A("ci", 15), [[0, 1]], 0, 1, False)
     ms(A("ta"), 0.0)
+    ms(A("psi", 0, 96), 4.0)
     ms(A("ones"), 1.0)
-    ms(A("mx", 128, 160), 0.0)
-    ms(A("idn", 128, 130), 1.0)
+    ms(A("mx", 128), TINY)
+    ms(LV(0, SG), 0.5)
+    ms(A("psi", 0, 32, 1, 32, 64), 4.0 * BELOW)
+    ms(A("psi", 0, 32, 1, 96, 128), 4.0 * BELOW)
     act(A("the"), A("ta", 0, 516))
-    ts(A("idn", 0, 128), A("row"), C(PP), OP.is_equal)
-    ts(A("sf"), A("row"), C(PP), OP.is_lt, 1.0, OP.add)
+    ts(A("idn"), A("row"), C(PP), OP.is_equal)
+    ts(A("sf"), A("row"), C(PP), OP.is_gt, 1.0, OP.add)
     run("g", [A("sf")], [A("am")], lambda: g.affine_select(T.am[:], T.sf[:], [[-1, 128]], OP.not_equal, 128.0, 0, 1))
     iota(A("ra"), [[0, 8], [1, 4], [0, 4]])
-    iota(A("r16"), [[0, 8], [1, 16]])
-    iota(S(R16X, 4), [[16, 4]])
-    iota(S(KT, 4), [[6, 2], [1, 2]])
-    iota(S(KT + 4, 4), [[4, 2], [-3, 2]], 3)
-    iota(A("tz"), [[0, 832]])
+    iota(A("tz"), [[0, 840]])
     pi = A("ci", 15)
     ts(A("ci", P31), pi, 31, OP.bitwise_and)
     ts(A("ci", P15), pi, 15, OP.bitwise_and)
     ts(A("ci", PH), pi, 4, OP.logical_shift_right)
     ts(A("ci", P3), pi, 3, OP.bitwise_and)
-    cp(A("cf", 0, 4), A("ci", 0, 4))
-    act(A("the", 3, 515, 4), A("idn", 0, 128), 0.5)
+    ts(A("ci", PQ), pi, 5, OP.logical_shift_right, 1, OP.bitwise_and)
+    ms(C(HB, 0, 64), BIG)
+    ms(C(HB, 64, 128), -BIG)
+    cp(A("cf", 0, 5), A("ci", 0, 5))
+    act(A("the", 3, 515, 4), A("idn"), 0.5)
+    ms(A("bm", 128), -64.5)
+    ms(A("ta", 516), SB)
+    ts(A("psi", 96, 128), A("row", 0, 32), C(P31), OP.is_ge, BELOW, OP.max)
     act(A("ts"), A("ta", 0, 512), 1.0, SA)
-    act(A("kk", 0, 130), A("idn"), 64.5, -1.0)
+    act(A("psi", 96, 128), A("psi", 96, 128), 4.0)
+    act(A("ta", 1, 512, 4), A("idn"), -0.5 * SB)
     act(A("ts", 0, 512, 4), A("am"), SA)
-    act(A("ta", 1, 512, 4), A("idn", 0, 128), -0.5 * SB)
-    ms(A("fm", 32, 128), 1.0)
-    for c0, p0, p1 in ((32, 64, 128), (96, 64, 128), (64, 32, 64), (64, 96, 128)):
-        ms(A("fm", c0, c0 + 32, 1, p0, p1), BELOW)
-    ts(A("fm", 0, 32), A("row", 0, 32), C(P31), OP.is_ge, BELOW, OP.max)
-    for b in range(2):
-        quant("qe", 128 * b, "the", 3 - b, 128)
-    for t in range(4):
-        ts(A("tg", t, 512, 4), A("ra"), float(t), OP.is_equal, 64.0, OP.mult)
     act(C(IL), C(P15), 1.0 / 16)
-    ms(A("o0", 4, 10), 1)
-    quant("qs0", 0, "ts", 0, 128)
-    quant("buf0", BO[0], "xt", 0, 128)
+    quant("buf0", 64, "xt", 0, 128)
     wait("s", ("d1", 16))
     dma("s", T.wt[:], T.w[:], [], [A("wt")])
 
-    def k64(l):
-        ts(A("k64", 64 * l, 64 * l + 64), A("row", 0, 64), C(NK[l]), OP.subtract, SA * SB, OP.mult)
+    def u_list(*groups):
+        for c0, c1, v in groups:
+            ms(A("ou", c0, c1), v)
 
-    def rows(src, scal, n):
-        for t in range(n):
-            ts(A("tg", t, 512, 4), A(src), scal, OP.is_equal)
-
-    def send_u():
-        remote(rank ^ PART[0], 6, A("uq", 0, 2), A("ub", 0, 2), True)
-        remote(rank ^ PART[0], 7, A("uqs", 0, 2), A("ubs", 0, 2), False)
-        iota(A("te", 256, 512), [[0, 256]])
+    def u_send():
+        quant("uq", 0, "ut", 0, 128)
+        send_u()
         iota(A("th", 0, 256), [[0, 256]])
+        iota(A("te", 0, 256), [[0, 256]])
+        iota(A("r16"), [[0, 8], [1, 16]])
 
-    def columns1():
-        ts(A("ci", PA32), pi, 1, OP.logical_shift_right, 32, OP.bitwise_and)
-        ts(A("ci", PA48), pi, 1, OP.logical_shift_right, 48, OP.bitwise_and)
-        ts(A("ci", PB32), pi, 32, OP.bitwise_and)
+    def u_pick(k):
+        pick("ur", 128 * k, "uq", 0, 160, A("ou", 8 * k, 8 * k + 8))
 
-    def s_tile(l):
-        for b in range(4):
-            act(A(["", "ts", "ts2"][l], 128 * b, 128 * b + 128, 4), A("am", 32 * b, 32 * b + 32),
-                A("sm", Q4S + (4 + b % 2 if l == 1 else b)))
+    def rows4(t0, t1):
+        for t in range(t0, t1):
+            ts(A("tg", t, 512, 4), A("ra"), float(t), OP.is_equal, 64.0, OP.mult)
 
-    def masks():
-        ts(S(M8), A("row", 0, 8), C(PH), OP.is_equal)
-        ts(S(M8B), A("row", 0, 8), C(PH), OP.is_equal, 128.0, OP.mult)
-        ts(S(MK0), S(KT), C(PH), OP.is_equal)
+    def rows16(t0, t1):
+        for t in range(t0, t1):
+            ts(A("tg", t, 512, 4), A("r16"), C(P15), OP.is_equal)
+
+    def unpackers(b0, b1):
+        for b in range(b0, b1):
+            quant("qe", 128 * b, "the", 3 - b, 128)
+
+    def halves(f):
+        f(0, 64, 64)
+        f(64, 128, 0)
+
+    def quarters(name, c, ks):
+        for k in ks:
+            ms(A(name, 32 * (k ^ 1), 32 * (k ^ 1) + 32, 1, 32 * k, 32 * k + 32), c)
+
+    def counts(l):
+        ms(A("tz", 4 * TF + 2, 4 * TF + 512, 4, 0, 1), -float(64 >> l))
+        ms(A("tz", 4 * TF + 513), 0.5 - (64 >> l))
+        ms(A("bm", 128), -0.5 - (64 >> l))
+
+    def score_order():
+        ts(A("ls", 0, 64, 1, 0, 64), A("row", 0, 64, 1, 0, 64), C(PP, 0, 64), OP.is_lt, -TINY, OP.mult)
+        ts(A("ls", 64, 128, 1, 64, 128), A("row", 64, 128, 1, 64, 128), C(PP, 64, 128), OP.is_gt, -TINY, OP.mult)
 
     def kin_piv(l):
-        th = (64 >> l) - 0.5
-        ts(LV(l, NON), LV(l, RANK), th, OP.is_ge)
-        ts(LV(l, PC), LV(l, RANK), th, OP.is_lt, C(P128 if l == 2 else P64), OP.mult)
-        ts(LV(l, PJ), LV(l, RANK), th, OP.is_lt, C([PP, PL1, P31][l]), OP.mult)
+        ts(LV(l, NON), LV(l, RANK), 0.0, OP.is_gt)
+        ts(LV(l, PC), LV(l, RANK), 0.0, OP.is_lt, C(P64), OP.mult)
+        ts(LV(l, PJ), LV(l, RANK), 0.0, OP.is_lt, C(PP), OP.mult)
 
     def kin_pos(l):
         ts(A("th", 0, 256, 4), A("k64", 64 * l, 64 * l + 64), LV(l, PM), OP.is_equal, 64.0, OP.mult)
 
-    def kin_par(l):
-        ts(A("th", 256, 768, 4), A("row"), LV(l, V_), OP.is_equal)
+    def kin_vp(l):
+        act(LV(l, VP), LV(l, V_), LV(l, NON), LV(l, PJ))
 
-    RM = [(M8, M8B, 8, "qwc"), (MC0, MC0B, 4, "qk0"), (MC1, MC1B, 4, "qk1")]
-    HB = [7, 7, 6]
+    def kin_par(l, k):
+        ts(A("th", 256, 768, 4), A("row"), LV(l, k), OP.is_equal)
+
+    NOR = [8, 4, 4]
 
     def kin_a(l):
-        n, e = RM[l][2], 4 * (TL + 8)
-        return [lambda: ts(LV(l, UU), LV(l, PM), 1.0 / (SA * SB), OP.mult, C(NK[l]), OP.add),
+        n, e = NOR[l], 4 * (TL + 8)
+        return [lambda: ts(LV(l, UU), LV(l, PM), 1.0 / (SA * SB), OP.mult, LV(l, NK) if l else 191.0, OP.subtract),
                 lambda: ts(LV(l, AA), LV(l, UU), LV(l, NON), OP.mult, LV(l, PC), OP.add),
                 lambda: ts(LV(l, HA), LV(l, AA), M32, OP.add, M32, OP.subtract),
                 lambda: (ts(A("tz", e, e + 4 * n, 4), A("ones", 0, n), LV(l, HA), OP.mult),
-                         ts(A("tz", e + 1, e + 4 * n, 4), S(RM[l][0], n), LV(l, AA), OP.mult, LV(l, HA), OP.subtract))]
+                         ts(A("tz", e + 1, e + 4 * n, 4), S(M8, n), LV(l, AA), OP.mult, LV(l, HA), OP.subtract))]
 
-    def kin_h(l):
-        quant("qh", 0, "th", 0, 192)
-        mm(HB[l], "qh", 64, "qh", 0)
+    HBK = [7, 7, 6]
+    LBK = [7, 7, 6]
+
+    def kin_h(l, n=192):
+        quant("qh", 0, "th", 0, n)
+        mm(HBK[l], "qh", 64, "qh", 0)
 
     def kin_first(l):
-        scan(A("so", 0, 64), P(HB[l], 0, 64), A("ones"), -64.0, OP.max, OP.add)
-        scan(A("so", 64, 128), P(HB[l], 0, 64), A("st16"), -64.0, OP.max, OP.add)
+        scan(A("so", 0, 64), P(HBK[l], 0, 64), A("ones"), -64.0, OP.max, OP.add)
+        scan(A("so", 64, 128), P(HBK[l], 0, 64), A("st16"), -64.0, OP.max, OP.add)
 
     def kin_has(l):
-        n, e = RM[l][2], 4 * (TL + 8) + 2
-        ts(A("tz", e, e + 4 * n - 2, 4), S(RM[l][1], n), A("so", 63), OP.mult, 128.0, OP.min)
+        n, e = NOR[l], 4 * (TL + 8) + 2
+        ts(A("tz", e, e + 4 * n - 2, 4), S(M8B, n), A("so", 63), OP.mult, 128.0, OP.min)
 
     def kin_tile(l):
         ts(A("tz", 4 * TL, 4 * TL + 32, 4), A("ones", 0, 8), A("so", 127), OP.mult)
@@ -332,93 +353,165 @@ def rank_program(g, core, T, topo):
             kin_has(l)
 
     def kin_list(l):
-        quant("ql", 0, "tz", 4 * TL, 136)
-        mm(6, "qwc", 0, "ql", 0)
-        if l < 2:
-            mm(7, RM[l][3], 0, "ql", 8)
+        quant("ql", 0, "tz", 4 * TL, 128)
+        mm(LBK[l], "qwc", 0, "ql", 0)
 
     def kin_c(l):
-        ts(A("oc%d" % l), P(6, 0, 8), -1.0, OP.mult, 64.0, OP.add)
+        ts(A("oc%d" % l), P(LBK[l], 0, 8), -1.0, OP.mult, 64.0, OP.add)
 
-    def kin_r(l):
-        n = RM[l][2]
-        cp(A("or%d" % l, 0, n), P(7, 0, n))
+    def kin_r(l, c):
+        cp(A("or%d" % l, 0, NOR[l]), P(7, c, c + NOR[l]))
+
+    def place_of(l):
+        ts(LV(l, PLV), LV(l, PLR), 1.0 / (SA * SB), OP.mult, LV(l, NK2), OP.add)
+
+    def place_tile(l):
+        ts(A("th", 768, 1280, 4), A("row"), LV(l, PLV), OP.is_equal)
+
+    def place_row(l):
+        mm(5, "qo", 0, "qs%d" % l, 0)
+        act(A("plr", 0, 128), P(5, 0, 128), 1.0 / SA, -511.0 - (128 >> l))
+
+    def place_mm(bank):
+        mm(bank, "qh", 192, "qh", 64)
+
+    def place_pick(bank):
+        tt(A("plr", 128, 256), P(bank, 0, 128), A("plr", 0, 128), OP.mult)
+
+    def place_out(l):
+        act(A("jk", 144, 272), A("plr", 128, 256), acc=LV(l, PAO))
+        parents_out(l)
 
     def parents_out(l):
-        v = LV(l, V_)
-        if l == 1:
-            ts(LV(l, T1), v, 63.5, OP.is_ge, -32.0, OP.mult)
-            act(LV(l, T2), LV(l, T1), 1.0, v)
-            v = LV(l, T2)
-        act(LV(l, PAO), v, LV(l, NON), LV(l, PJ))
-        k = 32 + 16 * l + PAO
-        for p0, p1, at in [[(0, 128, 0)], [(0, 32, 128), (64, 96, 160)], [(0, 32, 192)]][l]:
-            src = C(k, p0, p1)
-            stores.append(lambda src=src, at=at, n=p1 - p0: dma("s", T.pa[0, at:at + n], src[0], [src], []))
+        n, at = 128 >> l, [0, 128, 192][l]
+        src = LV(l, PAO if l else VP, 0, n)
+        stores.append(lambda: dma("s", T.pa[0, at:at + n], src[0], [src], []))
 
-    def up(l):
-        n, bn, bo = 128 >> l, "buf%d" % l, BO[l]
+    def store():
+        while stores:
+            stores.pop(0)()
+
+    def up(l, F):
+        bn, bo = "buf%d" % l, BASE[l] + 64
+
+        def L(k, p0=0, p1=128):
+            return LV(l, k, p0, p1)
+
+        def fill(k):
+            if k in F:
+                F[k]()
+
+        def unpack():
+            for b in range(4):
+                mm(b, "qe", 128 * b, bn, bo)
         mm(4, bn, bo, bn, bo)
-        fill(1)
-        tt(A("mx", 0, 128), P(4, 0, 128), A("idn", 0, 128), OP.mult)
-        if l == 0:
-            quant("qe", 256, "the", 1, 128)
-        act(A("gs"), P(4, 0, 128), 2.0 ** -18)
-        scan(A("xs"), A("mx"), A("mx"), TINY, OP.max, OP.max)
-        if l == 0:
-            quant("qe", 384, "the", 0, 128)
-        for b in range(4):
-            mm(b, "qe", 128 * b, bn, bo)
-        act(A("thr", 0, n), A("fm", 0, n), A("xs", 159))
-        tr(A("zz", 0, 32), A("xs", 128, 160))
+        if l:
+            mm(5, "ur", 256 * l - 256, bn, bo, 128, True, False)
+            mm(5, bn, bo, "ur", 256 * l - 128, 128, False, True)
+        fill(0)
+        tt(A("mx", 0, 128), P(4, 0, 128), A("idn"), OP.mult)
+        if l:
+            tt(A("tz", 4 * TF + 1, 4 * TF + 512, 4), P(5, 0, 128), A("ls"), OP.is_gt)
+            act(A("jk", 0, 129), A("mx", 0, 129), acc=L(D_))
+            fill(1)
+            red(L(R_), A("tz", 4 * TF + 1, 4 * TF + 514, 4))
+            quant("qb", 0, "tz", 4 * TF, 128)
+            mm(6, "qs0", 0, "qb", 0)
+            unpack()
+            act(L(T1), L(D_), BELOW)
+            act(A("gs"), P(4, 0, 128), 2.0 ** -18)
+            ts(L(SG), L(R_), -0.5, OP.max, 0.5, OP.min)
+            ts(L(SH), L(R_), C(HB), OP.mult)
+            ts(L(NR), L(R_), -1024.0, OP.mult)
+            ts(L(PHI), L(R_), 0.0, OP.is_gt, BELOW, OP.max)
+            act(L(KAP), L(SG), C(HS), 1.5 * SA)
+            act(L(NK), L(SG), 32.0, 143.0 if l == 1 else C(NA))
+        else:
+            fill(1)
+            red(L(D_), A("mx", 0, 129), OP.max)
+            act(A("gs"), P(4, 0, 128), 2.0 ** -18)
+            act(L(T1), L(D_), BELOW)
+            fill(2)
+        ts(A("xs", 64, 128), A("psi", 64, 128), L(D_), OP.mult, L(SG), OP.mult)
         if l < 2:
-            tr(A("zz", 32, 64, 1, 64, 128), A("xs", 128, 160, 1, 0, 64))
-            tr(A("zz", 32, 64, 1, 0, 64), A("xs", 128, 160, 1, 64, 128))
+            for k in range(4):
+                a, b = 32 * k, 32 * (k ^ 1)
+                ts(A("xs", 0, 64, 1, b, b + 32), A("psi", 0, 64, 1, a, a + 32), L(D_, a, a + 32), OP.mult, L(SG, a, a + 32), OP.mult)
+        if l:
+            ts(L(TAU), L(SG), 0.0, OP.min, 2.0 ** -109, OP.mult)
+            act(A("same"), P(6, 0, 128), L(NR), None, AF.Relu)
+            halves(lambda p0, p1, c: act(A("am", c, c + 64, 1, p0, p1), A("ones" if l == 1 else "pc", 0, 64, 1, p0, p1), L(KAP, p0, p1)))
+            act(A("gt", 0, 64), A("gs", 0, 64), L(PHI), L(TAU))
+            act(A("gt", 64, 128), A("gs", 64, 128), L(PHI))
+        ts(L(T2), L(SH) if l else C(HB), L(T1), OP.max, L(D_), OP.min)
+        fill(3)
+        w = 64 if l < 2 else 32
+        tr(A("zz", 0, 32), A("xs", 96, 128))
+        if l < 2:
+            tr(A("zz", 32, 64), A("xs", 0, 32))
+        halves(lambda p0, p1, c: tr(A("zz", w, 2 * w, 1, c, c + 64), A("xs", 96 - w, 96, 1, p0, p1)))
         if l == 0:
-            act(A("zz", 64, 128, 1, 96, 128), A("zz", 0, 64, 1, 64, 96))
-            cp(A("zz", 64, 128, 1, 32, 64), A("zz", 0, 64, 1, 0, 32))
-            cp(A("zz", 64, 128, 1, 0, 32), A("zz", 0, 64, 1, 32, 64))
-            act(A("zz", 64, 128, 1, 64, 96), A("zz", 0, 64, 1, 96, 128))
+            unpack()
         for b in range(4):
             act(A("dm", b, 512, 4), P(b, 0, 128), -1.0)
-        tt(A("bm", 0, n), A("zz", 0, n), A("thr", 0, n), OP.is_gt)
-        if l < 2:
-            fill(1)
-        red(LV(l, RANK), A("bm", 0, n))
-        if l < 2:
-            fill(1)
-        ts(A("ta", 0, 517, 4), A("kk", 130 * l, 130 * l + 130), LV(l, RANK), OP.is_gt, SB, OP.mult)
+        fill(4)
+        ts(A("bm", 128 - 2 * w, 128 - w), A("zz", 0, w), L(SG), OP.mult, L(T1), OP.is_gt)
+        ts(A("bm", 128 - w, 128), A("zz", w, 2 * w), L(SG), OP.mult, L(T2), OP.is_gt)
+        if l:
+            tt(A("ts", 0, 512, 4), A("same"), A("am"), OP.min)
+        else:
+            quant("qs0", 0, "ts", 0, 128)
+        red(L(RANK), A("bm", 128 - 2 * w, 129))
+        if l:
+            quant("qs%d" % l, 0, "ts", 0, 128)
+        fill(5)
+        ts(A("ta", 512), L(RANK), 0.0, OP.is_gt, SB, OP.mult)
+        ts(A("ta", 0, 512, 4), A("kk"), L(RANK), OP.is_gt, SB, OP.mult)
+        if l:
+            tt(A("gs", 0, 64), A("gs", 0, 64), A("gt", 0, 64), OP.min)
+        fill(6)
         quant("qa", 0, "ta", 0, 130)
         mm(5, "qs%d" % l, 0, "qa", 0, 130)
+        if l:
+            tt(A("gs", 64, 128), A("gs", 64, 128), A("gt", 64, 128), OP.max)
+            ts(A("k64", 64 * l, 64 * l + 64), A("row", 0, 64), L(NK), OP.add, SA * SB, OP.mult)
+            act(L(NK2), L(SG), -64.0, -159.0 if l == 1 else C(NB))
         if l == 2:
             kin_piv(l)
-        fill(1)
+        fill(7)
         kk, pm = A("k64", 64 * l, 64 * l + 64), P(5, 128)
         tt(A("mk"), A("gs"), P(5, 0, 128), OP.min)
         ts(A("tz", 4 * TN, 4 * TN + 64), kk, pm, OP.is_equal, C(PH), OP.mult)
         ts(A("tz", 4 * TN + 64, 4 * TN + 128), kk, pm, OP.is_equal, C(IL), OP.mult)
         scan(A("rm"), A("mk"), A("mk"), -BIG, OP.max, OP.max)
-        act(A("jk", 0, 128), A("rm"), -1.0, A("rm", 127), AF.Sign, LV(l, V_))
-        act(A("jk", 128, 136), A("rm", 15, 128, 16), -1.0, A("rm", 127), AF.Sign, LV(l, H_))
-        act(A("tz", 4 * TP, 4 * TP + 64), A("ones"), LV(l, H_))
+        act(A("jk", 0, 128), A("rm"), -1.0, A("rm", 127), AF.Sign, L(V_))
+        act(A("jk", 128, 136), A("rm", 15, 128, 16), -1.0, A("rm", 127), AF.Sign, L(H_))
+        act(A("tz", 4 * TP, 4 * TP + 64), A("ones"), L(H_))
         quant("qn", 0, "tz", 4 * TN, 144)
         mm(6, "qw64", 0, "qn", 0, 128, True, False)
         mm(6, "qw64", 0, "qn", 16, 128, False, True)
         ts(A("eq"), kk, pm, OP.is_equal, 1.0 / 16, OP.mult)
-        cp(LV(l, PM), pm)
+        cp(A("cf", 16 + 28 * l + PM, 16 + 28 * l + PM + 2), P(5, 128, 130))
         if l == 2:
             kin_pos(l)
             kin_a(l)[0]()
-            kin_par(l)
-        ts(A("tz", 4 * TP + 64, 4 * TP + 128), A("eq"), LV(l, V_), OP.mult, LV(l, H_), OP.subtract)
+            kin_par(l, V_)
+        else:
+            fill(8)
+        ts(A("tz", 4 * TP + 64, 4 * TP + 128), A("eq"), L(V_), OP.mult, L(H_), OP.subtract)
         ts(A("on"), P(6, 0, 16), C(P3), OP.add)
         run("a", [A("dm"), A("on")], [A("dn")],
             lambda: g.scalar.activation(T.dn[:], T.dm[:].indirect(T.on[:]), AF.Copy, scale=-2.0))
         if l == 2:
             kin_h(l)
+        else:
+            kin_piv(l)
         quant("qp", 0, "tz", 4 * TP, 144)
         mm(7, "qw64", 0, "qp", 0, 128, True, False)
         mm(7, "qw64", 0, "qp", 16, 128, False, True)
+        kin_vp(l)
+        if l:
+            place_row(l)
         if l == 2:
             kin_a(l)[1]()
             kin_first(l)
@@ -427,163 +520,111 @@ def rank_program(g, core, T, topo):
                 mm(b, "qe", 128 * b, bn, bo, 128, True, False)
             kin_tile(l)
         else:
-            fill(1)
+            kin_a(l)[0]()
+            kin_pos(l)
+            fill(9)
         ts(A("op"), P(7, 0, 16), C(P3), OP.add)
         if l == 2:
             kin_list(l)
-        run("v", [A("dm"), A("op"), A("dn")], [A("te", 0, 256)],
-            lambda: g.vector.tensor_tensor(T.te[:, 0:256], T.dm[:].indirect(T["op"][:]), T.dn[:], OP.add))
+        else:
+            kin_a(l)[1]()
+            if l:
+                place_of(l)
+            fill(10)
+        run("v", [A("dm"), A("op"), A("dn")], [A("te", 256, 512)],
+            lambda: g.vector.tensor_tensor(T.te[:, 256:512], T.dm[:].indirect(T["op"][:]), T.dn[:], OP.add))
         if l == 2:
             kin_c(l)
-        if l == 0:
-            fill(1)
-        quant("buf2" if l == 2 else "pool%d" % l, 0, "te", 0, 128)
+        else:
+            kin_par(l, VP)
+            kin_a(l)[2]()
+        quant("buf%d" % min(l + 1, 2), [0, 64, 0][l], "te", 0, 128)
 
     def exchange(l):
-        pool, peer = "pool%d" % l, rank ^ PART[l]
-        remote(peer, 3 * l, A(pool, 0, 64), A(pool, 128, 192), True)
-        remote(peer, 3 * l + 1, A(pool + "s", 0, 64), A(pool + "s", 128, 192), False)
-        mm(4, "ur", 96 * l, pool, 0)
-        mm(5, pool, 0, "ur", 96 * l)
-        kin_pos(l)
-        kin_par(l)
-        if l == 0:
-            ts(A("mk", 0, 64, 1, 0, 64), P(4, 0, 64, 0, 64), P(5, 0, 1, 0, 64), OP.subtract)
+        nb, at, peer = "buf%d" % (l + 1), BASE[l + 1] + 64, rank ^ PART[l]
+        remote(peer, 2 * l, A(nb, at, at + 64), A(nb, at + 64, at + 128), True)
+        remote(peer, 2 * l + 1, A(nb + "s", at, at + 64), A(nb + "s", at + 64, at + 128), False)
+        if l:
+            place_tile(l)
+            kin_a(l)[3]()
+            kin_h(l, 320)
+            place_mm(3)
+            quarters("am", 0.0, range(4))
+            kin_first(l)
+            place_pick(3)
+            place_out(l)
         else:
-            ts(A("mk", 0, 64, 1, 0, 32), P(4, 0, 64, 0, 32), P(5, 0, 1, 0, 32), OP.subtract)
-            ts(A("mk", 0, 64, 1, 32, 64), P(4, 0, 64, 32, 64), P(5, 32, 33, 32, 64), OP.subtract)
-        kin_h(l)
-        tt(A("tz", 4 * TF + 1, 4 * TF + 256, 4, 0, 64), A("mk", 0, 64, 1, 0, 64), A("ls", 64 * l, 64 * l + 64, 1, 0, 64), OP.is_lt)
-        fill(1)
-        quant("qf", 0, "tz", 4 * TF, 128)
-        mm(6, "qs0", 0, "qf", 0)
-        kin_first(l)
-        fill(1)
-        ts(A("d0"), P(6, 0, 64), ((32 >> l) - 0.5) * SA, OP.is_lt, -1.0, OP.mult)
+            iota(A("th", 768, 1280), [[0, 512]])
+            parents_out(l)
+            kin_h(l)
+            u_pick(0)
+            u_pick(1)
+            ts(A("st16"), A("r16", 0, 64), 15.0, OP.is_equal, 16.0, OP.mult)
+            kin_a(l)[3]()
+            kin_first(l)
+            rows16(0, 3)
+            quant("qwc", 0, "tg", 0, 128)
         kin_tile(l)
-        scan(A("cs", 0, 64), A("d0"), A("ones"), 0.0, OP.add, OP.add)
-        scan(A("cs", 64, 128), A("d0"), A("ones"), 0.0, OP.add, OP.min)
-        for go, c in ((0, 0), (0, 1), (1, 0), (1, 1)):
-            at = 2 * go + c if l == 0 else 2 * c + 1 - go
-            act(A("jk", 64 * at, 64 * at + 64), A("cs", 64 * go, 64 * go + 64), 2.0 * go - 1.0, C(KB + c), AF.Sign, C(ACC + at))
-        ka = kin_a(l)
-        ka[0]()
-        fill(1)
-        ka[1]()
-        acc = A("cf", ACC, ACC + 4)
-        ts(A("lst%d" % l), acc, 0.5, OP.mult, 32.0, OP.add)
-        remote(peer, 3 * l + 2, A("lst%d" % l), A("lin%d" % l), False)
-        nb, bo = "buf%d" % (l + 1), BO[l + 1]
-        if l == 1:
-            ts(A("o2", 0, 8, 2), acc, 0.5, OP.mult, 32.0, OP.add)
-        tt(S(KT, 4), acc, S(MK0 + 4 * l, 4), OP.mult)
-        ka[2]()
-        if l == 0:
-            pick(nb, bo, pool, 0, 64, A("lst0", 0, 2))
-            pick(nb, bo + 96, pool, 0, 64, A("lst0", 2, 4))
-        else:
-            for c, at in ((1, 0), (0, 48), (3, 64), (2, 112)):
-                pick(nb, bo + at, pool, 0, 64, A("o2", 2 * c))
-        red(C(KO), S(KT, 4))
-        ka[3]()
 
-    def origin_a(l):
-        return [lambda: ts(C(KT1), C(KO), 0.5, OP.mult, 24.5, OP.add),
-                lambda: ts(C(KHI), C(KT1), M16, OP.add, M16, OP.subtract),
-                lambda: ts(C(KLO), C(KT1), 7.5, OP.add, C(KHI), OP.subtract)]
-
-    def origin_v(l):
-        mc, mcb = [(MC0, MC0B), (MC1, MC1B)][l]
-        ts(S(mc, 4), S(R16X, 4), C(KHI), OP.is_equal, C(OWN0 + l), OP.mult)
-        act(S(mcb, 4), S(mc, 4), 128.0)
-        rows("r16", C(KLO), 3)
-
-    def arrive(l):
-        nb, bo, pool = "buf%d" % (l + 1), BO[l + 1], "pool%d" % l
-        if l == 0:
-            pick(nb, bo + 32, pool, 128, 192, A("lin0"))
-        else:
-            pick(nb, bo + 16, pool, 128, 192, A("lin1", 0, 2))
-            pick(nb, bo + 80, pool, 128, 192, A("lin1", 2, 4))
-
-    def down(l):
-        bn, bo, ch = "buf%d" % l, BO[l], "ch%d" % l
-        pick(ch, 0, bn, 0, bo + (0 if l == 2 else 128), A("oc%d" % l))
+    def down(l, F):
+        bn, b0, ch = "buf%d" % l, BASE[l], "ch%d" % l
+        pick(ch, 0, bn, b0, b0 + 192, A("oc%d" % l))
         for b in range(4):
             mm(b, "qe", 128 * b, ch, 0, 128, False, True)
-        if l == 2:
-            kin_a(l)[3]()
-            kin_has(l)
-            quant("qr", 0, "tz", 4 * (TL + 8), 128)
-            mm(7, RM[l][3], 0, "qr", 0)
-        else:
-            fill(1)
+        F[0]()
         for b in range(4):
             if b % 2:
                 cp(A("td", b, 512, 4), P(b, 0, 128))
             else:
                 act(A("td", b, 512, 4), P(b, 0, 128))
-        if l == 2:
-            kin_r(l)
-        quant(bn, bo + 128, "td", 0, 128)
+        F[1]()
+        quant(bn, b0 + 192, "td", 0, 128)
         if l:
             for b in range(4):
-                mm(b, "qe", 128 * b, "buf%d" % (l - 1), BO[l - 1], 128, True, False)
-            pick("buf%d" % (l - 1), 0, bn, 0, bo + 256, A("or%d" % l, 0, 4))
+                mm(b, "qe", 128 * b, "buf%d" % (l - 1), BASE[l - 1] + 64, 128, True, False)
+            F[2]()
+            pick("buf%d" % (l - 1), BASE[l - 1], bn, b0, b0 + 320, A("or%d" % l, 0, 4))
+            F[3]()
         else:
-            pick("ff", 0, bn, 0, bo + 256, A("or0"))
+            pick("ff", 0, bn, 0, 320, A("or0"))
 
-    later += [lambda: (quant("uq", 0, "ut", 0, 128), send_u()),
-              lambda: (columns1(), act(A("th", 256, 768), A("ts"), 0.0, 1.0)),
-              lambda: (k64(0), ts(A("cf", KB, KB + 2), S(R16X, 2), C(P15), OP.add, 0.5, OP.add),
-                       cp(A("cf", PA32, PA32 + 3), A("ci", PA32, PA32 + 3))),
-              lambda: (quant("qw64", 0, "tg", 0, 128), ms(A("o0", 0, 4), 0),
-                       ts(A("st16"), A("r16", 0, 64), 15.0, OP.is_equal, 16.0, OP.mult)),
-              lambda: (pick("ur", 0, "uq", 0, 32, A("o0", 0, 8)),
-                       act(A("ls", 0, 64), A("am", 0, 64), -TINY, 2 * TINY, AF.Relu)),
-              lambda: (ms(A("th", 1, 256, 4, 0, 1), -64.0), ts(C(PL1), C(P31), C(PA32), OP.add),
-                       ts(S(Q4S + 4, 2), A("sm", R16X, R16X + 4, 2), C(PB32), OP.is_equal, SA, OP.mult))]
-    up(0)
-    later += [lambda: (masks(), s_tile(1)),
-              lambda: kin_piv(0),
-              lambda: rows("r16", C(P15), 3)]
+    def nothing():
+        pass
+
+    up(0, {0: lambda: (ts(A("kk"), A("row"), C(PP), OP.not_equal, -1000.0, OP.mult),
+                       ts(A("ut", 8, 16), A("ut", 0, 8), -1.0, OP.mult), unpackers(0, 2)),
+           1: lambda: unpackers(2, 3),
+           2: lambda: u_send(),
+           3: lambda: (unpackers(3, 4), act(A("th", 256, 768), A("ts"), 0.0, 1.0)),
+           4: lambda: rows4(0, 3),
+           5: lambda: (rows4(3, 4), ts(A("k64", 0, 64), A("row", 0, 64), 191.0, OP.add, SA * SB, OP.mult),
+                       u_list((0, 4, 0))),
+           6: lambda: quant("qw64", 0, "tg", 0, 128),
+           7: lambda: (quant("qo", 0, "th", 256, 128), ms(A("ls"), BIG), u_list((4, 8, 130), (8, 12, 2), (12, 16, 128))),
+           8: lambda: (score_order(), counts(1)),
+           9: lambda: (act(A("am"), A("am"), SA), act(C(HS), C(HB), SA / BIG), ms(A("th", 1, 256, 4, 0, 1), -64.0),
+                       ms(A("tz", 4 * TF + 3, 4 * TF + 512, 4, 0, 1), 0.5), ts(S(M8), A("row", 0, 8), C(PH), OP.is_equal)),
+           10: lambda: ts(S(M8B), A("row", 0, 8), C(PH), OP.is_equal, 128.0, OP.mult)})
     exchange(0)
-    weave(origin_a(0), [lambda: quant("qwc", 0, "tg", 0, 128),
-                        lambda: (ts(C(NK[1]), C(PL1), C(PB32), OP.add, -64.0, OP.add), quant("qs1", 0, "ts", 0, 128))])
-    kin_list(0)
-    k64(1)
-    act(A("kk", 130, 260), A("idn"), 32.5, -1.0)
-    parents_out(0)
-    red(C(OWN0), S(MK0, 4))
-    red(C(OWN0 + 1), S(MK0 + 4, 4))
-    cp(A("ls", 64, 128), A("ls", 0, 64))
-    arrive(0)
-    later += [lambda: (kin_c(0), kin_r(0)),
-              lambda: (ms(A("ls", 96, 128, 1, 0, 32), -BIG), ms(A("ls", 64, 96, 1, 32, 64), -BIG)),
-              lambda: ts(S(Q4S, 4), S(R16X, 4), C(PA48), OP.is_equal, SA, OP.mult),
-              lambda: pick("ur", 128, "ub", 0, 32, A("o0", 4, 10)),
-              lambda: (origin_v(0), act(A("ts2"), A("ts"), 0.0, SA), s_tile(2))]
-    up(1)
-    later += [lambda: quant("qk0", 0, "tg", 0, 128),
-              lambda: kin_piv(1),
-              lambda: quant("wq", 0, "wt", 0, 128)]
+    up(1, {1: lambda: kin_list(0),
+           4: lambda: (kin_c(0), kin_r(0, 8), u_list((16, 18, 1))),
+           7: lambda: (u_list((18, 20, 129), (20, 22, 135), (22, 24, 139), (24, 26, 3)),
+                       act(C(NA), C(PQ), -16.0, 127.0), act(C(NB), C(PQ), 32.0, -127.0)),
+           8: lambda: (u_list((26, 28, 131), (28, 30, 133), (30, 32, 137)), quarters("ls", BIG, (0, 1))),
+           9: lambda: (u_pick(2), quarters("ls", BIG, (2, 3)), counts(2)),
+           10: lambda: ts(A("pc"), A("row", 0, 64), 32.0, OP.is_ge, C(PQ), OP.is_equal)})
+    u_pick(3)
     exchange(1)
-    act(A("kk", 260, 390), A("idn"), 16.5, -1.0)
-    weave(origin_a(1), [lambda: quant("qs2", 0, "ts2", 0, 128),
-                        lambda: (ts(C(NK[2]), C(P31), C(PA48), OP.add, -32.0, OP.add), kin_list(1))])
-    k64(2)
-    parents_out(1)
-    origin_v(1)
-    arrive(1)
-    later += [lambda: (kin_c(1), kin_r(1)), lambda: quant("qk1", 0, "tg", 0, 128)]
-    up(2)
-    later += [lambda: quant("wq", 128, "wt", 512, 128), lambda: quant("wq", 256, "wt", 1024, 128)]
-    down(2)
-    parents_out(2)
-    for f in stores:
-        f()
-    down(1)
-    down(0)
+    up(2, {1: lambda: kin_list(1),
+           3: lambda: (kin_c(1), kin_r(1, 8)),
+           4: lambda: quant("wq", 0, "wt", 0, 128),
+           7: lambda: quant("wq", 128, "wt", 512, 128)})
+    down(2, [lambda: (kin_a(2)[3](), kin_has(2), place_of(2), quant("qr", 0, "tz", 4 * (TL + 8), 128), mm(7, "qwc", 0, "qr", 0)),
+             lambda: kin_r(2, 0), lambda: kin_par(2, VP), lambda: place_tile(2)])
+    store()
+    down(1, [lambda: (quant("qh", 64, "th", 256, 256), place_mm(4)), nothing,
+             lambda: quant("wq", 256, "wt", 1024, 128), nothing])
+    down(0, [lambda: place_pick(4), lambda: (place_out(2), store())])
     for o in range(3):
         mm(4 + o, "wq", 128 * o, "ff", 0)
     dma("s", T.oc[:], T.ff[:].bitcast(dt.uint8), [A("ff")], [])

@@ -6,23 +6,27 @@ AF = ActivationFunctionType
 MX, U8, F32, BF, U16, I32 = "float8_e4m3fn_x4", "uint8", "float32", "bfloat16", "uint16", "int32"
 
 CODES = {"qa": 130, "qn": 144, "qp": 144, "ql": 128, "qr": 128, "qb": 128, "qh": 320, "qs0": 128, "qs1": 128, "qs2": 128,
-         "qe": 512, "qw64": 128, "qwc": 128, "qo": 128, "uq": 160, "ur": 512, "wq": 384,
-         "buf0": 320, "buf1": 320, "buf2": 384, "ch0": 128, "ch1": 128, "ch2": 128, "ff": 128}
+         "qe": 512, "qw64": 128, "qwc": 128, "qo": 128, "uq": 288, "ur": 512, "wq": 384,
+         "buf0": 448, "buf1": 448, "buf2": 384, "ch0": 128, "ch1": 128, "ch2": 128, "ff": 128, "pz": 128, "fo": 128,
+         "qc": 128}
 SCRATCH = {}
 for _n, _c in CODES.items():
     SCRATCH[_n] = ("sbuf", [128, _c], MX)
     SCRATCH[_n + "s"] = ("sbuf", [128, _c], U8)
-for _n, _c, _d in [("xt", 512, BF), ("ut", 512, BF), ("wt", 1536, BF), ("ta", 520, BF), ("ts", 512, BF),
-                   ("the", 516, BF), ("tz", 840, BF), ("te", 512, BF), ("th", 1280, BF), ("tg", 512, BF),
+for _n, _c, _d in [("xt", 768, BF), ("tf", 520, BF), ("cl", 264, F32), ("sr", 264, F32),
+                   ("ut", 512, BF), ("wt", 1536, BF), ("ta", 520, BF), ("ts", 512, BF),
+                   ("the", 648, BF), ("te", 512, BF), ("th", 1280, BF), ("tg", 512, BF),
                    ("td", 512, BF), ("r16", 128, BF), ("ra", 128, BF),
                    ("row", 128, F32), ("idn", 128, F32), ("am", 128, F32), ("sf", 128, F32), ("kk", 128, F32),
                    ("psi", 128, F32), ("k64", 192, F32), ("ls", 128, F32), ("ones", 64, F32), ("pc", 64, F32),
                    ("mx", 136, F32), ("xs", 128, F32), ("zz", 128, F32), ("bm", 136, F32), ("same", 128, F32),
-                   ("gs", 128, F32), ("gt", 128, F32), ("mk", 128, F32), ("rm", 128, F32), ("jk", 272, F32),
-                   ("eq", 64, F32), ("dm", 512, F32), ("dn", 256, F32), ("so", 128, F32), ("plr", 256, F32),
-                   ("st16", 64, F32), ("sm", 16, F32), ("cf", 128, F32), ("ci", 16, I32), ("ysb", 384, F32),
+                   ("gs", 128, F32), ("gt", 128, F32), ("mk", 128, F32), ("rm", 128, F32), ("jk", 400, F32),
+                   ("eq", 64, F32), ("rw", 72, F32), ("m16", 128, F32), ("r0", 128, F32), ("gc", 128, F32),
+                   ("gd", 128, F32), ("dm", 512, F32), ("dn", 256, F32), ("so", 128, F32), ("plr", 256, F32),
+                   ("st16", 64, F32), ("sm", 16, F32), ("cf", 128, F32), ("ci", 16, I32), ("oi", 32, I32),
+                   ("ysb", 384, F32),
                    ("on", 16, U16), ("op", 16, U16), ("oc0", 8, U16), ("oc1", 8, U16), ("oc2", 8, U16),
-                   ("or0", 8, U16), ("or1", 8, U16), ("or2", 8, U16), ("ou", 32, U16)]:
+                   ("or0", 24, U16), ("or1", 8, U16), ("or2", 8, U16), ("ou", 32, U16), ("od", 8, U16)]:
     SCRATCH[_n] = ("sbuf", [128, _c], _d)
 for _k in range(8):
     SCRATCH["ps%d" % _k] = ("psum", [128, 512], F32)
@@ -32,13 +36,35 @@ SEMAPHORES = ["sv", "sa", "sp", "sg", "sent", "ru"] + ["d%d" % k for k in range(
 
 PART = [4, 2]
 BASE = [0, 0, 64]
-USLOT = {4: 128, 2: 132, 6: 136}
+ZERO = 320
+USLOT = {4: 128, 2: 132, 6: 260}
 TINY = 2.0 ** -100
 BIG = 1e29
 BELOW = 1.0 - 2.0 ** -24
 M32 = 1.5 * 2.0 ** 28
 SA, SB = 2.0 ** 22, 2.0 ** 29
-TP, TN, TL, TF = 0, 32, 64, 80
+SC = 2.0 ** -18
+CFG = {"so2": "v", "pm0": "v", "pm1": "v", "pm2": "v", "ut": "v", "y1": "v"}
+OPS = []
+
+ORDER = [int(_k) for _k in """
+6 8 9 5 3 21 22 19 7 4 18 27 20 14 24 23 13 37 0 26 25 15 11 29 35 49 12 54 42 85 1 39 48 31 34 38 50 36 30 10 70 41 46 17 16
+43 40 57 60 61 74 45 58 59 76 52 67 64 66 44 65 28 81 69 80 62 143 83 33 82 86 87 142 79 84 32 68 89 2 71 78 77 72 151 116 47
+90 63 88 93 56 95 96 92 94 119 53 109 103 100 75 101 102 98 130 128 97 110 156 99 113 114 115 111 104 118 51 73 91 122 117 131
+159 112 158 120 134 135 137 157 160 124 126 138 139 144 55 133 129 127 106 121 145 146 150 132 108 105 147 154 148 173 149 123
+174 136 165 164 167 166 155 125 153 152 162 176 169 172 175 171 168 178 161 107 181 163 179 170 177 190 192 191 193 194 195
+188 185 214 208 206 187 183 209 207 189 220 180 198 197 196 219 199 204 205 222 186 221 225 224 223 201 227 200 229 226 278
+265 228 202 257 245 184 230 247 212 213 182 141 248 250 246 249 255 252 266 258 251 211 259 256 253 210 262 254 286 260 261
+140 239 279 215 216 217 218 267 231 238 273 263 264 276 232 233 234 269 203 243 289 304 268 280 235 281 283 236 270 237 292
+442 284 285 293 294 271 315 272 277 287 282 274 295 297 291 305 303 288 275 316 317 296 307 449 306 301 300 314 240 308 326
+318 319 302 298 290 323 324 309 450 320 335 334 310 330 336 333 332 345 352 346 329 347 339 325 338 355 337 341 356 321 322
+358 357 340 360 361 327 359 363 331 342 343 395 362 365 328 353 366 350 364 367 349 369 368 378 401 370 344 397 371 374 377
+382 379 402 381 380 372 299 373 348 383 351 375 376 384 386 354 388 244 387 389 390 462 398 385 394 393 396 415 404 405 406
+407 399 408 403 411 409 410 400 412 413 425 424 417 414 416 418 423 419 422 420 441 465 426 421 242 427 428 429 430 436 431
+432 437 433 440 241 439 434 435 438 443 444 311 451 447 455 448 445 453 446 391 312 460 456 454 313 392 457 466 452 463 467
+464 458 459 473 461 468 477 481 472 471 470 479 480 469 482 483 475 478 484 476 474 489 488 485 490 493 495 496 497 487 486
+492 494 491 498
+""".split()]
 
 
 def rank_program(g, core, T, topo):
@@ -51,7 +77,10 @@ def rank_program(g, core, T, topo):
     count = {}
     snap = {}
     log = {}
+    when = {}
+    ytok = [None]
     ndma = [0]
+    ops = []
 
     def A(name, c0=None, c1=None, step=1, p0=0, p1=128):
         if c0 is None:
@@ -86,47 +115,63 @@ def rank_program(g, core, T, topo):
                         continue
                     if need.get(tok[0], 0) < tok[1]:
                         need[tok[0]] = tok[1]
-        for s in sorted(need, key=lambda k: k == SEM.get(q)):
-            wait(q, (s, need[s]))
+        keep, seen = [], dict(clock[q])
+        for tok in sorted(need.items(), key=lambda t: -when[t]):
+            if seen.get(tok[0], 0) < tok[1]:
+                keep.append(tok)
+                for k, m in snap.get(tok, {}).items():
+                    seen[k] = max(seen.get(k, 0), m)
+        for tok in keep[::-1]:
+            wait(q, tok)
 
     def note(q, reads, writes, tok):
         snap[tok] = dict(clock[q]) if q in clock else {}
+        when[tok] = len(when) + (0 if q in clock else 1000)
         for accs, wr in ((reads, False), (writes, True)):
             for a in accs:
                 log.setdefault(a[1], []).append((a[2], a[3], a[4], wr, q, tok))
 
-    def run(q, reads, writes, fn):
+    def run(q, reads, writes, fn, alone=False):
         reads = [a for a in reads if isinstance(a, tuple)]
-        order(q, reads, writes)
-        s = SEM[q]
-        count[s] = count.get(s, 0) + 1
-        fn().then_inc(T.sem[s], 1)
-        note(q, reads, writes, (s, count[s]))
+
+        def issue():
+            s = SEM[q]
+            if alone:
+                wait(q, (s, count[s]))
+            order(q, reads, writes)
+            count[s] = count.get(s, 0) + 1
+            fn().then_inc(T.sem[s], 1)
+            note(q, reads, writes, (s, count[s]))
+        ops.append((q, reads, writes, issue))
 
     def val(x):
         return x[0] if isinstance(x, tuple) else x
 
     def dma(q, out, in_, reads, writes):
-        order(q, reads, writes)
-        s = "d%d" % ndma[0]
-        ndma[0] += 1
-        Q[q].dma_start(out, in_).then_inc(T.sem[s], 16)
-        count[s] = 16
-        note("dma", reads, writes, (s, 16))
-        snap[(s, 16)] = dict(clock[q])
+        def issue():
+            order(q, reads, writes)
+            s = "d%d" % ndma[0]
+            ndma[0] += 1
+            Q[q].dma_start(out, in_).then_inc(T.sem[s], 16)
+            count[s] = 16
+            note("dma", reads, writes, (s, 16))
+            snap[(s, 16)] = dict(clock[q])
+            if q == "a":
+                ytok[0] = (s, 16)
+        ops.append((q, reads, writes, issue))
 
     def remote(peer_rank, k, src, dst, codes):
         peer = T.cores[peer_rank]
         rid, pid = topo.addr(peer, core)
-        m = topo.mask(core, peer)
-        n = len(topo.engines(core, peer))
-        order("g", [src], [])
-        a, b = (src[0].bitcast(dt.uint8), dst[0].bitcast(dt.uint8)) if codes else (src[0], dst[0])
-        g.remote_dma(b, a, T.sem["r%d" % k], T.sem.sent, pid, rid, m)
-        count["sent"] = count.get("sent", 0) + n
-        back = len(topo.engines(peer, core))
-        count["r%d" % k] = back
-        note("net", [], [dst], ("r%d" % k, back))
+
+        def issue():
+            order("g", [src], [])
+            a, b = (src[0].bitcast(dt.uint8), dst[0].bitcast(dt.uint8)) if codes else (src[0], dst[0])
+            g.remote_dma(b, a, T.sem["r%d" % k], T.sem.sent, pid, rid, topo.mask(core, peer))
+            count["sent"] = count.get("sent", 0) + len(topo.engines(core, peer))
+            count["r%d" % k] = len(topo.engines(peer, core))
+            note("net", [], [dst], ("r%d" % k, count["r%d" % k]))
+        ops.append(("g", [src], [dst], issue))
 
     def send_u():
         peers = [T.cores[rank ^ k] for k in USLOT]
@@ -135,17 +180,21 @@ def rank_program(g, core, T, topo):
             m &= topo.mask(core, c) & topo.mask(c, core)
         n = bin(m).count("1")
         ids = [DstId(rid=topo.addr(c, core)[0], pnc=topo.addr(c, core)[1]) for c in peers]
-        for name in ("uq", "uqs"):
-            src, dsts = A(name, 0, 4), [A(name, USLOT[k], USLOT[k] + 4) for k in USLOT]
-            order("g", [src], [])
-            a, bs = src[0], [d[0] for d in dsts]
-            if name == "uq":
-                a, bs = a.bitcast(dt.uint8), [b.bitcast(dt.uint8) for b in bs]
-            g.remote_dma_fused([RemoteDMATransfer(dst_ids=ids, dma_engine_mask=m, remote_sem=T.sem.ru, srcs=[a], dsts=bs)],
-                               local_sem=T.sem.sent)
-            count["sent"] = count.get("sent", 0) + n
-        count["ru"] = 2 * len(peers) * n
-        note("net", [], [A("uq", 128, 140), A("uqs", 128, 140)], ("ru", count["ru"]))
+        srcs = [A(name, 0, 4) for name in ("uq", "uqs")]
+        lands = [[A(name, USLOT[k], USLOT[k] + 4) for k in USLOT] for name in ("uq", "uqs")]
+
+        def issue():
+            order("g", srcs, [])
+            for src, dsts in zip(srcs, lands):
+                a, bs = src[0], [d[0] for d in dsts]
+                if src[1] == "uq":
+                    a, bs = a.bitcast(dt.uint8), [b.bitcast(dt.uint8) for b in bs]
+                g.remote_dma_fused([RemoteDMATransfer(dst_ids=ids, dma_engine_mask=m, remote_sem=T.sem.ru, srcs=[a], dsts=bs)],
+                                   local_sem=T.sem.sent)
+                count["sent"] = count.get("sent", 0) + n
+            count["ru"] = 2 * len(peers) * n
+            note("net", [], lands[0] + lands[1], ("ru", count["ru"]))
+        ops.append(("g", srcs, lands[0] + lands[1], issue))
 
     def ts(out, in0, s1, op0, s2=None, op1=None):
         if op1 is None:
@@ -182,11 +231,25 @@ def rank_program(g, core, T, topo):
             return g.scalar.activation(out[0], a[0], fn, **kw)
         run("a", [a, scale, bias], [out] + ([acc] if acc is not None else []), go)
 
+    def lin(k, out, a, scale, bias=None):
+        if CFG.get(k, "a") == "a":
+            act(out, a, scale, bias)
+        elif bias is None:
+            ts(out, a, scale, OP.mult)
+        else:
+            ts(out, a, scale, OP.mult, bias, OP.add)
+
     def iota(out, pat, base=0, cm=0, small=True):
         if small:
             run("g", [], [out], lambda: g.iota(out[0], pat, base, cm, allow_small_or_imprecise_dtypes=True))
         else:
             run("g", [], [out], lambda: g.iota(out[0], pat, base, cm))
+
+    def afill(out, c):
+        lin("fill", out, A("row", 0, len(out[4]), 1, out[2], out[3]), 0.0, c)
+
+    def gfill(out, c):
+        run("g", [out], [out], lambda: g.affine_select(out[0], out[0], [[0, len(out[4])]], OP.is_gt, c, 0, 0), True)
 
     def quant(name, c0, tile, e0, n):
         o, s, i = A(name, c0, c0 + n), A(name + "s", c0, c0 + n), A(tile, e0, e0 + 4 * n)
@@ -210,22 +273,21 @@ def rank_program(g, core, T, topo):
     def C(k, p0=0, p1=128):
         return A("cf", k, k + 1, 1, p0, p1)
 
-    P31, P15, PH, P3, PQ, IL, HB, HS, NA, NB = range(10)
+    P31, P15, PH, P3, PQ, IL, HB, NA, NB, HS, HI, HAS, NH = range(13)
     PP, P64 = 122, 123
 
     def LV(l, k, p0=0, p1=128):
         return C(16 + 28 * l + k, p0, p1)
     (RANK, V_, H_, PM, PLR, NON, PC, PJ, UU, AA, VP, HA, D_, SG, R_, SH, T1, T2, KAP, PHI, TAU, NK, NR, NK2, PLV,
-     PAO) = range(26)
+     PAO, SN, NKS) = range(28)
     M8, M8B = 0, 8
 
     def S(k, n=8):
         return A("sm", k, k + n)
 
-    stores = []
-
-    dma("s", T.xt[:], T.x[:], [], [A("xt")])
+    dma("s", T.xt[:, 128:640], T.x[:], [], [A("xt", 128, 640)])
     dma("s", T.ut[:], T.u[:], [], [A("ut")])
+    dma("s", T.wt[:], T.w[:], [A("ut", 256)], [A("wt")])
     iota(A("row"), [[1, 128]])
     iota(A("cf", 120, 125), [[64, 5]], -128, 1)
     iota(A("ci", 15), [[0, 1]], 0, 1, False)
@@ -236,12 +298,11 @@ def rank_program(g, core, T, topo):
     ms(LV(0, SG), 0.5)
     ms(A("psi", 0, 32, 1, 32, 64), 4.0 * BELOW)
     ms(A("psi", 0, 32, 1, 96, 128), 4.0 * BELOW)
-    act(A("the"), A("ta", 0, 516))
+    act(A("the", 128, 648), A("ta"))
     ts(A("idn"), A("row"), C(PP), OP.is_equal)
     ts(A("sf"), A("row"), C(PP), OP.is_gt, 1.0, OP.add)
     run("g", [A("sf")], [A("am")], lambda: g.affine_select(T.am[:], T.sf[:], [[-1, 128]], OP.not_equal, 128.0, 0, 1))
     iota(A("ra"), [[0, 8], [1, 4], [0, 4]])
-    iota(A("tz"), [[0, 840]])
     pi = A("ci", 15)
     ts(A("ci", P31), pi, 31, OP.bitwise_and)
     ts(A("ci", P15), pi, 15, OP.bitwise_and)
@@ -251,7 +312,7 @@ def rank_program(g, core, T, topo):
     ms(C(HB, 0, 64), BIG)
     ms(C(HB, 64, 128), -BIG)
     cp(A("cf", 0, 5), A("ci", 0, 5))
-    act(A("the", 3, 515, 4), A("idn"), 0.5)
+    act(A("the", 131, 643, 4), A("idn"), 0.5)
     ms(A("bm", 128), -64.5)
     ms(A("ta", 516), SB)
     ts(A("psi", 96, 128), A("row", 0, 32), C(P31), OP.is_ge, BELOW, OP.max)
@@ -260,110 +321,138 @@ def rank_program(g, core, T, topo):
     act(A("ta", 1, 512, 4), A("idn"), -0.5 * SB)
     act(A("ts", 0, 512, 4), A("am"), SA)
     act(C(IL), C(P15), 1.0 / 16)
-    quant("buf0", 64, "xt", 0, 128)
-    wait("s", ("d1", 16))
-    dma("s", T.wt[:], T.w[:], [], [A("wt")])
-
-    def u_list(*groups):
-        for c0, c1, v in groups:
-            ms(A("ou", c0, c1), v)
+    quant("buf0", 64, "xt", 128, 128)
 
     def u_send():
         quant("uq", 0, "ut", 0, 128)
         send_u()
         iota(A("th", 0, 256), [[0, 256]])
         iota(A("te", 0, 256), [[0, 256]])
+        a, b = USLOT[PART[0]], USLOT[PART[1]]
+        iota(A("oi", 0, 8), [[a + 2, 2], [0, 4]], 0, 0, False)
+        iota(A("oi", 8, 16), [[a - 2, 2], [0, 4]], 2, 0, False)
+        iota(A("oi", 16, 24), [[b + 2, 2], [a, 2], [0, 2]], 1, 0, False)
+        iota(A("oi", 24, 32), [[b - 2, 2], [a, 2], [0, 2]], 3, 0, False)
         iota(A("r16"), [[0, 8], [1, 16]])
+        iota(A("the", 0, 128), [[0, 128]])
+        iota(A("tf"), [[0, 520]])
 
     def u_pick(k):
-        pick("ur", 128 * k, "uq", 0, 160, A("ou", 8 * k, 8 * k + 8))
+        pick("ur", 128 * k, "uq", 0, 288, A("ou", 8 * k, 8 * k + 8))
 
     def rows4(t0, t1):
         for t in range(t0, t1):
             ts(A("tg", t, 512, 4), A("ra"), float(t), OP.is_equal, 64.0, OP.mult)
 
-    def rows16(t0, t1):
-        for t in range(t0, t1):
-            ts(A("tg", t, 512, 4), A("r16"), C(P15), OP.is_equal)
+    def rows16():
+        ts(A("tg", 0, 512, 4), A("r16"), C(P15), OP.is_equal)
+        for t in range(1, 4):
+            lin("r16", A("tg", t, 512, 4), A("tg", 0, 512, 4), 1.0)
 
     def unpackers(b0, b1):
         for b in range(b0, b1):
-            quant("qe", 128 * b, "the", 3 - b, 128)
+            quant("qe", 128 * b, "the", 131 - b, 128)
 
     def halves(f):
         f(0, 64, 64)
         f(64, 128, 0)
 
-    def quarters(name, c, ks):
-        for k in ks:
-            ms(A(name, 32 * (k ^ 1), 32 * (k ^ 1) + 32, 1, 32 * k, 32 * k + 32), c)
+    def quarters(name, c):
+        for k in range(4):
+            gfill(A(name, 32 * (k ^ 1), 32 * (k ^ 1) + 32, 1, 32 * k, 32 * k + 32), c)
 
-    def counts(l):
-        ms(A("tz", 4 * TF + 2, 4 * TF + 512, 4, 0, 1), -float(64 >> l))
-        ms(A("tz", 4 * TF + 513), 0.5 - (64 >> l))
-        ms(A("bm", 128), -0.5 - (64 >> l))
+    def counts(l, f):
+        f(A("tf", 2, 512, 4, 0, 1), -float(64 >> l))
+        f(A("tf", 513), 0.5 - (64 >> l))
+        f(A("bm", 128), -0.5 - (64 >> l))
 
     def score_order():
         ts(A("ls", 0, 64, 1, 0, 64), A("row", 0, 64, 1, 0, 64), C(PP, 0, 64), OP.is_lt, -TINY, OP.mult)
         ts(A("ls", 64, 128, 1, 64, 128), A("row", 64, 128, 1, 64, 128), C(PP, 64, 128), OP.is_gt, -TINY, OP.mult)
 
     def kin_piv(l):
+        ts(LV(l, SN), LV(l, RANK), 0.0, OP.is_lt)
         ts(LV(l, NON), LV(l, RANK), 0.0, OP.is_gt)
-        ts(LV(l, PC), LV(l, RANK), 0.0, OP.is_lt, C(P64), OP.mult)
-        ts(LV(l, PJ), LV(l, RANK), 0.0, OP.is_lt, C(PP), OP.mult)
+        act(LV(l, PJ), LV(l, SN), C(PP), None, AF.Relu)
+        act(LV(l, PC), LV(l, SN), C(P64), None, AF.Relu)
 
     def kin_pos(l):
         ts(A("th", 0, 256, 4), A("k64", 64 * l, 64 * l + 64), LV(l, PM), OP.is_equal, 64.0, OP.mult)
 
     def kin_vp(l):
-        act(LV(l, VP), LV(l, V_), LV(l, NON), LV(l, PJ))
+        lin("vp", LV(l, VP), LV(l, V_), LV(l, NON), LV(l, PJ))
 
     def kin_par(l, k):
         ts(A("th", 256, 768, 4), A("row"), LV(l, k), OP.is_equal)
 
     NOR = [8, 4, 4]
 
-    def kin_a(l):
-        n, e = NOR[l], 4 * (TL + 8)
-        return [lambda: ts(LV(l, UU), LV(l, PM), 1.0 / (SA * SB), OP.mult, LV(l, NK) if l else 191.0, OP.subtract),
-                lambda: ts(LV(l, AA), LV(l, UU), LV(l, NON), OP.mult, LV(l, PC), OP.add),
-                lambda: ts(LV(l, HA), LV(l, AA), M32, OP.add, M32, OP.subtract),
-                lambda: (ts(A("tz", e, e + 4 * n, 4), A("ones", 0, n), LV(l, HA), OP.mult),
-                         ts(A("tz", e + 1, e + 4 * n, 4), S(M8, n), LV(l, AA), OP.mult, LV(l, HA), OP.subtract))]
+    def TZ(c, t, n=8):
+        return A("the", 4 * c + t, 4 * (c + n), 4)
 
-    HBK = [7, 7, 6]
-    LBK = [7, 7, 6]
+    def kin_a(l):
+        n = NOR[l]
+        return [lambda: lin("uu", LV(l, UU), LV(l, PM), 1.0 / (SA * SB), LV(l, NK) if l else -191.0),
+                lambda: lin("aa", LV(l, AA), LV(l, UU), LV(l, NON), LV(l, PC)),
+                lambda: ts(LV(l, HA), LV(l, AA), M32, OP.add, M32, OP.subtract),
+                lambda: (lin("ha", TZ(8, 0, n), A("ones", 0, n), LV(l, HA)),
+                         ts(TZ(8, 1, n), S(M8, n), LV(l, AA), OP.mult, LV(l, HA), OP.subtract))]
+
+    KB = [7, 7, 6]
 
     def kin_h(l, n=192):
         quant("qh", 0, "th", 0, n)
-        mm(HBK[l], "qh", 64, "qh", 0)
+        mm(KB[l], "qh", 64, "qh", 0)
 
     def kin_first(l):
-        scan(A("so", 0, 64), P(HBK[l], 0, 64), A("ones"), -64.0, OP.max, OP.add)
-        scan(A("so", 64, 128), P(HBK[l], 0, 64), A("st16"), -64.0, OP.max, OP.add)
+        scan(A("so", 0, 64), P(KB[l], 0, 64), A("ones"), -64.0, OP.max, OP.add)
+        scan(A("so", 64, 128), P(KB[l], 0, 64), A("st16"), -64.0, OP.max, OP.add)
 
     def kin_has(l):
-        n, e = NOR[l], 4 * (TL + 8) + 2
-        ts(A("tz", e, e + 4 * n - 2, 4), S(M8B, n), A("so", 63), OP.mult, 128.0, OP.min)
+        ts(TZ(8, 2, NOR[l]), S(M8B, NOR[l]), A("so", 63), OP.mult, 128.0, OP.min)
 
     def kin_tile(l):
-        ts(A("tz", 4 * TL, 4 * TL + 32, 4), A("ones", 0, 8), A("so", 127), OP.mult)
-        ts(A("tz", 4 * TL + 1, 4 * TL + 32, 4), S(M8), A("so", 63), OP.mult, A("so", 127), OP.subtract)
+        lin("so%d" % l, TZ(0, 0), A("ones", 0, 8), A("so", 127))
+        ts(TZ(0, 1), S(M8), A("so", 63), OP.mult, A("so", 127), OP.subtract)
         if l < 2:
             kin_has(l)
 
+    def kin_zero():
+        ts(C(HAS), A("so", 63), 1.0, OP.min)
+        lin("z", TZ(16, 0), S(M8), float(ZERO))
+        ts(TZ(16, 1), S(M8), C(HAS), OP.mult, C(HI), OP.mult)
+        ts(TZ(16, 2), S(M8), C(HAS), OP.mult, C(P15), OP.mult)
+        lin("z", TZ(24, 0), TZ(8, 0), 1.0)
+        lin("z", TZ(24, 1), TZ(8, 1), 1.0)
+        lin("z", TZ(24, 2), TZ(16, 1), -1.0)
+        lin("z", TZ(24, 3), TZ(16, 2), -1.0)
+
+    def kin_through():
+        lin("z", A("tg", 0, 256, 4), A("ones"), 0.0)
+        ts(A("tg", 1, 256, 4), A("idn", 0, 64), LV(1, AA), OP.mult, LV(1, HA), OP.subtract)
+        lin("z", A("tg", 2, 256, 4), A("idn", 0, 64), C(NH))
+        lin("z", A("tg", 3, 256, 4), A("ones"), LV(1, HA))
+        quant("qc", 0, "tg", 0, 128)
+        mm(3, "qo", 0, "qc", 0)
+        act(A("rw", 0, 64), P(3, 0, 64))
+        run("v", [A("rw"), A("oc0"), A("m16")], [A("gc")],
+            lambda: g.vector.tensor_tensor(T["gc"][:], T.rw[:].indirect(T.oc0[:]), T.m16[:], OP.mult))
+        scan(A("gd"), A("r0"), A("gc"), 0.0, OP.mult, OP.add)
+        cp(A("od"), A("gd", 15, 128, 16))
+
     def kin_list(l):
-        quant("ql", 0, "tz", 4 * TL, 128)
-        mm(LBK[l], "qwc", 0, "ql", 0)
+        quant("ql", 0, "the", 0, 128)
+        mm(KB[l], "qwc", 0, "ql", 0)
 
     def kin_c(l):
-        ts(A("oc%d" % l), P(LBK[l], 0, 8), -1.0, OP.mult, 64.0, OP.add)
+        ts(A("oc%d" % l), P(KB[l], 0, 8), -1.0, OP.mult, 64.0, OP.add)
 
     def kin_r(l, c):
-        cp(A("or%d" % l, 0, NOR[l]), P(7, c, c + NOR[l]))
+        n = NOR[l] if l else 24
+        cp(A("or%d" % l, 0, n), P(7, c, c + n))
 
     def place_of(l):
-        ts(LV(l, PLV), LV(l, PLR), 1.0 / (SA * SB), OP.mult, LV(l, NK2), OP.add)
+        lin("plv", LV(l, PLV), LV(l, PLR), 1.0 / (SA * SB), LV(l, NK2))
 
     def place_tile(l):
         ts(A("th", 768, 1280, 4), A("row"), LV(l, PLV), OP.is_equal)
@@ -375,26 +464,22 @@ def rank_program(g, core, T, topo):
     def place_mm(bank):
         mm(bank, "qh", 192, "qh", 64)
 
-    def place_pick(bank):
+    def place_out(l, bank):
         tt(A("plr", 128, 256), P(bank, 0, 128), A("plr", 0, 128), OP.mult)
-
-    def place_out(l):
-        act(A("jk", 144, 272), A("plr", 128, 256), acc=LV(l, PAO))
+        act(A("jk", 272, 400), A("plr", 128, 256), acc=LV(l, PAO))
         parents_out(l)
 
     def parents_out(l):
         n, at = 128 >> l, [0, 128, 192][l]
         src = LV(l, PAO if l else VP, 0, n)
-        stores.append(lambda: dma("s", T.pa[0, at:at + n], src[0], [src], []))
-
-    def store():
-        while stores:
-            stores.pop(0)()
+        dma("s", T.pa[0, at:at + n], src[0], [src], [])
 
     def up(l, F):
         bn, bo = "buf%d" % l, BASE[l] + 64
 
         def L(k, p0=0, p1=128):
+            if l and k in (SG, R_):
+                return A("sr", 258, 259, 1, p0, p1)
             return LV(l, k, p0, p1)
 
         def fill(k):
@@ -411,26 +496,23 @@ def rank_program(g, core, T, topo):
         fill(0)
         tt(A("mx", 0, 128), P(4, 0, 128), A("idn"), OP.mult)
         if l:
-            tt(A("tz", 4 * TF + 1, 4 * TF + 512, 4), P(5, 0, 128), A("ls"), OP.is_gt)
+            tt(A("tf", 1, 512, 4), P(5, 0, 128), A("ls"), OP.is_gt)
             act(A("jk", 0, 129), A("mx", 0, 129), acc=L(D_))
             fill(1)
-            red(L(R_), A("tz", 4 * TF + 1, 4 * TF + 514, 4))
-            quant("qb", 0, "tz", 4 * TF, 128)
+            scan(A("sr", 0, 259), A("tf", 1, 518, 2), A("cl", 0, 259), 0.0, OP.subtract, OP.min)
+            quant("qb", 0, "tf", 0, 128)
             mm(6, "qs0", 0, "qb", 0)
             unpack()
-            act(L(T1), L(D_), BELOW)
-            act(A("gs"), P(4, 0, 128), 2.0 ** -18)
-            ts(L(SG), L(R_), -0.5, OP.max, 0.5, OP.min)
-            ts(L(SH), L(R_), C(HB), OP.mult)
-            ts(L(NR), L(R_), -1024.0, OP.mult)
-            ts(L(PHI), L(R_), 0.0, OP.is_gt, BELOW, OP.max)
-            act(L(KAP), L(SG), C(HS), 1.5 * SA)
-            act(L(NK), L(SG), 32.0, 143.0 if l == 1 else C(NA))
+            lin("t1", L(T1), L(D_), BELOW)
+            act(A("gs"), P(4, 0, 128), SC)
+            lin("nr", L(NR), L(R_), -1024.0)
+            lin("sh", L(SH), L(R_), C(HB))
+            ts(L(PHI), L(R_), SC * BELOW, OP.max, SC, OP.min)
         else:
             fill(1)
             red(L(D_), A("mx", 0, 129), OP.max)
-            act(A("gs"), P(4, 0, 128), 2.0 ** -18)
-            act(L(T1), L(D_), BELOW)
+            act(A("gs"), P(4, 0, 128), SC)
+            lin("t1", L(T1), L(D_), BELOW)
             fill(2)
         ts(A("xs", 64, 128), A("psi", 64, 128), L(D_), OP.mult, L(SG), OP.mult)
         if l < 2:
@@ -438,12 +520,15 @@ def rank_program(g, core, T, topo):
                 a, b = 32 * k, 32 * (k ^ 1)
                 ts(A("xs", 0, 64, 1, b, b + 32), A("psi", 0, 64, 1, a, a + 32), L(D_, a, a + 32), OP.mult, L(SG, a, a + 32), OP.mult)
         if l:
-            ts(L(TAU), L(SG), 0.0, OP.min, 2.0 ** -109, OP.mult)
+            lin("kap", L(KAP), L(SG), C(HS), 1.5 * SA)
             act(A("same"), P(6, 0, 128), L(NR), None, AF.Relu)
-            halves(lambda p0, p1, c: act(A("am", c, c + 64, 1, p0, p1), A("ones" if l == 1 else "pc", 0, 64, 1, p0, p1), L(KAP, p0, p1)))
-            act(A("gt", 0, 64), A("gs", 0, 64), L(PHI), L(TAU))
-            act(A("gt", 64, 128), A("gs", 64, 128), L(PHI))
-        ts(L(T2), L(SH) if l else C(HB), L(T1), OP.max, L(D_), OP.min)
+            halves(lambda p0, p1, c: lin("am", A("am", c, c + 64, 1, p0, p1), A("ones" if l == 1 else "pc", 0, 64, 1, p0, p1),
+                                         L(KAP, p0, p1)))
+            lin("tau", L(TAU), L(SG), 2.0 ** -109, -2.0 ** -110)
+            act(A("gt", 64, 128), P(4, 64, 128), L(PHI))
+            act(A("gt", 0, 64), P(4, 0, 64), L(PHI), L(TAU))
+            lin("nk", L(NKS), L(SG), 32.0 * SA * SB, 143.0 * SA * SB if l == 1 else C(NA))
+            lin("nk", L(NK), L(NKS), -1.0 / (SA * SB))
         fill(3)
         w = 64 if l < 2 else 32
         tr(A("zz", 0, 32), A("xs", 96, 128))
@@ -454,6 +539,7 @@ def rank_program(g, core, T, topo):
             unpack()
         for b in range(4):
             act(A("dm", b, 512, 4), P(b, 0, 128), -1.0)
+        ts(L(T2), L(SH) if l else C(HB), L(T1), OP.max, L(D_), OP.min)
         fill(4)
         ts(A("bm", 128 - 2 * w, 128 - w), A("zz", 0, w), L(SG), OP.mult, L(T1), OP.is_gt)
         ts(A("bm", 128 - w, 128), A("zz", w, 2 * w), L(SG), OP.mult, L(T2), OP.is_gt)
@@ -468,54 +554,52 @@ def rank_program(g, core, T, topo):
         ts(A("ta", 512), L(RANK), 0.0, OP.is_gt, SB, OP.mult)
         ts(A("ta", 0, 512, 4), A("kk"), L(RANK), OP.is_gt, SB, OP.mult)
         if l:
-            tt(A("gs", 0, 64), A("gs", 0, 64), A("gt", 0, 64), OP.min)
+            tt(A("gs", 64, 128), A("gs", 64, 128), A("gt", 64, 128), OP.max)
         fill(6)
         quant("qa", 0, "ta", 0, 130)
         mm(5, "qs%d" % l, 0, "qa", 0, 130)
         if l:
-            tt(A("gs", 64, 128), A("gs", 64, 128), A("gt", 64, 128), OP.max)
-            ts(A("k64", 64 * l, 64 * l + 64), A("row", 0, 64), L(NK), OP.add, SA * SB, OP.mult)
-            act(L(NK2), L(SG), -64.0, -159.0 if l == 1 else C(NB))
-        if l == 2:
-            kin_piv(l)
+            tt(A("gs", 0, 64), A("gs", 0, 64), A("gt", 0, 64), OP.min)
+            lin("k64", A("k64", 64 * l, 64 * l + 64), A("row", 0, 64), SA * SB, L(NKS))
         fill(7)
         kk, pm = A("k64", 64 * l, 64 * l + 64), P(5, 128)
         tt(A("mk"), A("gs"), P(5, 0, 128), OP.min)
-        ts(A("tz", 4 * TN, 4 * TN + 64), kk, pm, OP.is_equal, C(PH), OP.mult)
-        ts(A("tz", 4 * TN + 64, 4 * TN + 128), kk, pm, OP.is_equal, C(IL), OP.mult)
+        ts(A("xt", 640, 704), kk, pm, OP.is_equal, C(PH), OP.mult)
+        ts(A("xt", 704, 768), kk, pm, OP.is_equal, C(IL), OP.mult)
         scan(A("rm"), A("mk"), A("mk"), -BIG, OP.max, OP.max)
         act(A("jk", 0, 128), A("rm"), -1.0, A("rm", 127), AF.Sign, L(V_))
-        act(A("jk", 128, 136), A("rm", 15, 128, 16), -1.0, A("rm", 127), AF.Sign, L(H_))
-        act(A("tz", 4 * TP, 4 * TP + 64), A("ones"), L(H_))
-        quant("qn", 0, "tz", 4 * TN, 144)
+        act(A("jk", 136, 144), A("rm", 15, 128, 16), -1.0, A("rm", 127), AF.Sign, L(H_))
+        lin("tp", A("xt", 0, 64), A("ones"), L(H_))
+        quant("qn", 0, "xt", 192, 144)
         mm(6, "qw64", 0, "qn", 0, 128, True, False)
         mm(6, "qw64", 0, "qn", 16, 128, False, True)
         ts(A("eq"), kk, pm, OP.is_equal, 1.0 / 16, OP.mult)
-        cp(A("cf", 16 + 28 * l + PM, 16 + 28 * l + PM + 2), P(5, 128, 130))
+        lin("pm%d" % l, A("cf", 16 + 28 * l + PM, 16 + 28 * l + PM + 2), P(5, 128, 130), 1.0)
         if l == 2:
             kin_pos(l)
-            kin_a(l)[0]()
-            kin_par(l, V_)
+            ts(A("th", 1, 256, 4), kk, L(PM), OP.is_equal, 64.0, OP.mult)
+            ts(A("th", 256, 768, 4), A("rm"), A("rm", 127), OP.is_ge)
+            ts(A("th", 261, 768, 4), A("rm", 0, 127), A("rm", 127), OP.is_ge, -1.0, OP.mult)
         else:
             fill(8)
-        ts(A("tz", 4 * TP + 64, 4 * TP + 128), A("eq"), L(V_), OP.mult, L(H_), OP.subtract)
-        ts(A("on"), P(6, 0, 16), C(P3), OP.add)
+        ts(A("xt", 64, 128), A("eq"), L(V_), OP.mult, L(H_), OP.subtract)
+        ts(A("on"), P(6, 112, 128), C(P3), OP.add)
         run("a", [A("dm"), A("on")], [A("dn")],
             lambda: g.scalar.activation(T.dn[:], T.dm[:].indirect(T.on[:]), AF.Copy, scale=-2.0))
         if l == 2:
             kin_h(l)
-        else:
-            kin_piv(l)
-        quant("qp", 0, "tz", 4 * TP, 144)
+        quant("qp", 0, "xt", 0, 144)
         mm(7, "qw64", 0, "qp", 0, 128, True, False)
         mm(7, "qw64", 0, "qp", 16, 128, False, True)
-        kin_vp(l)
+        if l < 2:
+            kin_piv(l)
+            kin_vp(l)
         if l:
             place_row(l)
         if l == 2:
-            kin_a(l)[1]()
             kin_first(l)
-            kin_a(l)[2]()
+            kin_piv(l)
+            kin_vp(l)
             for b in range(4):
                 mm(b, "qe", 128 * b, bn, bo, 128, True, False)
             kin_tile(l)
@@ -525,15 +609,17 @@ def rank_program(g, core, T, topo):
             fill(9)
         ts(A("op"), P(7, 0, 16), C(P3), OP.add)
         if l == 2:
+            kin_a(l)[0]()
             kin_list(l)
         else:
             kin_a(l)[1]()
             if l:
-                place_of(l)
+                lin("nk2", L(NK2), L(SG), -64.0, -159.0)
             fill(10)
         run("v", [A("dm"), A("op"), A("dn")], [A("te", 256, 512)],
             lambda: g.vector.tensor_tensor(T.te[:, 256:512], T.dm[:].indirect(T["op"][:]), T.dn[:], OP.add))
         if l == 2:
+            kin_a(l)[1]()
             kin_c(l)
         else:
             kin_par(l, VP)
@@ -545,30 +631,39 @@ def rank_program(g, core, T, topo):
         remote(peer, 2 * l, A(nb, at, at + 64), A(nb, at + 64, at + 128), True)
         remote(peer, 2 * l + 1, A(nb + "s", at, at + 64), A(nb + "s", at + 64, at + 128), False)
         if l:
+            place_of(l)
+            u_pick(3)
             place_tile(l)
             kin_a(l)[3]()
             kin_h(l, 320)
             place_mm(3)
-            quarters("am", 0.0, range(4))
             kin_first(l)
-            place_pick(3)
-            place_out(l)
+            place_out(l, 3)
+            kin_tile(l)
+            ts(C(NH), A("so", 63), 128.0, OP.mult, 128.0, OP.min)
         else:
             iota(A("th", 768, 1280), [[0, 512]])
             parents_out(l)
+            act(C(HS), C(HB), SA / BIG)
+            act(C(HI), C(PH), 16.0, 64.0 - ZERO)
             kin_h(l)
+            cp(A("ou"), A("oi"))
             u_pick(0)
             u_pick(1)
             ts(A("st16"), A("r16", 0, 64), 15.0, OP.is_equal, 16.0, OP.mult)
             kin_a(l)[3]()
             kin_first(l)
-            rows16(0, 3)
+            rows16()
             quant("qwc", 0, "tg", 0, 128)
-        kin_tile(l)
+            kin_tile(l)
+            kin_zero()
 
     def down(l, F):
         bn, b0, ch = "buf%d" % l, BASE[l], "ch%d" % l
-        pick(ch, 0, bn, b0, b0 + 192, A("oc%d" % l))
+        if l:
+            pick(ch, 0, bn, b0, b0 + 192, A("oc%d" % l))
+        else:
+            pick(ch, 0, "buf1", 0, ZERO + 2, A("od"))
         for b in range(4):
             mm(b, "qe", 128 * b, ch, 0, 128, False, True)
         F[0]()
@@ -581,58 +676,69 @@ def rank_program(g, core, T, topo):
         quant(bn, b0 + 192, "td", 0, 128)
         if l:
             for b in range(4):
-                mm(b, "qe", 128 * b, "buf%d" % (l - 1), BASE[l - 1] + 64, 128, True, False)
+                if l == 2:
+                    mm(b, "qe", 128 * b, "buf1", 64, 128, True, False)
+                else:
+                    mm(b, "qe", 128 * b, "pz", 0, 128, True, False)
             F[2]()
             pick("buf%d" % (l - 1), BASE[l - 1], bn, b0, b0 + 320, A("or%d" % l, 0, 4))
             F[3]()
-        else:
-            pick("ff", 0, bn, 0, 320, A("or0"))
 
     def nothing():
         pass
 
-    up(0, {0: lambda: (ts(A("kk"), A("row"), C(PP), OP.not_equal, -1000.0, OP.mult),
-                       ts(A("ut", 8, 16), A("ut", 0, 8), -1.0, OP.mult), unpackers(0, 2)),
+    up(0, {0: lambda: (lin("kk", A("kk"), A("idn"), 1000.0, -1000.0),
+                       lin("ut", A("ut", 8, 16), A("ut", 0, 8), -1.0), unpackers(0, 2)),
            1: lambda: unpackers(2, 3),
            2: lambda: u_send(),
            3: lambda: (unpackers(3, 4), act(A("th", 256, 768), A("ts"), 0.0, 1.0)),
            4: lambda: rows4(0, 3),
-           5: lambda: (rows4(3, 4), ts(A("k64", 0, 64), A("row", 0, 64), 191.0, OP.add, SA * SB, OP.mult),
-                       u_list((0, 4, 0))),
+           5: lambda: (rows4(3, 4), lin("k0", A("k64", 0, 64), A("row", 0, 64), SA * SB, 191.0 * SA * SB)),
            6: lambda: quant("qw64", 0, "tg", 0, 128),
-           7: lambda: (quant("qo", 0, "th", 256, 128), ms(A("ls"), BIG), u_list((4, 8, 130), (8, 12, 2), (12, 16, 128))),
-           8: lambda: (score_order(), counts(1)),
-           9: lambda: (act(A("am"), A("am"), SA), act(C(HS), C(HB), SA / BIG), ms(A("th", 1, 256, 4, 0, 1), -64.0),
-                       ms(A("tz", 4 * TF + 3, 4 * TF + 512, 4, 0, 1), 0.5), ts(S(M8), A("row", 0, 8), C(PH), OP.is_equal)),
-           10: lambda: ts(S(M8B), A("row", 0, 8), C(PH), OP.is_equal, 128.0, OP.mult)})
+           7: lambda: (quant("qo", 0, "th", 256, 128), lin("ls", A("ls"), A("row"), 0.0, BIG)),
+           8: lambda: (score_order(), counts(1, afill)),
+           9: lambda: (act(A("am"), A("am"), SA), afill(A("th", 2, 256, 4, 0, 1), -64.0),
+                       afill(A("tf", 2, 512, 4, 32, 33), 0.5), afill(A("cl", 0, 128), 1000.0), afill(A("cl", 128, 256), 1000.0),
+                       ms(A("cl", 256), 1000.0), ms(A("cl", 257, 259), 0.5), ts(S(M8), A("row", 0, 8), C(PH), OP.is_equal)),
+           10: lambda: lin("m8", S(M8B), S(M8), 128.0)})
     exchange(0)
-    up(1, {1: lambda: kin_list(0),
-           4: lambda: (kin_c(0), kin_r(0, 8), u_list((16, 18, 1))),
-           7: lambda: (u_list((18, 20, 129), (20, 22, 135), (22, 24, 139), (24, 26, 3)),
-                       act(C(NA), C(PQ), -16.0, 127.0), act(C(NB), C(PQ), 32.0, -127.0)),
-           8: lambda: (u_list((26, 28, 131), (28, 30, 133), (30, 32, 137)), quarters("ls", BIG, (0, 1))),
-           9: lambda: (u_pick(2), quarters("ls", BIG, (2, 3)), counts(2)),
+    up(1, {3: lambda: kin_list(0),
+           4: lambda: quarters("ls", BIG),
+           7: lambda: (counts(2, gfill), quarters("am", 0.0), quant("buf0", ZERO, "th", 768, 128),
+                       quant("buf1", ZERO, "th", 768, 128), ms(A("rw", 64, 72), float(ZERO)),
+                       ts(A("m16"), A("r16"), C(P15), OP.is_equal), ts(A("r0"), A("r16"), 0.5, OP.is_gt),
+                       act(C(NA), C(PQ), -16.0 * SA * SB, 127.0 * SA * SB), act(C(NB), C(PQ), 32.0, -127.0)),
+           8: lambda: (kin_c(0), kin_r(0, 8)),
+           9: lambda: u_pick(2),
            10: lambda: ts(A("pc"), A("row", 0, 64), 32.0, OP.is_ge, C(PQ), OP.is_equal)})
-    u_pick(3)
     exchange(1)
+    kin_through()
+    afill(A("th", 257), 0.0)
     up(2, {1: lambda: kin_list(1),
-           3: lambda: (kin_c(1), kin_r(1, 8)),
-           4: lambda: quant("wq", 0, "wt", 0, 128),
-           7: lambda: quant("wq", 128, "wt", 512, 128)})
-    down(2, [lambda: (kin_a(2)[3](), kin_has(2), place_of(2), quant("qr", 0, "tz", 4 * (TL + 8), 128), mm(7, "qwc", 0, "qr", 0)),
-             lambda: kin_r(2, 0), lambda: kin_par(2, VP), lambda: place_tile(2)])
-    store()
-    down(1, [lambda: (quant("qh", 64, "th", 256, 256), place_mm(4)), nothing,
-             lambda: quant("wq", 256, "wt", 1024, 128), nothing])
-    down(0, [lambda: place_pick(4), lambda: (place_out(2), store())])
+           4: lambda: (kin_c(1), kin_r(1, 8))})
+    kin_a(2)[2]()
+    lin("nk2", LV(2, NK2), A("sr", 258), -64.0, C(NB))
+    down(2, [lambda: (kin_a(2)[3](), kin_has(2), place_of(2), quant("qr", 0, "the", 32, 128), mm(7, "qwc", 0, "qr", 0)),
+             lambda: kin_r(2, 0), lambda: kin_par(2, VP), lambda: (place_tile(2), quant("wq", 0, "wt", 0, 128))])
+    down(1, [lambda: (pick("pz", 0, "buf0", 0, ZERO + 2, A("or0", 8, 16)), quant("qh", 64, "th", 256, 256), place_mm(7)),
+             nothing, lambda: quant("wq", 128, "wt", 512, 128), lambda: quant("wq", 256, "wt", 1024, 128)])
+    down(0, [lambda: (pick("fo", 0, "buf0", 0, ZERO + 2, A("or0", 16, 24)),
+                      [mm(4 + o, "wq", 128 * o, "fo", 0, 128, True, False) for o in range(3)]),
+             lambda: place_out(2, 7)])
     for o in range(3):
-        mm(4 + o, "wq", 128 * o, "ff", 0)
+        mm(4 + o, "wq", 128 * o, "buf0", 192, 128, False, True)
+    pick("ff", 0, "buf0", 0, 320, A("or0", 0, 8))
+    cp(A("ysb", 0, 128), P(4, 0, 128))
+    lin("y1", A("ysb", 128, 256), P(5, 0, 128), 1.0)
+    cp(A("ysb", 256, 384), P(6, 0, 128))
     dma("s", T.oc[:], T.ff[:].bitcast(dt.uint8), [A("ff")], [])
     for k in range(4):
-        dma("s", T.osc[4 * k:4 * k + 4, :], T.ffs[32 * k:32 * k + 4, :], [A("ffs")], [])
-    cp(A("ysb", 0, 128), P(4, 0, 128))
-    act(A("ysb", 128, 256), P(5, 0, 128))
-    cp(A("ysb", 256, 384), P(6, 0, 128))
+        dma("asss"[k], T.osc[4 * k:4 * k + 4, :], T.ffs[32 * k:32 * k + 4, :], [A("ffs")], [])
     dma("a", T.y[:], T.ysb[:], [A("ysb")], [])
-    for s, n in count.items():
-        wait("g", (s, n))
+
+    OPS[:] = ops
+    for k in ORDER or range(len(ops)):
+        ops[k][3]()
+    last = [(s, n) for s, n in count.items() if all(clock[q].get(s, 0) < n for q in Q)]
+    for tok in sorted(last, key=lambda t: (t == ytok[0], when.get(t, 0))):
+        wait("g", tok)

from concourse.bass import DstId, RemoteDMATransfer
from concourse.mybir import dt, AluOpType, AxisListType, ActivationFunctionType

OP = AluOpType
AF = ActivationFunctionType
MX, U8, F32, BF, U16, I32 = "float8_e4m3fn_x4", "uint8", "float32", "bfloat16", "uint16", "int32"

CODES = {"qa": 130, "qn": 144, "qp": 144, "ql": 128, "qr": 128, "qb": 128, "qh": 320, "qs0": 128, "qs1": 128, "qs2": 128,
         "qe": 512, "qw64": 128, "qwc": 128, "qo": 128, "uq": 288, "ur": 512, "wq": 384,
         "buf0": 448, "buf1": 448, "buf2": 384, "ch0": 128, "ch1": 128, "ch2": 128, "ff": 128, "pz": 128, "fo": 128,
         "qc": 128}
SCRATCH = {}
for _n, _c in CODES.items():
    SCRATCH[_n] = ("sbuf", [128, _c], MX)
    SCRATCH[_n + "s"] = ("sbuf", [128, _c], U8)
for _n, _c, _d in [("xt", 768, BF), ("tf", 520, BF), ("cl", 264, F32), ("sr", 264, F32),
                   ("ut", 512, BF), ("wt", 1536, BF), ("ta", 520, BF), ("ts", 512, BF),
                   ("the", 648, BF), ("te", 512, BF), ("th", 1280, BF), ("tg", 512, BF),
                   ("td", 512, BF), ("r16", 128, BF), ("ra", 128, BF),
                   ("row", 128, F32), ("idn", 128, F32), ("am", 128, F32), ("sf", 128, F32), ("kk", 128, F32),
                   ("psi", 128, F32), ("k64", 192, F32), ("ls", 128, F32), ("ones", 64, F32), ("pc", 64, F32),
                   ("mx", 136, F32), ("xs", 128, F32), ("zz", 128, F32), ("bm", 136, F32), ("same", 128, F32),
                   ("gs", 128, F32), ("gt", 128, F32), ("mk", 128, F32), ("rm", 128, F32), ("jk", 400, F32),
                   ("eq", 64, F32), ("rw", 72, F32), ("m16", 128, F32), ("r0", 128, F32), ("gc", 128, F32),
                   ("gd", 128, F32), ("dm", 512, F32), ("dn", 256, F32), ("so", 128, F32), ("plr", 256, F32),
                   ("st16", 64, F32), ("sm", 16, F32), ("cf", 128, F32), ("ci", 16, I32), ("oi", 32, I32),
                   ("ysb", 384, F32),
                   ("on", 16, U16), ("op", 16, U16), ("oc0", 8, U16), ("oc1", 8, U16), ("oc2", 8, U16),
                   ("or0", 24, U16), ("or1", 8, U16), ("or2", 8, U16), ("ou", 32, U16), ("od", 8, U16)]:
    SCRATCH[_n] = ("sbuf", [128, _c], _d)
for _k in range(8):
    SCRATCH["ps%d" % _k] = ("psum", [128, 512], F32)

NDMA = 16
SEMAPHORES = ["sv", "sa", "sp", "sg", "sent", "ru"] + ["d%d" % k for k in range(NDMA)] + ["r%d" % k for k in range(4)]

PART = [4, 2]
BASE = [0, 0, 64]
ZERO = 320
USLOT = {4: 128, 2: 132, 6: 260}
TINY = 2.0 ** -100
BIG = 1e29
BELOW = 1.0 - 2.0 ** -24
M32 = 1.5 * 2.0 ** 28
SA, SB = 2.0 ** 22, 2.0 ** 29
SC = 2.0 ** -18
CFG = {"so2": "v", "pm0": "v", "pm1": "v", "pm2": "v", "ut": "v", "y1": "v"}
OPS = []

ORDER = [int(_k) for _k in """
6 8 9 5 3 21 22 19 7 4 18 27 20 14 24 23 13 37 0 26 25 15 11 29 35 49 12 54 42 85 1 39 48 31 34 38 50 36 30 10 70 41 46 17 16
43 40 57 60 61 74 45 58 59 76 52 67 64 66 44 65 28 81 69 80 62 143 83 33 82 86 87 142 79 84 32 68 89 2 71 78 77 72 151 116 47
90 63 88 93 56 95 96 92 94 119 53 109 103 100 75 101 102 98 130 128 97 110 156 99 113 114 115 111 104 118 51 73 91 122 117 131
159 112 158 120 134 135 137 157 160 124 126 138 139 144 55 133 129 127 106 121 145 146 150 132 108 105 147 154 148 173 149 123
174 136 165 164 167 166 155 125 153 152 162 176 169 172 175 171 168 178 161 107 181 163 179 170 177 190 192 191 193 194 195
188 185 214 208 206 187 183 209 207 189 220 180 198 197 196 219 199 204 205 222 186 221 225 224 223 201 227 200 229 226 278
265 228 202 257 245 184 230 247 212 213 182 141 248 250 246 249 255 252 266 258 251 211 259 256 253 210 262 254 286 260 261
140 239 279 215 216 217 218 267 231 238 273 263 264 276 232 233 234 269 203 243 289 304 268 280 235 281 283 236 270 237 292
442 284 285 293 294 271 315 272 277 287 282 274 295 297 291 305 303 288 275 316 317 296 307 449 306 301 300 314 240 308 326
318 319 302 298 290 323 324 309 450 320 335 334 310 330 336 333 332 345 352 346 329 347 339 325 338 355 337 341 356 321 322
358 357 340 360 361 327 359 363 331 342 343 395 362 365 328 353 366 350 364 367 349 369 368 378 401 370 344 397 371 374 377
382 379 402 381 380 372 299 373 348 383 351 375 376 384 386 354 388 244 387 389 390 462 398 385 394 393 396 415 404 405 406
407 399 408 403 411 409 410 400 412 413 425 424 417 414 416 418 423 419 422 420 441 465 426 421 242 427 428 429 430 436 431
432 437 433 440 241 439 434 435 438 443 444 311 451 447 455 448 445 453 446 391 312 460 456 454 313 392 457 466 452 463 467
464 458 459 473 461 468 477 481 472 471 470 479 480 469 482 483 475 478 484 476 474 489 488 485 490 493 495 496 497 487 486
492 494 491 498
""".split()]


def rank_program(g, core, T, topo):
    rank = T.rank_of(core)
    if rank is None:
        return
    Q = {"v": g.vector, "a": g.scalar, "p": g.tensor, "g": g, "s": g.sync}
    SEM = {"v": "sv", "a": "sa", "p": "sp", "g": "sg"}
    clock = {q: {} for q in Q}
    count = {}
    snap = {}
    log = {}
    when = {}
    ytok = [None]
    ndma = [0]
    ops = []

    def A(name, c0=None, c1=None, step=1, p0=0, p1=128):
        if c0 is None:
            c0, c1 = 0, SCRATCH[name][1][1]
        if c1 is None:
            c1 = c0 + 1
        t = T[name]
        ps = slice(None) if (p0, p1) == (0, 128) else slice(p0, p1)
        v = t[ps, c0:c1] if step == 1 else t[ps, c0:c1:step]
        return (v, name, p0, p1, frozenset(range(c0, c1, step)))

    def wait(q, tok):
        s, n = tok
        if clock[q].get(s, 0) >= n:
            return
        Q[q].wait_ge(T.sem[s], n)
        clock[q][s] = n
        for k, m in snap.get(tok, {}).items():
            if clock[q].get(k, 0) < m:
                clock[q][k] = m

    def order(q, reads, writes):
        need = {}
        for accs, wr in ((reads, False), (writes, True)):
            for a in accs:
                psum = SCRATCH[a[1]][0] == "psum"
                for (p0, p1, cols, w, oq, tok) in log.get(a[1], []):
                    if psum:
                        if oq == q and (q == "p" or not (w or wr)):
                            continue
                    elif not (w or wr) or p1 <= a[2] or a[3] <= p0 or cols.isdisjoint(a[4]):
                        continue
                    if need.get(tok[0], 0) < tok[1]:
                        need[tok[0]] = tok[1]
        keep, seen = [], dict(clock[q])
        for tok in sorted(need.items(), key=lambda t: -when[t]):
            if seen.get(tok[0], 0) < tok[1]:
                keep.append(tok)
                for k, m in snap.get(tok, {}).items():
                    seen[k] = max(seen.get(k, 0), m)
        for tok in keep[::-1]:
            wait(q, tok)

    def note(q, reads, writes, tok):
        snap[tok] = dict(clock[q]) if q in clock else {}
        when[tok] = len(when) + (0 if q in clock else 1000)
        for accs, wr in ((reads, False), (writes, True)):
            for a in accs:
                log.setdefault(a[1], []).append((a[2], a[3], a[4], wr, q, tok))

    def run(q, reads, writes, fn, alone=False):
        reads = [a for a in reads if isinstance(a, tuple)]

        def issue():
            s = SEM[q]
            if alone:
                wait(q, (s, count[s]))
            order(q, reads, writes)
            count[s] = count.get(s, 0) + 1
            fn().then_inc(T.sem[s], 1)
            note(q, reads, writes, (s, count[s]))
        ops.append((q, reads, writes, issue))

    def val(x):
        return x[0] if isinstance(x, tuple) else x

    def dma(q, out, in_, reads, writes):
        def issue():
            order(q, reads, writes)
            s = "d%d" % ndma[0]
            ndma[0] += 1
            Q[q].dma_start(out, in_).then_inc(T.sem[s], 16)
            count[s] = 16
            note("dma", reads, writes, (s, 16))
            snap[(s, 16)] = dict(clock[q])
            if q == "a":
                ytok[0] = (s, 16)
        ops.append((q, reads, writes, issue))

    def remote(peer_rank, k, src, dst, codes):
        peer = T.cores[peer_rank]
        rid, pid = topo.addr(peer, core)

        def issue():
            order("g", [src], [])
            a, b = (src[0].bitcast(dt.uint8), dst[0].bitcast(dt.uint8)) if codes else (src[0], dst[0])
            g.remote_dma(b, a, T.sem["r%d" % k], T.sem.sent, pid, rid, topo.mask(core, peer))
            count["sent"] = count.get("sent", 0) + len(topo.engines(core, peer))
            count["r%d" % k] = len(topo.engines(peer, core))
            note("net", [], [dst], ("r%d" % k, count["r%d" % k]))
        ops.append(("g", [src], [dst], issue))

    def send_u():
        peers = [T.cores[rank ^ k] for k in USLOT]
        m = topo.mask(core, peers[0])
        for c in peers:
            m &= topo.mask(core, c) & topo.mask(c, core)
        n = bin(m).count("1")
        ids = [DstId(rid=topo.addr(c, core)[0], pnc=topo.addr(c, core)[1]) for c in peers]
        srcs = [A(name, 0, 4) for name in ("uq", "uqs")]
        lands = [[A(name, USLOT[k], USLOT[k] + 4) for k in USLOT] for name in ("uq", "uqs")]

        def issue():
            order("g", srcs, [])
            for src, dsts in zip(srcs, lands):
                a, bs = src[0], [d[0] for d in dsts]
                if src[1] == "uq":
                    a, bs = a.bitcast(dt.uint8), [b.bitcast(dt.uint8) for b in bs]
                g.remote_dma_fused([RemoteDMATransfer(dst_ids=ids, dma_engine_mask=m, remote_sem=T.sem.ru, srcs=[a], dsts=bs)],
                                   local_sem=T.sem.sent)
                count["sent"] = count.get("sent", 0) + n
            count["ru"] = 2 * len(peers) * n
            note("net", [], lands[0] + lands[1], ("ru", count["ru"]))
        ops.append(("g", srcs, lands[0] + lands[1], issue))

    def ts(out, in0, s1, op0, s2=None, op1=None):
        if op1 is None:
            run("v", [in0, s1], [out], lambda: g.vector.tensor_scalar(out[0], in0[0], val(s1), None, op0))
        else:
            run("v", [in0, s1, s2], [out], lambda: g.vector.tensor_scalar(out[0], in0[0], val(s1), val(s2), op0, op1))

    def tt(out, a, b, op):
        run("v", [a, b], [out], lambda: g.vector.tensor_tensor(out[0], a[0], b[0], op))

    def cp(out, a):
        run("v", [a], [out], lambda: g.vector.tensor_copy(out[0], a[0]))

    def ms(out, c):
        run("v", [], [out], lambda: g.vector.memset(out[0], c))

    def red(out, a, op=OP.add):
        run("v", [a], [out], lambda: g.vector.tensor_reduce(out[0], a[0], AxisListType.X, op))

    def scan(out, a, b, init, op0, op1):
        run("v", [a, b], [out], lambda: g.vector.tensor_tensor_scan(out[0], a[0], b[0], init, op0, op1))

    def tr(out, a):
        run("v", [a], [out], lambda: g.vector.transpose(out[0], a[0]))

    def act(out, a, scale=1.0, bias=None, func=None, acc=None):
        def go():
            kw = {"scale": val(scale)}
            if bias is not None:
                kw["bias"] = val(bias)
            if acc is not None:
                kw["accum_out"] = acc[0]
            fn = func if func is not None else (AF.Copy if bias is None else AF.Identity)
            return g.scalar.activation(out[0], a[0], fn, **kw)
        run("a", [a, scale, bias], [out] + ([acc] if acc is not None else []), go)

    def lin(k, out, a, scale, bias=None):
        if CFG.get(k, "a") == "a":
            act(out, a, scale, bias)
        elif bias is None:
            ts(out, a, scale, OP.mult)
        else:
            ts(out, a, scale, OP.mult, bias, OP.add)

    def iota(out, pat, base=0, cm=0, small=True):
        if small:
            run("g", [], [out], lambda: g.iota(out[0], pat, base, cm, allow_small_or_imprecise_dtypes=True))
        else:
            run("g", [], [out], lambda: g.iota(out[0], pat, base, cm))

    def afill(out, c):
        lin("fill", out, A("row", 0, len(out[4]), 1, out[2], out[3]), 0.0, c)

    def gfill(out, c):
        run("g", [out], [out], lambda: g.affine_select(out[0], out[0], [[0, len(out[4])]], OP.is_gt, c, 0, 0), True)

    def quant(name, c0, tile, e0, n):
        o, s, i = A(name, c0, c0 + n), A(name + "s", c0, c0 + n), A(tile, e0, e0 + 4 * n)
        run("v", [i], [o, s], lambda: g.vector.quantize_mx(o[0], s[0], i[0]))

    def mm(bank, wn, wc, xn, xc, n=128, start=True, stop=True):
        o = A("ps%d" % bank, 0, n)
        w, ws, x, xs = A(wn, wc, wc + 128), A(wn + "s", wc, wc + 128), A(xn, xc, xc + n), A(xn + "s", xc, xc + n)
        run("p", [w, ws, x, xs], [o], lambda: g.tensor.matmul_mx(o[0], w[0], ws[0], x[0], xs[0], start, stop))

    def pick(dn, dc, sn, s0, s1, off):
        n = 16 * len(off[4])
        o, w = A(dn, dc, dc + n), A(sn, s0, s1)
        run("v", [w, off], [o], lambda: g.vector.tensor_copy(o[0].bitcast(dt.uint32), w[0].bitcast(dt.uint32).indirect(off[0])))
        o2, w2 = A(dn + "s", dc, dc + n), A(sn + "s", s0, s1)
        run("a", [w2, off], [o2], lambda: g.scalar.activation(o2[0], w2[0].indirect(off[0]), AF.Copy))

    def P(k, c0, c1=None, p0=0, p1=128):
        return A("ps%d" % k, c0, c1, 1, p0, p1)

    def C(k, p0=0, p1=128):
        return A("cf", k, k + 1, 1, p0, p1)

    P31, P15, PH, P3, PQ, IL, HB, NA, NB, HS, HI, HAS, NH = range(13)
    PP, P64 = 122, 123

    def LV(l, k, p0=0, p1=128):
        return C(16 + 28 * l + k, p0, p1)
    (RANK, V_, H_, PM, PLR, NON, PC, PJ, UU, AA, VP, HA, D_, SG, R_, SH, T1, T2, KAP, PHI, TAU, NK, NR, NK2, PLV,
     PAO, SN, NKS) = range(28)
    M8, M8B = 0, 8

    def S(k, n=8):
        return A("sm", k, k + n)

    dma("s", T.xt[:, 128:640], T.x[:], [], [A("xt", 128, 640)])
    dma("s", T.ut[:], T.u[:], [], [A("ut")])
    dma("s", T.wt[:], T.w[:], [A("ut", 256)], [A("wt")])
    iota(A("row"), [[1, 128]])
    iota(A("cf", 120, 125), [[64, 5]], -128, 1)
    iota(A("ci", 15), [[0, 1]], 0, 1, False)
    ms(A("ta"), 0.0)
    ms(A("psi", 0, 96), 4.0)
    ms(A("ones"), 1.0)
    ms(A("mx", 128), TINY)
    ms(LV(0, SG), 0.5)
    ms(A("psi", 0, 32, 1, 32, 64), 4.0 * BELOW)
    ms(A("psi", 0, 32, 1, 96, 128), 4.0 * BELOW)
    act(A("the", 128, 648), A("ta"))
    ts(A("idn"), A("row"), C(PP), OP.is_equal)
    ts(A("sf"), A("row"), C(PP), OP.is_gt, 1.0, OP.add)
    run("g", [A("sf")], [A("am")], lambda: g.affine_select(T.am[:], T.sf[:], [[-1, 128]], OP.not_equal, 128.0, 0, 1))
    iota(A("ra"), [[0, 8], [1, 4], [0, 4]])
    pi = A("ci", 15)
    ts(A("ci", P31), pi, 31, OP.bitwise_and)
    ts(A("ci", P15), pi, 15, OP.bitwise_and)
    ts(A("ci", PH), pi, 4, OP.logical_shift_right)
    ts(A("ci", P3), pi, 3, OP.bitwise_and)
    ts(A("ci", PQ), pi, 5, OP.logical_shift_right, 1, OP.bitwise_and)
    ms(C(HB, 0, 64), BIG)
    ms(C(HB, 64, 128), -BIG)
    cp(A("cf", 0, 5), A("ci", 0, 5))
    act(A("the", 131, 643, 4), A("idn"), 0.5)
    ms(A("bm", 128), -64.5)
    ms(A("ta", 516), SB)
    ts(A("psi", 96, 128), A("row", 0, 32), C(P31), OP.is_ge, BELOW, OP.max)
    act(A("ts"), A("ta", 0, 512), 1.0, SA)
    act(A("psi", 96, 128), A("psi", 96, 128), 4.0)
    act(A("ta", 1, 512, 4), A("idn"), -0.5 * SB)
    act(A("ts", 0, 512, 4), A("am"), SA)
    act(C(IL), C(P15), 1.0 / 16)
    quant("buf0", 64, "xt", 128, 128)

    def u_send():
        quant("uq", 0, "ut", 0, 128)
        send_u()
        iota(A("th", 0, 256), [[0, 256]])
        iota(A("te", 0, 256), [[0, 256]])
        a, b = USLOT[PART[0]], USLOT[PART[1]]
        iota(A("oi", 0, 8), [[a + 2, 2], [0, 4]], 0, 0, False)
        iota(A("oi", 8, 16), [[a - 2, 2], [0, 4]], 2, 0, False)
        iota(A("oi", 16, 24), [[b + 2, 2], [a, 2], [0, 2]], 1, 0, False)
        iota(A("oi", 24, 32), [[b - 2, 2], [a, 2], [0, 2]], 3, 0, False)
        iota(A("r16"), [[0, 8], [1, 16]])
        iota(A("the", 0, 128), [[0, 128]])
        iota(A("tf"), [[0, 520]])

    def u_pick(k):
        pick("ur", 128 * k, "uq", 0, 288, A("ou", 8 * k, 8 * k + 8))

    def rows4(t0, t1):
        for t in range(t0, t1):
            ts(A("tg", t, 512, 4), A("ra"), float(t), OP.is_equal, 64.0, OP.mult)

    def rows16():
        ts(A("tg", 0, 512, 4), A("r16"), C(P15), OP.is_equal)
        for t in range(1, 4):
            lin("r16", A("tg", t, 512, 4), A("tg", 0, 512, 4), 1.0)

    def unpackers(b0, b1):
        for b in range(b0, b1):
            quant("qe", 128 * b, "the", 131 - b, 128)

    def halves(f):
        f(0, 64, 64)
        f(64, 128, 0)

    def quarters(name, c):
        for k in range(4):
            gfill(A(name, 32 * (k ^ 1), 32 * (k ^ 1) + 32, 1, 32 * k, 32 * k + 32), c)

    def counts(l, f):
        f(A("tf", 2, 512, 4, 0, 1), -float(64 >> l))
        f(A("tf", 513), 0.5 - (64 >> l))
        f(A("bm", 128), -0.5 - (64 >> l))

    def score_order():
        ts(A("ls", 0, 64, 1, 0, 64), A("row", 0, 64, 1, 0, 64), C(PP, 0, 64), OP.is_lt, -TINY, OP.mult)
        ts(A("ls", 64, 128, 1, 64, 128), A("row", 64, 128, 1, 64, 128), C(PP, 64, 128), OP.is_gt, -TINY, OP.mult)

    def kin_piv(l):
        ts(LV(l, SN), LV(l, RANK), 0.0, OP.is_lt)
        ts(LV(l, NON), LV(l, RANK), 0.0, OP.is_gt)
        act(LV(l, PJ), LV(l, SN), C(PP), None, AF.Relu)
        act(LV(l, PC), LV(l, SN), C(P64), None, AF.Relu)

    def kin_pos(l):
        ts(A("th", 0, 256, 4), A("k64", 64 * l, 64 * l + 64), LV(l, PM), OP.is_equal, 64.0, OP.mult)

    def kin_vp(l):
        lin("vp", LV(l, VP), LV(l, V_), LV(l, NON), LV(l, PJ))

    def kin_par(l, k):
        ts(A("th", 256, 768, 4), A("row"), LV(l, k), OP.is_equal)

    NOR = [8, 4, 4]

    def TZ(c, t, n=8):
        return A("the", 4 * c + t, 4 * (c + n), 4)

    def kin_a(l):
        n = NOR[l]
        return [lambda: lin("uu", LV(l, UU), LV(l, PM), 1.0 / (SA * SB), LV(l, NK) if l else -191.0),
                lambda: lin("aa", LV(l, AA), LV(l, UU), LV(l, NON), LV(l, PC)),
                lambda: ts(LV(l, HA), LV(l, AA), M32, OP.add, M32, OP.subtract),
                lambda: (lin("ha", TZ(8, 0, n), A("ones", 0, n), LV(l, HA)),
                         ts(TZ(8, 1, n), S(M8, n), LV(l, AA), OP.mult, LV(l, HA), OP.subtract))]

    KB = [7, 7, 6]

    def kin_h(l, n=192):
        quant("qh", 0, "th", 0, n)
        mm(KB[l], "qh", 64, "qh", 0)

    def kin_first(l):
        scan(A("so", 0, 64), P(KB[l], 0, 64), A("ones"), -64.0, OP.max, OP.add)
        scan(A("so", 64, 128), P(KB[l], 0, 64), A("st16"), -64.0, OP.max, OP.add)

    def kin_has(l):
        ts(TZ(8, 2, NOR[l]), S(M8B, NOR[l]), A("so", 63), OP.mult, 128.0, OP.min)

    def kin_tile(l):
        lin("so%d" % l, TZ(0, 0), A("ones", 0, 8), A("so", 127))
        ts(TZ(0, 1), S(M8), A("so", 63), OP.mult, A("so", 127), OP.subtract)
        if l < 2:
            kin_has(l)

    def kin_zero():
        ts(C(HAS), A("so", 63), 1.0, OP.min)
        lin("z", TZ(16, 0), S(M8), float(ZERO))
        ts(TZ(16, 1), S(M8), C(HAS), OP.mult, C(HI), OP.mult)
        ts(TZ(16, 2), S(M8), C(HAS), OP.mult, C(P15), OP.mult)
        lin("z", TZ(24, 0), TZ(8, 0), 1.0)
        lin("z", TZ(24, 1), TZ(8, 1), 1.0)
        lin("z", TZ(24, 2), TZ(16, 1), -1.0)
        lin("z", TZ(24, 3), TZ(16, 2), -1.0)

    def kin_through():
        lin("z", A("tg", 0, 256, 4), A("ones"), 0.0)
        ts(A("tg", 1, 256, 4), A("idn", 0, 64), LV(1, AA), OP.mult, LV(1, HA), OP.subtract)
        lin("z", A("tg", 2, 256, 4), A("idn", 0, 64), C(NH))
        lin("z", A("tg", 3, 256, 4), A("ones"), LV(1, HA))
        quant("qc", 0, "tg", 0, 128)
        mm(3, "qo", 0, "qc", 0)
        act(A("rw", 0, 64), P(3, 0, 64))
        run("v", [A("rw"), A("oc0"), A("m16")], [A("gc")],
            lambda: g.vector.tensor_tensor(T["gc"][:], T.rw[:].indirect(T.oc0[:]), T.m16[:], OP.mult))
        scan(A("gd"), A("r0"), A("gc"), 0.0, OP.mult, OP.add)
        cp(A("od"), A("gd", 15, 128, 16))

    def kin_list(l):
        quant("ql", 0, "the", 0, 128)
        mm(KB[l], "qwc", 0, "ql", 0)

    def kin_c(l):
        ts(A("oc%d" % l), P(KB[l], 0, 8), -1.0, OP.mult, 64.0, OP.add)

    def kin_r(l, c):
        n = NOR[l] if l else 24
        cp(A("or%d" % l, 0, n), P(7, c, c + n))

    def place_of(l):
        lin("plv", LV(l, PLV), LV(l, PLR), 1.0 / (SA * SB), LV(l, NK2))

    def place_tile(l):
        ts(A("th", 768, 1280, 4), A("row"), LV(l, PLV), OP.is_equal)

    def place_row(l):
        mm(5, "qo", 0, "qs%d" % l, 0)
        act(A("plr", 0, 128), P(5, 0, 128), 1.0 / SA, -511.0 - (128 >> l))

    def place_mm(bank):
        mm(bank, "qh", 192, "qh", 64)

    def place_out(l, bank):
        tt(A("plr", 128, 256), P(bank, 0, 128), A("plr", 0, 128), OP.mult)
        act(A("jk", 272, 400), A("plr", 128, 256), acc=LV(l, PAO))
        parents_out(l)

    def parents_out(l):
        n, at = 128 >> l, [0, 128, 192][l]
        src = LV(l, PAO if l else VP, 0, n)
        dma("s", T.pa[0, at:at + n], src[0], [src], [])

    def up(l, F):
        bn, bo = "buf%d" % l, BASE[l] + 64

        def L(k, p0=0, p1=128):
            if l and k in (SG, R_):
                return A("sr", 258, 259, 1, p0, p1)
            return LV(l, k, p0, p1)

        def fill(k):
            if k in F:
                F[k]()

        def unpack():
            for b in range(4):
                mm(b, "qe", 128 * b, bn, bo)
        mm(4, bn, bo, bn, bo)
        if l:
            mm(5, "ur", 256 * l - 256, bn, bo, 128, True, False)
            mm(5, bn, bo, "ur", 256 * l - 128, 128, False, True)
        fill(0)
        tt(A("mx", 0, 128), P(4, 0, 128), A("idn"), OP.mult)
        if l:
            tt(A("tf", 1, 512, 4), P(5, 0, 128), A("ls"), OP.is_gt)
            act(A("jk", 0, 129), A("mx", 0, 129), acc=L(D_))
            fill(1)
            scan(A("sr", 0, 259), A("tf", 1, 518, 2), A("cl", 0, 259), 0.0, OP.subtract, OP.min)
            quant("qb", 0, "tf", 0, 128)
            mm(6, "qs0", 0, "qb", 0)
            unpack()
            lin("t1", L(T1), L(D_), BELOW)
            act(A("gs"), P(4, 0, 128), SC)
            lin("nr", L(NR), L(R_), -1024.0)
            lin("sh", L(SH), L(R_), C(HB))
            ts(L(PHI), L(R_), SC * BELOW, OP.max, SC, OP.min)
        else:
            fill(1)
            red(L(D_), A("mx", 0, 129), OP.max)
            act(A("gs"), P(4, 0, 128), SC)
            lin("t1", L(T1), L(D_), BELOW)
            fill(2)
        ts(A("xs", 64, 128), A("psi", 64, 128), L(D_), OP.mult, L(SG), OP.mult)
        if l < 2:
            for k in range(4):
                a, b = 32 * k, 32 * (k ^ 1)
                ts(A("xs", 0, 64, 1, b, b + 32), A("psi", 0, 64, 1, a, a + 32), L(D_, a, a + 32), OP.mult, L(SG, a, a + 32), OP.mult)
        if l:
            lin("kap", L(KAP), L(SG), C(HS), 1.5 * SA)
            act(A("same"), P(6, 0, 128), L(NR), None, AF.Relu)
            halves(lambda p0, p1, c: lin("am", A("am", c, c + 64, 1, p0, p1), A("ones" if l == 1 else "pc", 0, 64, 1, p0, p1),
                                         L(KAP, p0, p1)))
            lin("tau", L(TAU), L(SG), 2.0 ** -109, -2.0 ** -110)
            act(A("gt", 64, 128), P(4, 64, 128), L(PHI))
            act(A("gt", 0, 64), P(4, 0, 64), L(PHI), L(TAU))
            lin("nk", L(NKS), L(SG), 32.0 * SA * SB, 143.0 * SA * SB if l == 1 else C(NA))
            lin("nk", L(NK), L(NKS), -1.0 / (SA * SB))
        fill(3)
        w = 64 if l < 2 else 32
        tr(A("zz", 0, 32), A("xs", 96, 128))
        if l < 2:
            tr(A("zz", 32, 64), A("xs", 0, 32))
        halves(lambda p0, p1, c: tr(A("zz", w, 2 * w, 1, c, c + 64), A("xs", 96 - w, 96, 1, p0, p1)))
        if l == 0:
            unpack()
        for b in range(4):
            act(A("dm", b, 512, 4), P(b, 0, 128), -1.0)
        ts(L(T2), L(SH) if l else C(HB), L(T1), OP.max, L(D_), OP.min)
        fill(4)
        ts(A("bm", 128 - 2 * w, 128 - w), A("zz", 0, w), L(SG), OP.mult, L(T1), OP.is_gt)
        ts(A("bm", 128 - w, 128), A("zz", w, 2 * w), L(SG), OP.mult, L(T2), OP.is_gt)
        if l:
            tt(A("ts", 0, 512, 4), A("same"), A("am"), OP.min)
        else:
            quant("qs0", 0, "ts", 0, 128)
        red(L(RANK), A("bm", 128 - 2 * w, 129))
        if l:
            quant("qs%d" % l, 0, "ts", 0, 128)
        fill(5)
        ts(A("ta", 512), L(RANK), 0.0, OP.is_gt, SB, OP.mult)
        ts(A("ta", 0, 512, 4), A("kk"), L(RANK), OP.is_gt, SB, OP.mult)
        if l:
            tt(A("gs", 64, 128), A("gs", 64, 128), A("gt", 64, 128), OP.max)
        fill(6)
        quant("qa", 0, "ta", 0, 130)
        mm(5, "qs%d" % l, 0, "qa", 0, 130)
        if l:
            tt(A("gs", 0, 64), A("gs", 0, 64), A("gt", 0, 64), OP.min)
            lin("k64", A("k64", 64 * l, 64 * l + 64), A("row", 0, 64), SA * SB, L(NKS))
        fill(7)
        kk, pm = A("k64", 64 * l, 64 * l + 64), P(5, 128)
        tt(A("mk"), A("gs"), P(5, 0, 128), OP.min)
        ts(A("xt", 640, 704), kk, pm, OP.is_equal, C(PH), OP.mult)
        ts(A("xt", 704, 768), kk, pm, OP.is_equal, C(IL), OP.mult)
        scan(A("rm"), A("mk"), A("mk"), -BIG, OP.max, OP.max)
        act(A("jk", 0, 128), A("rm"), -1.0, A("rm", 127), AF.Sign, L(V_))
        act(A("jk", 136, 144), A("rm", 15, 128, 16), -1.0, A("rm", 127), AF.Sign, L(H_))
        lin("tp", A("xt", 0, 64), A("ones"), L(H_))
        quant("qn", 0, "xt", 192, 144)
        mm(6, "qw64", 0, "qn", 0, 128, True, False)
        mm(6, "qw64", 0, "qn", 16, 128, False, True)
        ts(A("eq"), kk, pm, OP.is_equal, 1.0 / 16, OP.mult)
        lin("pm%d" % l, A("cf", 16 + 28 * l + PM, 16 + 28 * l + PM + 2), P(5, 128, 130), 1.0)
        if l == 2:
            kin_pos(l)
            ts(A("th", 1, 256, 4), kk, L(PM), OP.is_equal, 64.0, OP.mult)
            ts(A("th", 256, 768, 4), A("rm"), A("rm", 127), OP.is_ge)
            ts(A("th", 261, 768, 4), A("rm", 0, 127), A("rm", 127), OP.is_ge, -1.0, OP.mult)
        else:
            fill(8)
        ts(A("xt", 64, 128), A("eq"), L(V_), OP.mult, L(H_), OP.subtract)
        ts(A("on"), P(6, 112, 128), C(P3), OP.add)
        run("a", [A("dm"), A("on")], [A("dn")],
            lambda: g.scalar.activation(T.dn[:], T.dm[:].indirect(T.on[:]), AF.Copy, scale=-2.0))
        if l == 2:
            kin_h(l)
        quant("qp", 0, "xt", 0, 144)
        mm(7, "qw64", 0, "qp", 0, 128, True, False)
        mm(7, "qw64", 0, "qp", 16, 128, False, True)
        if l < 2:
            kin_piv(l)
            kin_vp(l)
        if l:
            place_row(l)
        if l == 2:
            kin_first(l)
            kin_piv(l)
            kin_vp(l)
            for b in range(4):
                mm(b, "qe", 128 * b, bn, bo, 128, True, False)
            kin_tile(l)
        else:
            kin_a(l)[0]()
            kin_pos(l)
            fill(9)
        ts(A("op"), P(7, 0, 16), C(P3), OP.add)
        if l == 2:
            kin_a(l)[0]()
            kin_list(l)
        else:
            kin_a(l)[1]()
            if l:
                lin("nk2", L(NK2), L(SG), -64.0, -159.0)
            fill(10)
        run("v", [A("dm"), A("op"), A("dn")], [A("te", 256, 512)],
            lambda: g.vector.tensor_tensor(T.te[:, 256:512], T.dm[:].indirect(T["op"][:]), T.dn[:], OP.add))
        if l == 2:
            kin_a(l)[1]()
            kin_c(l)
        else:
            kin_par(l, VP)
            kin_a(l)[2]()
        quant("buf%d" % min(l + 1, 2), [0, 64, 0][l], "te", 0, 128)

    def exchange(l):
        nb, at, peer = "buf%d" % (l + 1), BASE[l + 1] + 64, rank ^ PART[l]
        remote(peer, 2 * l, A(nb, at, at + 64), A(nb, at + 64, at + 128), True)
        remote(peer, 2 * l + 1, A(nb + "s", at, at + 64), A(nb + "s", at + 64, at + 128), False)
        if l:
            place_of(l)
            u_pick(3)
            place_tile(l)
            kin_a(l)[3]()
            kin_h(l, 320)
            place_mm(3)
            kin_first(l)
            place_out(l, 3)
            kin_tile(l)
            ts(C(NH), A("so", 63), 128.0, OP.mult, 128.0, OP.min)
        else:
            iota(A("th", 768, 1280), [[0, 512]])
            parents_out(l)
            act(C(HS), C(HB), SA / BIG)
            act(C(HI), C(PH), 16.0, 64.0 - ZERO)
            kin_h(l)
            cp(A("ou"), A("oi"))
            u_pick(0)
            u_pick(1)
            ts(A("st16"), A("r16", 0, 64), 15.0, OP.is_equal, 16.0, OP.mult)
            kin_a(l)[3]()
            kin_first(l)
            rows16()
            quant("qwc", 0, "tg", 0, 128)
            kin_tile(l)
            kin_zero()

    def down(l, F):
        bn, b0, ch = "buf%d" % l, BASE[l], "ch%d" % l
        if l:
            pick(ch, 0, bn, b0, b0 + 192, A("oc%d" % l))
        else:
            pick(ch, 0, "buf1", 0, ZERO + 2, A("od"))
        for b in range(4):
            mm(b, "qe", 128 * b, ch, 0, 128, False, True)
        F[0]()
        for b in range(4):
            if b % 2:
                cp(A("td", b, 512, 4), P(b, 0, 128))
            else:
                act(A("td", b, 512, 4), P(b, 0, 128))
        F[1]()
        quant(bn, b0 + 192, "td", 0, 128)
        if l:
            for b in range(4):
                if l == 2:
                    mm(b, "qe", 128 * b, "buf1", 64, 128, True, False)
                else:
                    mm(b, "qe", 128 * b, "pz", 0, 128, True, False)
            F[2]()
            pick("buf%d" % (l - 1), BASE[l - 1], bn, b0, b0 + 320, A("or%d" % l, 0, 4))
            F[3]()

    def nothing():
        pass

    up(0, {0: lambda: (lin("kk", A("kk"), A("idn"), 1000.0, -1000.0),
                       lin("ut", A("ut", 8, 16), A("ut", 0, 8), -1.0), unpackers(0, 2)),
           1: lambda: unpackers(2, 3),
           2: lambda: u_send(),
           3: lambda: (unpackers(3, 4), act(A("th", 256, 768), A("ts"), 0.0, 1.0)),
           4: lambda: rows4(0, 3),
           5: lambda: (rows4(3, 4), lin("k0", A("k64", 0, 64), A("row", 0, 64), SA * SB, 191.0 * SA * SB)),
           6: lambda: quant("qw64", 0, "tg", 0, 128),
           7: lambda: (quant("qo", 0, "th", 256, 128), lin("ls", A("ls"), A("row"), 0.0, BIG)),
           8: lambda: (score_order(), counts(1, afill)),
           9: lambda: (act(A("am"), A("am"), SA), afill(A("th", 2, 256, 4, 0, 1), -64.0),
                       afill(A("tf", 2, 512, 4, 32, 33), 0.5), afill(A("cl", 0, 128), 1000.0), afill(A("cl", 128, 256), 1000.0),
                       ms(A("cl", 256), 1000.0), ms(A("cl", 257, 259), 0.5), ts(S(M8), A("row", 0, 8), C(PH), OP.is_equal)),
           10: lambda: lin("m8", S(M8B), S(M8), 128.0)})
    exchange(0)
    up(1, {3: lambda: kin_list(0),
           4: lambda: quarters("ls", BIG),
           7: lambda: (counts(2, gfill), quarters("am", 0.0), quant("buf0", ZERO, "th", 768, 128),
                       quant("buf1", ZERO, "th", 768, 128), ms(A("rw", 64, 72), float(ZERO)),
                       ts(A("m16"), A("r16"), C(P15), OP.is_equal), ts(A("r0"), A("r16"), 0.5, OP.is_gt),
                       act(C(NA), C(PQ), -16.0 * SA * SB, 127.0 * SA * SB), act(C(NB), C(PQ), 32.0, -127.0)),
           8: lambda: (kin_c(0), kin_r(0, 8)),
           9: lambda: u_pick(2),
           10: lambda: ts(A("pc"), A("row", 0, 64), 32.0, OP.is_ge, C(PQ), OP.is_equal)})
    exchange(1)
    kin_through()
    afill(A("th", 257), 0.0)
    up(2, {1: lambda: kin_list(1),
           4: lambda: (kin_c(1), kin_r(1, 8))})
    kin_a(2)[2]()
    lin("nk2", LV(2, NK2), A("sr", 258), -64.0, C(NB))
    down(2, [lambda: (kin_a(2)[3](), kin_has(2), place_of(2), quant("qr", 0, "the", 32, 128), mm(7, "qwc", 0, "qr", 0)),
             lambda: kin_r(2, 0), lambda: kin_par(2, VP), lambda: (place_tile(2), quant("wq", 0, "wt", 0, 128))])
    down(1, [lambda: (pick("pz", 0, "buf0", 0, ZERO + 2, A("or0", 8, 16)), quant("qh", 64, "th", 256, 256), place_mm(7)),
             nothing, lambda: quant("wq", 128, "wt", 512, 128), lambda: quant("wq", 256, "wt", 1024, 128)])
    down(0, [lambda: (pick("fo", 0, "buf0", 0, ZERO + 2, A("or0", 16, 24)),
                      [mm(4 + o, "wq", 128 * o, "fo", 0, 128, True, False) for o in range(3)]),
             lambda: place_out(2, 7)])
    for o in range(3):
        mm(4 + o, "wq", 128 * o, "buf0", 192, 128, False, True)
    pick("ff", 0, "buf0", 0, 320, A("or0", 0, 8))
    cp(A("ysb", 0, 128), P(4, 0, 128))
    lin("y1", A("ysb", 128, 256), P(5, 0, 128), 1.0)
    cp(A("ysb", 256, 384), P(6, 0, 128))
    dma("s", T.oc[:], T.ff[:].bitcast(dt.uint8), [A("ff")], [])
    for k in range(4):
        dma("asss"[k], T.osc[4 * k:4 * k + 4, :], T.ffs[32 * k:32 * k + 4, :], [A("ffs")], [])
    dma("a", T.y[:], T.ysb[:], [A("ysb")], [])

    OPS[:] = ops
    for k in ORDER or range(len(ops)):
        ops[k][3]()
    last = [(s, n) for s, n in count.items() if all(clock[q].get(s, 0) < n for q in Q)]
    for tok in sorted(last, key=lambda t: (t == ytok[0], when.get(t, 0))):
        wait("g", tok)
